import numpy as np
import ml_dtypes


def mxq(x, axis, fmt="e4m3"):
    dtype, down = {"e4m3": (ml_dtypes.float8_e4m3fn, 7), "e5m2": (ml_dtypes.float8_e5m2, 14)}[fmt]
    v = np.moveaxis(np.asarray(x, np.float32).astype(ml_dtypes.bfloat16).astype(np.float64), axis, -1)
    blocks = v.reshape(v.shape[:-1] + (-1, 32))
    amax = np.abs(blocks).max(-1, keepdims=True)
    byte = np.maximum(np.where(amax > 0, np.frexp(amax)[1] - 1 + 127, 0) - down, 1)
    scale = np.exp2(byte - 127.0)
    codes = (blocks / scale).astype(np.float32).astype(dtype).astype(np.float64)
    return np.moveaxis((codes * scale).reshape(v.shape), -1, axis)


WIDE = False


def mx_kscale(k):
    if not WIDE:
        return np.ones(k)
    levels = np.array([10, -10, 5, -5, 0])
    if k % 512:
        return np.exp2(np.random.permutation(np.resize(levels, k // 32))).repeat(32)
    a = np.empty((k // 512, 16))
    for p in range(k // 512):
        a[p, :8] = np.random.permutation(np.resize(levels, 8))
        for g in range(8):
            far = levels[np.abs(levels - a[p, g]) >= 10]
            a[p, g + 8] = far[np.random.randint(len(far))]
    return np.exp2(a.ravel()).repeat(32)


def f64(x):
    return np.asarray(x).astype(np.float64)


def striped(idx):
    return np.tile(np.asarray(idx).reshape(-1, 16).T, (8, 1)).astype(np.uint16)


def unstriped(offs):
    return offs[:16].T.reshape(-1).astype(np.int64)


E2M1 = np.array([0.0, 0.5, 1.0, 1.5, 2.0, 3.0, 4.0, 6.0, -0.0, -0.5, -1.0, -1.5, -2.0, -3.0, -4.0, -6.0])


def pack_weight(w, fmt):
    k, n = w.shape
    w = f64(np.asarray(w, np.float32).astype(ml_dtypes.bfloat16)).reshape(k // 32, 32, n)
    amax = np.abs(w).max(1)
    if fmt == "e4m3":
        byte = np.frexp(amax)[1] - 1 + 127 - 7
    else:
        mant, ex = np.frexp(amax / 6.0)
        byte = np.where(mant > 0.5, ex, ex - 1) + 127
    byte = np.clip(np.where(amax > 0, byte, 1), 1, 254)
    scaled = (w * np.exp2(127.0 - byte)[:, None, :]).reshape(k, n).astype(np.float32)
    by_word = np.ascontiguousarray(scaled.reshape(k // 512, 128, 4, n).transpose(0, 1, 3, 2))
    if fmt == "e4m3":
        words = by_word.astype(ml_dtypes.float8_e4m3fn).view(np.uint8)
    else:
        c = by_word.astype(ml_dtypes.float4_e2m1fn).view(np.uint8) & 0xF
        words = (c[..., 0::2] | (c[..., 1::2] << 4)).reshape(k // 512, 128, 2 * n)
    return np.ascontiguousarray(words), np.ascontiguousarray(byte.astype(np.uint8).reshape(k // 512, 16, n))


def unpack_weight(words, scales, fmt):
    g, _, n = scales.shape
    words = np.ascontiguousarray(words).reshape(g, 128, n, -1)
    if fmt == "e4m3":
        vals = words.view(ml_dtypes.float8_e4m3fn).astype(np.float64)
    else:
        nib = np.empty((g, 128, n, 4), np.uint8)
        nib[..., 0::2] = words & 0xF
        nib[..., 1::2] = words >> 4
        vals = E2M1[nib]
    vals = vals * np.repeat(np.exp2(scales.astype(np.float64) - 127.0), 8, axis=1)[..., None]
    return vals.transpose(0, 1, 3, 2).reshape(g * 512, n)


B, N, T, D, DV, NQ = 1, 1024, 4096, 512, 128, 128
PAGE = 512
DRAFT = 128


def setup_inputs():
    n = np.random.standard_normal
    pages = np.random.permutation(T // PAGE)[:B * N // PAGE]
    idx = (pages[:, None] * PAGE + np.arange(PAGE)[None, :]).reshape(-1)
    s = mx_kscale(D)[:, None]
    u = np.ones(T)
    u[idx] = mx_kscale(B * N)
    r = np.random.uniform(0.5, 2.0, T)
    qp = [pack_weight(x, "e4m3") for x in n((B, D, NQ)) * s * (0.80 / np.sqrt(D))]
    k = n((D, T)) / s
    v = n((DV, T)) / (u * r)
    kp = pack_weight(k, "e4m3")
    vp = pack_weight(v.T, "e4m3")
    when = np.zeros(T)
    when[idx] = np.concatenate([np.concatenate([np.arange(N - DRAFT), N - DRAFT + np.random.randint(0, 16, DRAFT)]) for b in range(B)])
    return {
        "q_words": np.stack([x[0] for x in qp]),
        "q_scales": np.stack([x[1] for x in qp]),
        "k_words": kp[0],
        "k_scales": kp[1],
        "v_words": vp[0],
        "v_scales": vp[1],
        "vs": np.tile(u * r, (128, 1)).astype(np.float32),
        "pos": np.tile(when, (128, 1)).astype(np.float32),
        "qpos": np.random.randint(N - DRAFT, N - DRAFT + 16, (B, NQ, 1)).astype(np.float32),
        "og": n((B, NQ, DV)).astype(np.float32),
        "offs": striped(idx),
        "voffs": striped((pages[:, None] * DV + np.arange(DV)[None, :]).reshape(-1)),
    }


def reference(q_words, q_scales, k_words, k_scales, v_words, v_scales, vs, pos, qpos, og, offs, voffs):
    idx = unstriped(offs)
    k = unpack_weight(k_words, k_scales, "e4m3")
    v = unpack_weight(v_words, v_scales, "e4m3")
    v = v.reshape(T // 512, 512, DV)[unstriped(voffs)[::DV] // DV].reshape(B, N, DV)
    pick = lambda x: x[:, idx].reshape(x.shape[0], B, N).transpose(1, 0, 2)
    q = np.stack([unpack_weight(q_words[b], q_scales[b], "e4m3") for b in range(B)])
    score = q.transpose(0, 2, 1) @ pick(k)
    score = np.where(pick(f64(pos))[:, :1, :] <= f64(qpos), score, -30000.0)
    m = score.max(-1, keepdims=True)
    p = np.exp(score - m)
    total = p.sum(-1, keepdims=True)
    w = p * pick(f64(vs))[:, :1, :]
    y = mxq(w, 2, "e4m3") @ v
    y = y / total
    y = y / (1.0 + np.exp(-f64(og)))
    return y

@@ -1,0 +1,202 @@
+from contextlib import ExitStack
+
+import concourse.mybir as mybir
+from concourse.masks import make_identity
+
+F32 = mybir.dt.float32
+BF16 = mybir.dt.bfloat16
+I32 = mybir.dt.int32
+U32 = mybir.dt.uint32
+U16 = mybir.dt.uint16
+U8 = mybir.dt.uint8
+FP8X4 = mybir.dt.float8_e4m3fn_x4
+ALU = mybir.AluOpType
+ACT = mybir.ActivationFunctionType
+
+P = 128
+N, T, D, DV, NQ = 1024, 4096, 512, 128, 128
+PAGE = 512
+PAGES = N // PAGE
+POOL_PAGES = T // PAGE
+PACK = 4
+LIST = 16
+ROW = P - 1
+MASKED = -30000.0
+NO_CAP = 1e38
+POS_SPLIT = 2448
+
+FLOPS = 2 * NQ * N * D + 2 * NQ * N * DV
+BYTES = T * D + 16 * T + T * DV + 16 * 8 * DV + D * NQ + 16 * NQ + 2 * 4 * T + 4 * NQ + 2 * 4 * NQ * DV + 2 * P * (N + 256) // 16
+
+
+def tile_attend_pkv8q_soft_draft_gate_kernel(
+    tc, q_words, q_scales, k_words, k_scales, v_words, v_scales, vs, pos, qpos, og, offs, voffs, out
+):
+    nc = tc.nc
+    with ExitStack() as ctx:
+        sb = ctx.enter_context(tc.tile_pool(name="sb", bufs=1))
+        ps = ctx.enter_context(tc.psum_pool(name="ps", bufs=1))
+
+        offs_t = sb.tile([P, N // LIST], U16)
+        voffs_t = sb.tile([P, PAGES * DV // LIST], U16)
+        kw_pool = sb.tile([P, T], I32, align_bytes=64)
+        ks_pool = sb.tile([P, T], U8, align_bytes=64)
+        vw_pool = sb.tile([P, POOL_PAGES * DV], I32, align_bytes=64)
+        vsc_pool = sb.tile([P, POOL_PAGES * DV], U8, align_bytes=64)
+        pos_pool = sb.tile([P, T], F32, align_bytes=64)
+        vs_pool = sb.tile([P, T], F32, align_bytes=64)
+        qw = sb.tile([P, NQ], I32, align_bytes=64)
+        qs = sb.tile([P, NQ], U8, align_bytes=64)
+        qpos_t = sb.tile([P, 1], F32)
+        og_t = sb.tile([P, DV], F32)
+        ident = sb.tile([P, P], F32, align_bytes=64)
+        warm = sb.tile([P, 1], F32)
+
+        nc.vector.memset(ks_pool[:].bitcast(I32), 0)
+        nc.vector.memset(pos_pool[0:ROW, 0 : POS_SPLIT - 1], 0.0)
+        nc.vector.memset(pos_pool[0:ROW, POS_SPLIT - 1 : POS_SPLIT], 0.0)
+        make_identity(nc, ident[:])
+        nc.gpsimd.memset(pos_pool[0:ROW, POS_SPLIT:T], 0.0)
+        nc.gpsimd.memset(qs[:].bitcast(I32), 0)
+        nc.gpsimd.memset(vsc_pool[:].bitcast(I32), 0)
+        for c in range(4):
+            nc.gpsimd.memset(vs_pool[0:ROW, c * 1024 : (c + 1) * 1024], 0.0)
+
+        nc.sync.dma_start(offs_t[:], offs)
+        nc.sync.dma_start(pos_pool[ROW:P, :], pos[0:1, :])
+        nc.sync.dma_start(kw_pool[:], k_words[0].rearrange("p n t -> p (n t)").bitcast(I32))
+        nc.scalar.dma_start(qpos_t[:], qpos[0])
+        for quad in range(4):
+            nc.scalar.dma_start(
+                ks_pool[32 * quad : 32 * quad + 4, :].bitcast(I32),
+                k_scales[0, 4 * quad : 4 * quad + 4, :].bitcast(I32),
+            )
+        for quad in range(4):
+            nc.scalar.dma_start(
+                qs[32 * quad : 32 * quad + 4, :].bitcast(I32),
+                q_scales[0, 0, 4 * quad : 4 * quad + 4, :].bitcast(I32),
+            )
+        nc.scalar.activation(warm[:], qpos_t[:, 0:1], ACT.Exp, scale=0.0)
+        for quad in range(4):
+            nc.scalar.dma_start(
+                vsc_pool[32 * quad : 32 * quad + 4, :].bitcast(I32).rearrange("p (u e) -> p u e", u=POOL_PAGES),
+                v_scales[:, 4 * quad : 4 * quad + 4, :].rearrange("u f e -> f u e").bitcast(I32),
+            )
+        nc.sync.dma_start(qw[:], q_words[0, 0].rearrange("p n t -> p (n t)").bitcast(I32))
+        nc.sync.dma_start(voffs_t[:], voffs)
+        nc.sync.dma_start(
+            vw_pool[:].rearrange("p (u e) -> p u e", u=POOL_PAGES),
+            v_words.rearrange("u p e t -> p u (e t)").bitcast(I32),
+        )
+        nc.sync.dma_start(vs_pool[ROW:P, :], vs[0:1, :])
+        nc.sync.dma_start(og_t[:], og[0])
+
+        def listed(h):
+            return offs_t[:, h * PAGE // LIST : (h + 1) * PAGE // LIST]
+
+        pos_row = [sb.tile([P, PAGE], F32, name=f"pos_row{h}", align_bytes=64) for h in range(PAGES)]
+        pos_col = [sb.tile([P, PACK], F32, name=f"pos_col{h}", align_bytes=64) for h in range(PAGES)]
+        cap = [sb.tile([P, PACK, P], F32, name=f"cap{h}", tag=f"cap{h}", align_bytes=64) for h in range(PAGES)]
+        ks = sb.tile([P, N], U8, align_bytes=64)
+        pos_all = []
+        for h in range(PAGES):
+            nc.vector.tensor_copy(pos_row[h][:], pos_pool[:].indirect(listed(h)))
+            turned = ps.tile([P, PACK, P], F32, name=f"pos_turned{h}", tag=f"turn{h}")
+            for c in range(PACK):
+                nc.tensor.transpose(turned[:, c, :], pos_row[h][:, c * P : (c + 1) * P], ident[:])
+            nc.vector.tensor_copy(pos_col[h][:], turned[:, :, ROW])
+            spread = ps.tile([P, PAGE], F32, name=f"pos_all{h}", tag=f"wide{h}")
+            for c in range(PACK):
+                nc.tensor.transpose(
+                    spread[:, c * P : (c + 1) * P], pos_col[h][:, c : c + 1].to_broadcast([P, P]), ident[:]
+                )
+            pos_all.append(spread)
+        for h in range(PAGES):
+            nc.vector.tensor_copy(ks[:, h * PAGE : (h + 1) * PAGE], ks_pool[:].indirect(listed(h)))
+        for h in range(PAGES):
+            nc.vector.tensor_scalar(
+                cap[h][:], pos_all[h][:].rearrange("p (j t) -> p t j", t=PACK), qpos_t[:, 0:1], NO_CAP, ALU.is_le, ALU.mult
+            )
+
+        kw = [sb.tile([P, PAGE], U32, name=f"kw{h}", align_bytes=64) for h in range(PAGES)]
+        s = sb.tile([P, PAGES, PACK, P], F32, align_bytes=64)
+        raw = []
+        for h in range(PAGES):
+            nc.vector.tensor_copy(kw[h][:], kw_pool[:].bitcast(U32).indirect(listed(h)))
+            bank = ps.tile([P, PAGE], F32, name=f"raw{h}", tag=f"raw{h}")
+            nc.tensor.matmul_mx(
+                out=bank[:],
+                lhsT=qw[:].bitcast(FP8X4),
+                lhsT_scale=qs[:],
+                rhs=kw[h][:].bitcast(FP8X4),
+                rhs_scale=ks[:, h * PAGE : (h + 1) * PAGE],
+                start=True,
+                stop=True,
+            )
+            raw.append(bank)
+        for h in range(PAGES):
+            nc.vector.scalar_tensor_tensor(
+                s[:, h], cap[h][:], MASKED, raw[h][:].rearrange("p (j t) -> p t j", t=PACK), ALU.add, ALU.min
+            )
+        neg_m = sb.tile([P, 1], F32)
+        nc.vector.tensor_reduce(
+            neg_m[:], s[:].rearrange("p h t j -> p (h t j)"), mybir.AxisListType.X, ALU.max, negate=True
+        )
+
+        p = [sb.tile([P, PACK, P], F32, name=f"p{h}", align_bytes=64) for h in range(PAGES)]
+        sums = sb.tile([P, PAGES], F32)
+        for h in range(PAGES):
+            nc.scalar.activation(p[h][:], s[:, h], ACT.Exp, bias=neg_m[:, 0:1], accum_out=sums[:, h : h + 1])
+        gate_t = sb.tile([P, DV], F32)
+        gate = sb.tile([P, DV], F32)
+        nc.scalar.activation(gate_t[:], og_t[:], ACT.Tanh, scale=0.5)
+        nc.scalar.activation(gate[:], gate_t[:], ACT.Copy, scale=0.5, bias=0.5)
+
+        vw = sb.tile([P, PAGES * DV], U32, tag="cap1", align_bytes=64)
+        nc.vector.tensor_copy(vw[:], vw_pool[:].bitcast(U32).indirect(voffs_t[:]))
+
+        vs_row = [sb.tile([P, PAGE], F32, name=f"vs_row{h}", align_bytes=64) for h in range(PAGES)]
+        vs_col = [sb.tile([P, PACK], F32, name=f"vs_col{h}", align_bytes=64) for h in range(PAGES)]
+        for h in range(PAGES):
+            nc.vector.tensor_copy(vs_row[h][:], vs_pool[:].indirect(listed(h)))
+            turned = ps.tile([P, PACK, P], F32, name=f"vs_turned{h}", tag=f"turn{h}")
+            for t in range(PACK):
+                nc.tensor.transpose(turned[:, t, :], vs_row[h][:, t:PAGE:PACK], ident[:])
+            nc.vector.tensor_copy(vs_col[h][:], turned[:, :, ROW])
+
+        vsc = sb.tile([P, PAGES * DV], U8, align_bytes=64)
+        nc.vector.tensor_copy(vsc[:], vsc_pool[:].indirect(voffs_t[:]))
+
+        acc = ps.tile([P, DV], F32, tag="acc")
+        w = [sb.tile([P, NQ, PACK], BF16, name=f"w{h}", align_bytes=64) for h in range(PAGES)]
+        codes = [sb.tile([P, NQ], U32, name=f"codes{h}", align_bytes=64) for h in range(PAGES)]
+        scales = [sb.tile([P, NQ], U8, name=f"scales{h}", align_bytes=64) for h in range(PAGES)]
+        for h in range(PAGES):
+            turned = ps.tile([P, PACK, NQ], F32, name=f"p_turned{h}", tag=f"wide{h}")
+            for t in range(PACK):
+                nc.tensor.transpose(turned[:, t, :], p[h][:, t, :], ident[:])
+            nc.vector.tensor_tensor(
+                w[h][:],
+                turned[:].rearrange("p t q -> p q t"),
+                vs_col[h][:].unsqueeze(1).to_broadcast([P, NQ, PACK]),
+                ALU.mult,
+            )
+        total = sb.tile([P, 1], F32)
+        inv = sb.tile([P, 1], F32)
+        nc.vector.quantize_mx(out=codes[0][:].bitcast(FP8X4), scales=scales[0][:], in_=w[0][:].rearrange("p q t -> p (q t)"))
+        nc.vector.tensor_tensor(total[:], sums[:, 0:1], sums[:, 1:2], ALU.add)
+        nc.vector.quantize_mx(out=codes[1][:].bitcast(FP8X4), scales=scales[1][:], in_=w[1][:].rearrange("p q t -> p (q t)"))
+        nc.vector.reciprocal(inv[:], total[:])
+        for h in range(PAGES):
+            nc.tensor.matmul_mx(
+                out=acc[:],
+                lhsT=codes[h][:].bitcast(FP8X4),
+                lhsT_scale=scales[h][:],
+                rhs=vw[:, h * DV : (h + 1) * DV].bitcast(FP8X4),
+                rhs_scale=vsc[:, h * DV : (h + 1) * DV],
+                start=(h == 0),
+                stop=(h == PAGES - 1),
+            )
+        result = sb.tile([P, DV], F32)
+        nc.vector.scalar_tensor_tensor(result[:], acc[:], inv[:, 0:1], gate[:], ALU.mult, ALU.mult)
+        nc.sync.dma_start(out[0], result[:])

@@ -23,7 +23,6 @@ LIST = 16
 ROW = P - 1
 MASKED = -30000.0
 NO_CAP = 1e38
-POS_SPLIT = 2448
 
 FLOPS = 2 * NQ * N * D + 2 * NQ * N * DV
 BYTES = T * D + 16 * T + T * DV + 16 * 8 * DV + D * NQ + 16 * NQ + 2 * 4 * T + 4 * NQ + 2 * 4 * NQ * DV + 2 * P * (N + 256) // 16
@@ -35,16 +34,15 @@ def tile_attend_pkv8q_soft_draft_gate_kernel(
     nc = tc.nc
     with ExitStack() as ctx:
         sb = ctx.enter_context(tc.tile_pool(name="sb", bufs=1))
+        big = ctx.enter_context(tc.tile_pool(name="big", bufs=1))
         ps = ctx.enter_context(tc.psum_pool(name="ps", bufs=1))
 
         offs_t = sb.tile([P, N // LIST], U16)
         voffs_t = sb.tile([P, PAGES * DV // LIST], U16)
-        kw_pool = sb.tile([P, T], I32, align_bytes=64)
+        kw_pool = big.tile([P, T], I32, align_bytes=64, offset=0)
+        pos_pool = big.tile([P, T], F32, align_bytes=64, offset=4 * T)
+        vs_pool = big.tile([P, T], F32, align_bytes=64, offset=8 * T)
         ks_pool = sb.tile([P, T], U8, align_bytes=64)
-        vw_pool = sb.tile([P, POOL_PAGES * DV], I32, align_bytes=64)
-        vsc_pool = sb.tile([P, POOL_PAGES * DV], U8, align_bytes=64)
-        pos_pool = sb.tile([P, T], F32, align_bytes=64)
-        vs_pool = sb.tile([P, T], F32, align_bytes=64)
         qw = sb.tile([P, NQ], I32, align_bytes=64)
         qs = sb.tile([P, NQ], U8, align_bytes=64)
         qpos_t = sb.tile([P, 1], F32)
@@ -52,15 +50,11 @@ def tile_attend_pkv8q_soft_draft_gate_kernel(
         ident = sb.tile([P, P], F32, align_bytes=64)
         warm = sb.tile([P, 1], F32)
 
-        nc.vector.memset(ks_pool[:].bitcast(I32), 0)
-        nc.vector.memset(pos_pool[0:ROW, 0 : POS_SPLIT - 1], 0.0)
-        nc.vector.memset(pos_pool[0:ROW, POS_SPLIT - 1 : POS_SPLIT], 0.0)
         make_identity(nc, ident[:])
-        nc.gpsimd.memset(pos_pool[0:ROW, POS_SPLIT:T], 0.0)
-        nc.gpsimd.memset(qs[:].bitcast(I32), 0)
-        nc.gpsimd.memset(vsc_pool[:].bitcast(I32), 0)
-        for c in range(4):
-            nc.gpsimd.memset(vs_pool[0:ROW, c * 1024 : (c + 1) * 1024], 0.0)
+        nc.vector.memset(ks_pool[:].bitcast(I32), 0)
+        nc.vector.memset(pos_pool[0:ROW, :], 0.0)
+        nc.vector.memset(qs[:].bitcast(I32), 0)
+        nc.vector.memset(vs_pool[0:ROW, :], 0.0)
 
         nc.sync.dma_start(offs_t[:], offs)
         nc.sync.dma_start(pos_pool[ROW:P, :], pos[0:1, :])
@@ -77,63 +71,71 @@ def tile_attend_pkv8q_soft_draft_gate_kernel(
                 q_scales[0, 0, 4 * quad : 4 * quad + 4, :].bitcast(I32),
             )
         nc.scalar.activation(warm[:], qpos_t[:, 0:1], ACT.Exp, scale=0.0)
-        for quad in range(4):
-            nc.scalar.dma_start(
-                vsc_pool[32 * quad : 32 * quad + 4, :].bitcast(I32).rearrange("p (u e) -> p u e", u=POOL_PAGES),
-                v_scales[:, 4 * quad : 4 * quad + 4, :].rearrange("u f e -> f u e").bitcast(I32),
-            )
         nc.sync.dma_start(qw[:], q_words[0, 0].rearrange("p n t -> p (n t)").bitcast(I32))
-        nc.sync.dma_start(voffs_t[:], voffs)
-        nc.sync.dma_start(
-            vw_pool[:].rearrange("p (u e) -> p u e", u=POOL_PAGES),
-            v_words.rearrange("u p e t -> p u (e t)").bitcast(I32),
-        )
         nc.sync.dma_start(vs_pool[ROW:P, :], vs[0:1, :])
         nc.sync.dma_start(og_t[:], og[0])
+        nc.sync.dma_start(voffs_t[:], voffs)
 
         def listed(h):
             return offs_t[:, h * PAGE // LIST : (h + 1) * PAGE // LIST]
 
         pos_row = [sb.tile([P, PAGE], F32, name=f"pos_row{h}", align_bytes=64) for h in range(PAGES)]
         pos_col = [sb.tile([P, PACK], F32, name=f"pos_col{h}", align_bytes=64) for h in range(PAGES)]
-        cap = [sb.tile([P, PACK, P], F32, name=f"cap{h}", tag=f"cap{h}", align_bytes=64) for h in range(PAGES)]
+        side = [sb.tile([P, PACK, P], F32, name=f"side{h}", align_bytes=64) for h in range(PAGES)]
+        cap = [sb.tile([P, PACK, P], F32, name=f"cap{h}", align_bytes=64) for h in range(PAGES)]
         ks = sb.tile([P, N], U8, align_bytes=64)
-        pos_all = []
         for h in range(PAGES):
             nc.vector.tensor_copy(pos_row[h][:], pos_pool[:].indirect(listed(h)))
+        for h in range(PAGES):
             turned = ps.tile([P, PACK, P], F32, name=f"pos_turned{h}", tag=f"turn{h}")
             for c in range(PACK):
                 nc.tensor.transpose(turned[:, c, :], pos_row[h][:, c * P : (c + 1) * P], ident[:])
-            nc.vector.tensor_copy(pos_col[h][:], turned[:, :, ROW])
+            nc.scalar.copy(pos_col[h][:], turned[:, :, ROW])
             spread = ps.tile([P, PAGE], F32, name=f"pos_all{h}", tag=f"wide{h}")
             for c in range(PACK):
                 nc.tensor.transpose(
                     spread[:, c * P : (c + 1) * P], pos_col[h][:, c : c + 1].to_broadcast([P, P]), ident[:]
                 )
-            pos_all.append(spread)
+            nc.scalar.activation(
+                side[h][:], spread[:].rearrange("p (j t) -> p t j", t=PACK), ACT.Sign, scale=-1.0, bias=qpos_t[:, 0:1]
+            )
+            nc.scalar.activation(cap[h][:], side[h][:], ACT.Copy, scale=NO_CAP, bias=NO_CAP)
         for h in range(PAGES):
             nc.vector.tensor_copy(ks[:, h * PAGE : (h + 1) * PAGE], ks_pool[:].indirect(listed(h)))
+        vs_row = [sb.tile([P, PAGE], F32, name=f"vs_row{h}", align_bytes=64) for h in range(PAGES)]
         for h in range(PAGES):
-            nc.vector.tensor_scalar(
-                cap[h][:], pos_all[h][:].rearrange("p (j t) -> p t j", t=PACK), qpos_t[:, 0:1], NO_CAP, ALU.is_le, ALU.mult
-            )
+            nc.vector.tensor_copy(vs_row[h][:], vs_pool[:].indirect(listed(h)))
 
-        kw = [sb.tile([P, PAGE], U32, name=f"kw{h}", align_bytes=64) for h in range(PAGES)]
+        kw = big.tile([P, N], U32, align_bytes=64, offset=8 * T)
         s = sb.tile([P, PAGES, PACK, P], F32, align_bytes=64)
         raw = []
         for h in range(PAGES):
-            nc.vector.tensor_copy(kw[h][:], kw_pool[:].bitcast(U32).indirect(listed(h)))
+            nc.vector.tensor_copy(kw[:, h * PAGE : (h + 1) * PAGE], kw_pool[:].bitcast(U32).indirect(listed(h)))
             bank = ps.tile([P, PAGE], F32, name=f"raw{h}", tag=f"raw{h}")
             nc.tensor.matmul_mx(
                 out=bank[:],
                 lhsT=qw[:].bitcast(FP8X4),
                 lhsT_scale=qs[:],
-                rhs=kw[h][:].bitcast(FP8X4),
+                rhs=kw[:, h * PAGE : (h + 1) * PAGE].bitcast(FP8X4),
                 rhs_scale=ks[:, h * PAGE : (h + 1) * PAGE],
                 start=True,
                 stop=True,
             )
             raw.append(bank)
+
+        vw_pool = big.tile([P, POOL_PAGES * DV], I32, align_bytes=64, offset=0)
+        vsc_pool = big.tile([P, POOL_PAGES * DV], U8, align_bytes=64, offset=4 * POOL_PAGES * DV)
+        nc.gpsimd.memset(vsc_pool[:].bitcast(I32), 0)
+        nc.sync.dma_start(
+            vw_pool[:].rearrange("p (u e) -> p u e", u=POOL_PAGES),
+            v_words.rearrange("u p e t -> p u (e t)").bitcast(I32),
+        )
+        for quad in range(4):
+            nc.sync.dma_start(
+                vsc_pool[32 * quad : 32 * quad + 4, :].bitcast(I32).rearrange("p (u e) -> p u e", u=POOL_PAGES),
+                v_scales[:, 4 * quad : 4 * quad + 4, :].rearrange("u f e -> f u e").bitcast(I32),
+            )
+
         for h in range(PAGES):
             nc.vector.scalar_tensor_tensor(
                 s[:, h], cap[h][:], MASKED, raw[h][:].rearrange("p (j t) -> p t j", t=PACK), ALU.add, ALU.min
@@ -143,34 +145,42 @@ def tile_attend_pkv8q_soft_draft_gate_kernel(
             neg_m[:], s[:].rearrange("p h t j -> p (h t j)"), mybir.AxisListType.X, ALU.max, negate=True
         )
 
-        p = [sb.tile([P, PACK, P], F32, name=f"p{h}", align_bytes=64) for h in range(PAGES)]
-        sums = sb.tile([P, PAGES], F32)
-        for h in range(PAGES):
-            nc.scalar.activation(p[h][:], s[:, h], ACT.Exp, bias=neg_m[:, 0:1], accum_out=sums[:, h : h + 1])
         gate_t = sb.tile([P, DV], F32)
         gate = sb.tile([P, DV], F32)
         nc.scalar.activation(gate_t[:], og_t[:], ACT.Tanh, scale=0.5)
         nc.scalar.activation(gate[:], gate_t[:], ACT.Copy, scale=0.5, bias=0.5)
 
-        vw = sb.tile([P, PAGES * DV], U32, tag="cap1", align_bytes=64)
-        nc.vector.tensor_copy(vw[:], vw_pool[:].bitcast(U32).indirect(voffs_t[:]))
+        p = [sb.tile([P, PACK, P], F32, name=f"p{h}", align_bytes=64) for h in range(PAGES)]
+        sums = sb.tile([P, 2 * PAGES], F32)
+        for h in range(PAGES):
+            for u in range(2):
+                nc.scalar.activation(
+                    p[h][:, 2 * u : 2 * u + 2, :],
+                    s[:, h, 2 * u : 2 * u + 2, :],
+                    ACT.Exp,
+                    bias=neg_m[:, 0:1],
+                    accum_out=sums[:, 2 * h + u : 2 * h + u + 1],
+                )
 
-        vs_row = [sb.tile([P, PAGE], F32, name=f"vs_row{h}", align_bytes=64) for h in range(PAGES)]
         vs_col = [sb.tile([P, PACK], F32, name=f"vs_col{h}", align_bytes=64) for h in range(PAGES)]
         for h in range(PAGES):
-            nc.vector.tensor_copy(vs_row[h][:], vs_pool[:].indirect(listed(h)))
-            turned = ps.tile([P, PACK, P], F32, name=f"vs_turned{h}", tag=f"turn{h}")
+            turned = ps.tile([P, PACK, P], F32, name=f"vs_turned{h}", tag=f"raw{h}")
             for t in range(PACK):
                 nc.tensor.transpose(turned[:, t, :], vs_row[h][:, t:PAGE:PACK], ident[:])
             nc.vector.tensor_copy(vs_col[h][:], turned[:, :, ROW])
 
+        vw = sb.tile([P, PAGES * DV], U32, align_bytes=64)
         vsc = sb.tile([P, PAGES * DV], U8, align_bytes=64)
+        nc.vector.tensor_copy(vw[:], vw_pool[:].bitcast(U32).indirect(voffs_t[:]))
         nc.vector.tensor_copy(vsc[:], vsc_pool[:].indirect(voffs_t[:]))
 
         acc = ps.tile([P, DV], F32, tag="acc")
         w = [sb.tile([P, NQ, PACK], BF16, name=f"w{h}", align_bytes=64) for h in range(PAGES)]
         codes = [sb.tile([P, NQ], U32, name=f"codes{h}", align_bytes=64) for h in range(PAGES)]
         scales = [sb.tile([P, NQ], U8, name=f"scales{h}", align_bytes=64) for h in range(PAGES)]
+        total = sb.tile([P, 1], F32)
+        inv = sb.tile([P, 1], F32)
+        nc.vector.tensor_reduce(total[:], sums[:], mybir.AxisListType.X, ALU.add)
         for h in range(PAGES):
             turned = ps.tile([P, PACK, NQ], F32, name=f"p_turned{h}", tag=f"wide{h}")
             for t in range(PACK):
@@ -181,11 +191,10 @@ def tile_attend_pkv8q_soft_draft_gate_kernel(
                 vs_col[h][:].unsqueeze(1).to_broadcast([P, NQ, PACK]),
                 ALU.mult,
             )
-        total = sb.tile([P, 1], F32)
-        inv = sb.tile([P, 1], F32)
-        nc.vector.quantize_mx(out=codes[0][:].bitcast(FP8X4), scales=scales[0][:], in_=w[0][:].rearrange("p q t -> p (q t)"))
-        nc.vector.tensor_tensor(total[:], sums[:, 0:1], sums[:, 1:2], ALU.add)
-        nc.vector.quantize_mx(out=codes[1][:].bitcast(FP8X4), scales=scales[1][:], in_=w[1][:].rearrange("p q t -> p (q t)"))
+        for h in range(PAGES):
+            nc.vector.quantize_mx(
+                out=codes[h][:].bitcast(FP8X4), scales=scales[h][:], in_=w[h][:].rearrange("p q t -> p (q t)")
+            )
         nc.vector.reciprocal(inv[:], total[:])
         for h in range(PAGES):
             nc.tensor.matmul_mx(

@@ -41,20 +41,23 @@ def tile_attend_pkv8q_soft_draft_gate_kernel(
         voffs_t = sb.tile([P, PAGES * DV // LIST], U16)
         kw_pool = big.tile([P, T], I32, align_bytes=64, offset=0)
         pos_pool = big.tile([P, T], F32, align_bytes=64, offset=4 * T)
-        vs_pool = big.tile([P, T], F32, align_bytes=64, offset=8 * T)
         ks_pool = sb.tile([P, T], U8, align_bytes=64)
         qw = sb.tile([P, NQ], I32, align_bytes=64)
         qs = sb.tile([P, NQ], U8, align_bytes=64)
         qpos_t = sb.tile([P, 1], F32)
         og_t = sb.tile([P, DV], F32)
         ident = sb.tile([P, P], F32, align_bytes=64)
-        warm = sb.tile([P, 1], F32)
+        warm = big.tile([P, 1], F32, align_bytes=64, offset=8 * T)
+        ones = sb.tile([P, PAGE], F32, align_bytes=64)
+        vw_pool = sb.tile([P, POOL_PAGES * DV], I32, align_bytes=64)
+        vsc_pool = sb.tile([P, POOL_PAGES * DV], U8, align_bytes=64)
 
         make_identity(nc, ident[:])
+        nc.gpsimd.memset(qs[:].bitcast(I32), 0)
+        nc.gpsimd.memset(vsc_pool[:].bitcast(I32), 0)
         nc.vector.memset(ks_pool[:].bitcast(I32), 0)
+        nc.vector.memset(ones[:], 1.0)
         nc.vector.memset(pos_pool[0:ROW, :], 0.0)
-        nc.vector.memset(qs[:].bitcast(I32), 0)
-        nc.vector.memset(vs_pool[0:ROW, :], 0.0)
 
         nc.sync.dma_start(offs_t[:], offs)
         nc.sync.dma_start(pos_pool[ROW:P, :], pos[0:1, :])
@@ -65,16 +68,27 @@ def tile_attend_pkv8q_soft_draft_gate_kernel(
                 ks_pool[32 * quad : 32 * quad + 4, :].bitcast(I32),
                 k_scales[0, 4 * quad : 4 * quad + 4, :].bitcast(I32),
             )
+        nc.scalar.activation(warm[:], ones[:, 0:1], ACT.Exp)
+        vs_pool = big.tile([P, T], F32, align_bytes=64, offset=8 * T)
+        nc.scalar.dma_start(vs_pool[ROW:P, :], vs[0:1, :])
+        nc.gpsimd.memset(vs_pool[0:ROW, :], 0.0)
+        nc.sync.dma_start(qw[:], q_words[0, 0].rearrange("p n t -> p (n t)").bitcast(I32))
         for quad in range(4):
-            nc.scalar.dma_start(
+            nc.sync.dma_start(
                 qs[32 * quad : 32 * quad + 4, :].bitcast(I32),
                 q_scales[0, 0, 4 * quad : 4 * quad + 4, :].bitcast(I32),
             )
-        nc.scalar.activation(warm[:], qpos_t[:, 0:1], ACT.Exp, scale=0.0)
-        nc.sync.dma_start(qw[:], q_words[0, 0].rearrange("p n t -> p (n t)").bitcast(I32))
-        nc.sync.dma_start(vs_pool[ROW:P, :], vs[0:1, :])
-        nc.sync.dma_start(og_t[:], og[0])
         nc.sync.dma_start(voffs_t[:], voffs)
+        for quad in range(4):
+            nc.sync.dma_start(
+                vsc_pool[32 * quad : 32 * quad + 4, :].bitcast(I32).rearrange("p (u e) -> p u e", u=POOL_PAGES),
+                v_scales[:, 4 * quad : 4 * quad + 4, :].rearrange("u f e -> f u e").bitcast(I32),
+            )
+        nc.sync.dma_start(og_t[:], og[0])
+        nc.sync.dma_start(
+            vw_pool[:].rearrange("p (u e) -> p u e", u=POOL_PAGES),
+            v_words.rearrange("u p e t -> p u (e t)").bitcast(I32),
+        )
 
         def listed(h):
             return offs_t[:, h * PAGE // LIST : (h + 1) * PAGE // LIST]
@@ -82,10 +96,12 @@ def tile_attend_pkv8q_soft_draft_gate_kernel(
         pos_row = [sb.tile([P, PAGE], F32, name=f"pos_row{h}", align_bytes=64) for h in range(PAGES)]
         pos_col = [sb.tile([P, PACK], F32, name=f"pos_col{h}", align_bytes=64) for h in range(PAGES)]
         side = [sb.tile([P, PACK, P], F32, name=f"side{h}", align_bytes=64) for h in range(PAGES)]
-        cap = [sb.tile([P, PACK, P], F32, name=f"cap{h}", align_bytes=64) for h in range(PAGES)]
+        cap = [
+            big.tile([P, PACK, P], F32, name=f"cap{h}", align_bytes=64, offset=12 * T + 4 * PAGE * h) for h in range(PAGES)
+        ]
         ks = sb.tile([P, N], U8, align_bytes=64)
         for h in range(PAGES):
-            nc.vector.tensor_copy(pos_row[h][:], pos_pool[:].indirect(listed(h)))
+            nc.vector.tensor_tensor(pos_row[h][:], pos_pool[:].indirect(listed(h)), ones[:], ALU.mult)
         for h in range(PAGES):
             turned = ps.tile([P, PACK, P], F32, name=f"pos_turned{h}", tag=f"turn{h}")
             for c in range(PACK):
@@ -104,7 +120,7 @@ def tile_attend_pkv8q_soft_draft_gate_kernel(
             nc.vector.tensor_copy(ks[:, h * PAGE : (h + 1) * PAGE], ks_pool[:].indirect(listed(h)))
         vs_row = [sb.tile([P, PAGE], F32, name=f"vs_row{h}", align_bytes=64) for h in range(PAGES)]
         for h in range(PAGES):
-            nc.vector.tensor_copy(vs_row[h][:], vs_pool[:].indirect(listed(h)))
+            nc.vector.tensor_tensor(vs_row[h][:], vs_pool[:].indirect(listed(h)), ones[:], ALU.mult)
 
         kw = big.tile([P, N], U32, align_bytes=64, offset=8 * T)
         s = sb.tile([P, PAGES, PACK, P], F32, align_bytes=64)
@@ -122,19 +138,6 @@ def tile_attend_pkv8q_soft_draft_gate_kernel(
                 stop=True,
             )
             raw.append(bank)
-
-        vw_pool = big.tile([P, POOL_PAGES * DV], I32, align_bytes=64, offset=0)
-        vsc_pool = big.tile([P, POOL_PAGES * DV], U8, align_bytes=64, offset=4 * POOL_PAGES * DV)
-        nc.gpsimd.memset(vsc_pool[:].bitcast(I32), 0)
-        nc.sync.dma_start(
-            vw_pool[:].rearrange("p (u e) -> p u e", u=POOL_PAGES),
-            v_words.rearrange("u p e t -> p u (e t)").bitcast(I32),
-        )
-        for quad in range(4):
-            nc.sync.dma_start(
-                vsc_pool[32 * quad : 32 * quad + 4, :].bitcast(I32).rearrange("p (u e) -> p u e", u=POOL_PAGES),
-                v_scales[:, 4 * quad : 4 * quad + 4, :].rearrange("u f e -> f u e").bitcast(I32),
-            )
 
         for h in range(PAGES):
             nc.vector.scalar_tensor_tensor(
@@ -162,6 +165,11 @@ def tile_attend_pkv8q_soft_draft_gate_kernel(
                     accum_out=sums[:, 2 * h + u : 2 * h + u + 1],
                 )
 
+        vw = big.tile([P, PAGES * DV], U32, align_bytes=64, offset=12 * T + 4 * PAGE)
+        vsc = big.tile([P, PAGES * DV], U8, align_bytes=64, offset=12 * T + 4 * PAGE + 4 * PAGES * DV)
+        nc.vector.tensor_copy(vsc[:], vsc_pool[:].indirect(voffs_t[:]))
+        nc.vector.tensor_copy(vw[:], vw_pool[:].bitcast(U32).indirect(voffs_t[:]))
+
         vs_col = [sb.tile([P, PACK], F32, name=f"vs_col{h}", align_bytes=64) for h in range(PAGES)]
         for h in range(PAGES):
             turned = ps.tile([P, PACK, P], F32, name=f"vs_turned{h}", tag=f"raw{h}")
@@ -169,10 +177,6 @@ def tile_attend_pkv8q_soft_draft_gate_kernel(
                 nc.tensor.transpose(turned[:, t, :], vs_row[h][:, t:PAGE:PACK], ident[:])
             nc.vector.tensor_copy(vs_col[h][:], turned[:, :, ROW])
 
-        vw = sb.tile([P, PAGES * DV], U32, align_bytes=64)
-        vsc = sb.tile([P, PAGES * DV], U8, align_bytes=64)
-        nc.vector.tensor_copy(vw[:], vw_pool[:].bitcast(U32).indirect(voffs_t[:]))
-        nc.vector.tensor_copy(vsc[:], vsc_pool[:].indirect(voffs_t[:]))
 
         acc = ps.tile([P, DV], F32, tag="acc")
         w = [sb.tile([P, NQ, PACK], BF16, name=f"w{h}", align_bytes=64) for h in range(PAGES)]

@@ -23,6 +23,7 @@ LIST = 16
 ROW = P - 1
 MASKED = -30000.0
 NO_CAP = 1e38
+CHUNKS = [(0, 128), (128, 384), (512, 384), (896, 128)]
 
 FLOPS = 2 * NQ * N * D + 2 * NQ * N * DV
 BYTES = T * D + 16 * T + T * DV + 16 * 8 * DV + D * NQ + 16 * NQ + 2 * 4 * T + 4 * NQ + 2 * 4 * NQ * DV + 2 * P * (N + 256) // 16
@@ -34,29 +35,25 @@ def tile_attend_pkv8q_soft_draft_gate_kernel(
     nc = tc.nc
     with ExitStack() as ctx:
         sb = ctx.enter_context(tc.tile_pool(name="sb", bufs=1))
-        big = ctx.enter_context(tc.tile_pool(name="big", bufs=1))
         ps = ctx.enter_context(tc.psum_pool(name="ps", bufs=1))
 
         offs_t = sb.tile([P, N // LIST], U16)
         voffs_t = sb.tile([P, PAGES * DV // LIST], U16)
-        kw_pool = big.tile([P, T], I32, align_bytes=64, offset=0)
-        pos_pool = big.tile([P, T], F32, align_bytes=64, offset=4 * T)
+        kw_pool = sb.tile([P, T], I32, align_bytes=64, tag="keys_then_value_scales")
         ks_pool = sb.tile([P, T], U8, align_bytes=64)
+        vw_pool = sb.tile([P, POOL_PAGES * DV], I32, align_bytes=64)
+        pos_pool = sb.tile([P, T], F32, align_bytes=64)
+        vs_pool = sb.tile([P, T], F32, align_bytes=64)
         qw = sb.tile([P, NQ], I32, align_bytes=64)
         qs = sb.tile([P, NQ], U8, align_bytes=64)
         qpos_t = sb.tile([P, 1], F32)
         og_t = sb.tile([P, DV], F32)
         ident = sb.tile([P, P], F32, align_bytes=64)
-        warm = big.tile([P, 1], F32, align_bytes=64, offset=8 * T)
-        ones = sb.tile([P, PAGE], F32, align_bytes=64)
-        vw_pool = sb.tile([P, POOL_PAGES * DV], I32, align_bytes=64)
-        vsc_pool = sb.tile([P, POOL_PAGES * DV], U8, align_bytes=64)
+        warm = sb.tile([P, 1], F32)
 
         make_identity(nc, ident[:])
         nc.gpsimd.memset(qs[:].bitcast(I32), 0)
-        nc.gpsimd.memset(vsc_pool[:].bitcast(I32), 0)
         nc.vector.memset(ks_pool[:].bitcast(I32), 0)
-        nc.vector.memset(ones[:], 1.0)
         nc.vector.memset(pos_pool[0:ROW, :], 0.0)
 
         nc.sync.dma_start(offs_t[:], offs)
@@ -68,40 +65,31 @@ def tile_attend_pkv8q_soft_draft_gate_kernel(
                 ks_pool[32 * quad : 32 * quad + 4, :].bitcast(I32),
                 k_scales[0, 4 * quad : 4 * quad + 4, :].bitcast(I32),
             )
-        nc.scalar.activation(warm[:], ones[:, 0:1], ACT.Exp)
-        vs_pool = big.tile([P, T], F32, align_bytes=64, offset=8 * T)
-        nc.scalar.dma_start(vs_pool[ROW:P, :], vs[0:1, :])
-        nc.gpsimd.memset(vs_pool[0:ROW, :], 0.0)
+        nc.scalar.activation(warm[:], qpos_t[:, 0:1], ACT.Exp, scale=0.0)
         nc.sync.dma_start(qw[:], q_words[0, 0].rearrange("p n t -> p (n t)").bitcast(I32))
         for quad in range(4):
             nc.sync.dma_start(
                 qs[32 * quad : 32 * quad + 4, :].bitcast(I32),
                 q_scales[0, 0, 4 * quad : 4 * quad + 4, :].bitcast(I32),
             )
-        nc.sync.dma_start(voffs_t[:], voffs)
-        for quad in range(4):
-            nc.sync.dma_start(
-                vsc_pool[32 * quad : 32 * quad + 4, :].bitcast(I32).rearrange("p (u e) -> p u e", u=POOL_PAGES),
-                v_scales[:, 4 * quad : 4 * quad + 4, :].rearrange("u f e -> f u e").bitcast(I32),
-            )
         nc.sync.dma_start(og_t[:], og[0])
+        nc.sync.dma_start(vs_pool[:], vs)
+        nc.sync.dma_start(voffs_t[:], voffs)
         nc.sync.dma_start(
             vw_pool[:].rearrange("p (u e) -> p u e", u=POOL_PAGES),
             v_words.rearrange("u p e t -> p u (e t)").bitcast(I32),
         )
 
-        def listed(h):
-            return offs_t[:, h * PAGE // LIST : (h + 1) * PAGE // LIST]
+        def listed(first, count):
+            return offs_t[:, first // LIST : (first + count) // LIST]
 
         pos_row = [sb.tile([P, PAGE], F32, name=f"pos_row{h}", align_bytes=64) for h in range(PAGES)]
         pos_col = [sb.tile([P, PACK], F32, name=f"pos_col{h}", align_bytes=64) for h in range(PAGES)]
-        side = [sb.tile([P, PACK, P], F32, name=f"side{h}", align_bytes=64) for h in range(PAGES)]
-        cap = [
-            big.tile([P, PACK, P], F32, name=f"cap{h}", align_bytes=64, offset=12 * T + 4 * PAGE * h) for h in range(PAGES)
-        ]
+        side = [sb.tile([P, PAGE], F32, name=f"side{h}", align_bytes=64) for h in range(PAGES)]
+        cap = [sb.tile([P, PAGE], F32, name=f"cap{h}", align_bytes=64) for h in range(PAGES)]
         ks = sb.tile([P, N], U8, align_bytes=64)
         for h in range(PAGES):
-            nc.vector.tensor_tensor(pos_row[h][:], pos_pool[:].indirect(listed(h)), ones[:], ALU.mult)
+            nc.vector.tensor_copy(pos_row[h][:], pos_pool[:].indirect(listed(h * PAGE, PAGE)))
         for h in range(PAGES):
             turned = ps.tile([P, PACK, P], F32, name=f"pos_turned{h}", tag=f"turn{h}")
             for c in range(PACK):
@@ -112,21 +100,18 @@ def tile_attend_pkv8q_soft_draft_gate_kernel(
                 nc.tensor.transpose(
                     spread[:, c * P : (c + 1) * P], pos_col[h][:, c : c + 1].to_broadcast([P, P]), ident[:]
                 )
-            nc.scalar.activation(
-                side[h][:], spread[:].rearrange("p (j t) -> p t j", t=PACK), ACT.Sign, scale=-1.0, bias=qpos_t[:, 0:1]
-            )
+            nc.scalar.activation(side[h][:], spread[:], ACT.Sign, scale=-1.0, bias=qpos_t[:, 0:1])
             nc.scalar.activation(cap[h][:], side[h][:], ACT.Copy, scale=NO_CAP, bias=NO_CAP)
         for h in range(PAGES):
-            nc.vector.tensor_copy(ks[:, h * PAGE : (h + 1) * PAGE], ks_pool[:].indirect(listed(h)))
-        vs_row = [sb.tile([P, PAGE], F32, name=f"vs_row{h}", align_bytes=64) for h in range(PAGES)]
-        for h in range(PAGES):
-            nc.vector.tensor_tensor(vs_row[h][:], vs_pool[:].indirect(listed(h)), ones[:], ALU.mult)
+            nc.vector.tensor_copy(ks[:, h * PAGE : (h + 1) * PAGE], ks_pool[:].indirect(listed(h * PAGE, PAGE)))
 
-        kw = big.tile([P, N], U32, align_bytes=64, offset=8 * T)
-        s = sb.tile([P, PAGES, PACK, P], F32, align_bytes=64)
+        kw = sb.tile([P, N], U32, align_bytes=64)
+        s = sb.tile([P, N], F32, align_bytes=64)
         raw = []
         for h in range(PAGES):
-            nc.vector.tensor_copy(kw[:, h * PAGE : (h + 1) * PAGE], kw_pool[:].bitcast(U32).indirect(listed(h)))
+            nc.vector.tensor_copy(
+                kw[:, h * PAGE : (h + 1) * PAGE], kw_pool[:].bitcast(U32).indirect(listed(h * PAGE, PAGE))
+            )
             bank = ps.tile([P, PAGE], F32, name=f"raw{h}", tag=f"raw{h}")
             nc.tensor.matmul_mx(
                 out=bank[:],
@@ -139,67 +124,62 @@ def tile_attend_pkv8q_soft_draft_gate_kernel(
             )
             raw.append(bank)
 
+        vsc_pool = sb.tile([P, POOL_PAGES * DV], U8, align_bytes=64, tag="keys_then_value_scales")
+        nc.gpsimd.memset(vsc_pool[:].bitcast(I32), 0)
+        for quad in range(4):
+            nc.scalar.dma_start(
+                vsc_pool[32 * quad : 32 * quad + 4, :].bitcast(I32).rearrange("p (u e) -> p u e", u=POOL_PAGES),
+                v_scales[:, 4 * quad : 4 * quad + 4, :].rearrange("u f e -> f u e").bitcast(I32),
+            )
+
         for h in range(PAGES):
             nc.vector.scalar_tensor_tensor(
-                s[:, h], cap[h][:], MASKED, raw[h][:].rearrange("p (j t) -> p t j", t=PACK), ALU.add, ALU.min
+                s[:, h * PAGE : (h + 1) * PAGE], cap[h][:], MASKED, raw[h][:], ALU.add, ALU.min
             )
         neg_m = sb.tile([P, 1], F32)
-        nc.vector.tensor_reduce(
-            neg_m[:], s[:].rearrange("p h t j -> p (h t j)"), mybir.AxisListType.X, ALU.max, negate=True
-        )
+        nc.vector.tensor_reduce(neg_m[:], s[:], mybir.AxisListType.X, ALU.max, negate=True)
 
         gate_t = sb.tile([P, DV], F32)
         gate = sb.tile([P, DV], F32)
         nc.scalar.activation(gate_t[:], og_t[:], ACT.Tanh, scale=0.5)
         nc.scalar.activation(gate[:], gate_t[:], ACT.Copy, scale=0.5, bias=0.5)
 
-        p = [sb.tile([P, PACK, P], F32, name=f"p{h}", align_bytes=64) for h in range(PAGES)]
-        sums = sb.tile([P, 2 * PAGES], F32)
-        for h in range(PAGES):
-            for u in range(2):
-                nc.scalar.activation(
-                    p[h][:, 2 * u : 2 * u + 2, :],
-                    s[:, h, 2 * u : 2 * u + 2, :],
-                    ACT.Exp,
-                    bias=neg_m[:, 0:1],
-                    accum_out=sums[:, 2 * h + u : 2 * h + u + 1],
-                )
+        p = [sb.tile([P, n], F32, name=f"p{c}", tag=f"p{c}", align_bytes=64) for c, (first, n) in enumerate(CHUNKS)]
+        w32 = [sb.tile([P, n], F32, name=f"w32_{c}", align_bytes=64) for c, (first, n) in enumerate(CHUNKS)]
+        w = [sb.tile([P, PAGE], BF16, name=f"w{h}", align_bytes=64) for h in range(PAGES)]
+        sums = sb.tile([P, len(CHUNKS)], F32)
+        for c, (first, n) in enumerate(CHUNKS):
+            nc.scalar.activation(
+                p[c][:], s[:, first : first + n], ACT.Exp, bias=neg_m[:, 0:1], accum_out=sums[:, c : c + 1]
+            )
+        for c, (first, n) in enumerate(CHUNKS):
+            nc.vector.tensor_tensor(w32[c][:], vs_pool[:].indirect(listed(first, n)), p[c][:], ALU.mult)
+        for c, (first, n) in enumerate(CHUNKS):
+            h, within = divmod(first, PAGE)
+            nc.scalar.activation(w[h][:, within : within + n], w32[c][:], ACT.Copy)
 
-        vw = big.tile([P, PAGES * DV], U32, align_bytes=64, offset=12 * T + 4 * PAGE)
-        vsc = big.tile([P, PAGES * DV], U8, align_bytes=64, offset=12 * T + 4 * PAGE + 4 * PAGES * DV)
-        nc.vector.tensor_copy(vsc[:], vsc_pool[:].indirect(voffs_t[:]))
-        nc.vector.tensor_copy(vw[:], vw_pool[:].bitcast(U32).indirect(voffs_t[:]))
-
-        vs_col = [sb.tile([P, PACK], F32, name=f"vs_col{h}", align_bytes=64) for h in range(PAGES)]
-        for h in range(PAGES):
-            turned = ps.tile([P, PACK, P], F32, name=f"vs_turned{h}", tag=f"raw{h}")
-            for t in range(PACK):
-                nc.tensor.transpose(turned[:, t, :], vs_row[h][:, t:PAGE:PACK], ident[:])
-            nc.vector.tensor_copy(vs_col[h][:], turned[:, :, ROW])
-
-
-        acc = ps.tile([P, DV], F32, tag="acc")
-        w = [sb.tile([P, NQ, PACK], BF16, name=f"w{h}", align_bytes=64) for h in range(PAGES)]
-        codes = [sb.tile([P, NQ], U32, name=f"codes{h}", align_bytes=64) for h in range(PAGES)]
-        scales = [sb.tile([P, NQ], U8, name=f"scales{h}", align_bytes=64) for h in range(PAGES)]
-        total = sb.tile([P, 1], F32)
+        vw = sb.tile([P, PAGES * DV], U32, tag="p3", align_bytes=64)
+        vsc = sb.tile([P, PAGES * DV], U8, tag="p2", align_bytes=64)
+        total = sb.tile([P, 1], F32, tag="p1", align_bytes=64)
         inv = sb.tile([P, 1], F32)
         nc.vector.tensor_reduce(total[:], sums[:], mybir.AxisListType.X, ALU.add)
-        for h in range(PAGES):
-            turned = ps.tile([P, PACK, NQ], F32, name=f"p_turned{h}", tag=f"wide{h}")
-            for t in range(PACK):
-                nc.tensor.transpose(turned[:, t, :], p[h][:, t, :], ident[:])
-            nc.vector.tensor_tensor(
-                w[h][:],
-                turned[:].rearrange("p t q -> p q t"),
-                vs_col[h][:].unsqueeze(1).to_broadcast([P, NQ, PACK]),
-                ALU.mult,
-            )
-        for h in range(PAGES):
-            nc.vector.quantize_mx(
-                out=codes[h][:].bitcast(FP8X4), scales=scales[h][:], in_=w[h][:].rearrange("p q t -> p (q t)")
-            )
+        nc.vector.tensor_copy(vsc[:], vsc_pool[:].indirect(voffs_t[:]))
         nc.vector.reciprocal(inv[:], total[:])
+        nc.vector.tensor_copy(vw[:], vw_pool[:].bitcast(U32).indirect(voffs_t[:]))
+
+        acc = ps.tile([P, DV], F32, tag="acc")
+        wt = [sb.tile([P, NQ, PACK], BF16, name=f"wt{h}", align_bytes=64) for h in range(PAGES)]
+        codes = [sb.tile([P, NQ], U32, name=f"codes{h}", align_bytes=64) for h in range(PAGES)]
+        scales = [sb.tile([P, NQ], U8, name=f"scales{h}", align_bytes=64) for h in range(PAGES)]
+        for h in range(PAGES):
+            pairs = w[h][:].bitcast(F32)
+            turned = ps.tile([P, 2, NQ], F32, name=f"w_turned{h}", tag=f"wide{h}")
+            for u in range(2):
+                nc.tensor.transpose(turned[:, u, :], pairs[:, u : PAGE // 2 : 2], ident[:])
+            nc.scalar.copy(wt[h][:].bitcast(F32), turned[:].rearrange("p u q -> p q u"))
+            nc.vector.quantize_mx(
+                out=codes[h][:].bitcast(FP8X4), scales=scales[h][:], in_=wt[h][:].rearrange("p q t -> p (q t)")
+            )
         for h in range(PAGES):
             nc.tensor.matmul_mx(
                 out=acc[:],

@@ -21,9 +21,8 @@ POOL_PAGES = T // PAGE
 PACK = 4
 LIST = 16
 ROW = P - 1
-MASKED = -30000.0
-NO_CAP = 1e38
-CHUNKS = [(0, 128), (128, 384), (512, 384), (896, 128)]
+STEEP = 2.0**96
+HIDDEN = 2.0**72
 
 FLOPS = 2 * NQ * N * D + 2 * NQ * N * DV
 BYTES = T * D + 16 * T + T * DV + 16 * 8 * DV + D * NQ + 16 * NQ + 2 * 4 * T + 4 * NQ + 2 * 4 * NQ * DV + 2 * P * (N + 256) // 16
@@ -35,6 +34,7 @@ def tile_attend_pkv8q_soft_draft_gate_kernel(
     nc = tc.nc
     with ExitStack() as ctx:
         sb = ctx.enter_context(tc.tile_pool(name="sb", bufs=1))
+        late = ctx.enter_context(tc.tile_pool(name="late", bufs=1))
         ps = ctx.enter_context(tc.psum_pool(name="ps", bufs=1))
 
         offs_t = sb.tile([P, N // LIST], U16)
@@ -44,12 +44,12 @@ def tile_attend_pkv8q_soft_draft_gate_kernel(
         vw_pool = sb.tile([P, POOL_PAGES * DV], I32, align_bytes=64)
         pos_pool = sb.tile([P, T], F32, align_bytes=64)
         vs_pool = sb.tile([P, T], F32, align_bytes=64)
+        vs_src = sb.tile([P, POOL_PAGES, PACK], F32, align_bytes=64)
         qw = sb.tile([P, NQ], I32, align_bytes=64)
         qs = sb.tile([P, NQ], U8, align_bytes=64)
         qpos_t = sb.tile([P, 1], F32)
         og_t = sb.tile([P, DV], F32)
         ident = sb.tile([P, P], F32, align_bytes=64)
-        warm = sb.tile([P, 1], F32)
 
         make_identity(nc, ident[:])
         nc.gpsimd.memset(qs[:].bitcast(I32), 0)
@@ -59,13 +59,13 @@ def tile_attend_pkv8q_soft_draft_gate_kernel(
         nc.sync.dma_start(offs_t[:], offs)
         nc.sync.dma_start(pos_pool[ROW:P, :], pos[0:1, :])
         nc.sync.dma_start(kw_pool[:], k_words[0].rearrange("p n t -> p (n t)").bitcast(I32))
-        nc.scalar.dma_start(qpos_t[:], qpos[0])
+        nc.scalar.dma_start(vs_src[:], vs[0:1, :].rearrange("o (u m t) -> (o m) u t", u=POOL_PAGES, t=PACK))
         for quad in range(4):
             nc.scalar.dma_start(
                 ks_pool[32 * quad : 32 * quad + 4, :].bitcast(I32),
                 k_scales[0, 4 * quad : 4 * quad + 4, :].bitcast(I32),
             )
-        nc.scalar.activation(warm[:], qpos_t[:, 0:1], ACT.Exp, scale=0.0)
+        nc.sync.dma_start(qpos_t[:], qpos[0])
         nc.sync.dma_start(qw[:], q_words[0, 0].rearrange("p n t -> p (n t)").bitcast(I32))
         for quad in range(4):
             nc.sync.dma_start(
@@ -73,7 +73,6 @@ def tile_attend_pkv8q_soft_draft_gate_kernel(
                 q_scales[0, 0, 4 * quad : 4 * quad + 4, :].bitcast(I32),
             )
         nc.sync.dma_start(og_t[:], og[0])
-        nc.sync.dma_start(vs_pool[:], vs)
         nc.sync.dma_start(voffs_t[:], voffs)
         nc.sync.dma_start(
             vw_pool[:].rearrange("p (u e) -> p u e", u=POOL_PAGES),
@@ -83,30 +82,45 @@ def tile_attend_pkv8q_soft_draft_gate_kernel(
         def listed(first, count):
             return offs_t[:, first // LIST : (first + count) // LIST]
 
+        nc.scalar.activation(
+            vs_pool[:].rearrange("m (u q t) -> m u q t", u=POOL_PAGES, t=PACK),
+            vs_src[:].rearrange("m u (o t) -> m u o t", o=1).to_broadcast([P, POOL_PAGES, NQ, PACK]),
+            ACT.Copy,
+        )
+
         pos_row = [sb.tile([P, PAGE], F32, name=f"pos_row{h}", align_bytes=64) for h in range(PAGES)]
         pos_col = [sb.tile([P, PACK], F32, name=f"pos_col{h}", align_bytes=64) for h in range(PAGES)]
-        side = [sb.tile([P, PAGE], F32, name=f"side{h}", align_bytes=64) for h in range(PAGES)]
-        cap = [sb.tile([P, PAGE], F32, name=f"cap{h}", align_bytes=64) for h in range(PAGES)]
+        hid = late.tile([P, N], F32, align_bytes=64, offset=0)
+        edge = sb.tile([P, 1], F32)
         ks = sb.tile([P, N], U8, align_bytes=64)
         for h in range(PAGES):
             nc.vector.tensor_copy(pos_row[h][:], pos_pool[:].indirect(listed(h * PAGE, PAGE)))
+        nc.vector.tensor_copy(ks[:], ks_pool[:].indirect(offs_t[:]))
+        sizes = [sb.tile([P, PAGE], F32, name="sizes0", align_bytes=64)]
+        nc.vector.tensor_copy(sizes[0][:], vs_pool[:].indirect(listed(0, PAGE)))
+
+        spread = []
         for h in range(PAGES):
             turned = ps.tile([P, PACK, P], F32, name=f"pos_turned{h}", tag=f"turn{h}")
             for c in range(PACK):
                 nc.tensor.transpose(turned[:, c, :], pos_row[h][:, c * P : (c + 1) * P], ident[:])
             nc.scalar.copy(pos_col[h][:], turned[:, :, ROW])
-            spread = ps.tile([P, PAGE], F32, name=f"pos_all{h}", tag=f"wide{h}")
+            spread.append(ps.tile([P, PAGE], F32, name=f"pos_all{h}", tag=f"wide{h}"))
             for c in range(PACK):
                 nc.tensor.transpose(
-                    spread[:, c * P : (c + 1) * P], pos_col[h][:, c : c + 1].to_broadcast([P, P]), ident[:]
+                    spread[h][:, c * P : (c + 1) * P], pos_col[h][:, c : c + 1].to_broadcast([P, P]), ident[:]
                 )
-            nc.scalar.activation(side[h][:], spread[:], ACT.Sign, scale=-1.0, bias=qpos_t[:, 0:1])
-            nc.scalar.activation(cap[h][:], side[h][:], ACT.Copy, scale=NO_CAP, bias=NO_CAP)
+        nc.scalar.activation(edge[:], qpos_t[:], ACT.Copy, scale=-STEEP)
         for h in range(PAGES):
-            nc.vector.tensor_copy(ks[:, h * PAGE : (h + 1) * PAGE], ks_pool[:].indirect(listed(h * PAGE, PAGE)))
+            nc.scalar.activation(
+                hid[:, h * PAGE : (h + 1) * PAGE], spread[h][:], ACT.Relu, scale=STEEP, bias=edge[:, 0:1]
+            )
+        gate_t = sb.tile([P, DV], F32)
+        gate = sb.tile([P, DV], F32)
+        nc.scalar.activation(gate_t[:], og_t[:], ACT.Tanh, scale=0.5)
+        nc.scalar.activation(gate[:], gate_t[:], ACT.Copy, scale=0.5, bias=0.5)
 
         kw = sb.tile([P, N], U32, align_bytes=64)
-        s = sb.tile([P, N], F32, align_bytes=64)
         raw = []
         for h in range(PAGES):
             nc.vector.tensor_copy(
@@ -127,59 +141,65 @@ def tile_attend_pkv8q_soft_draft_gate_kernel(
         vsc_pool = sb.tile([P, POOL_PAGES * DV], U8, align_bytes=64, tag="keys_then_value_scales")
         nc.gpsimd.memset(vsc_pool[:].bitcast(I32), 0)
         for quad in range(4):
-            nc.scalar.dma_start(
+            nc.sync.dma_start(
                 vsc_pool[32 * quad : 32 * quad + 4, :].bitcast(I32).rearrange("p (u e) -> p u e", u=POOL_PAGES),
                 v_scales[:, 4 * quad : 4 * quad + 4, :].rearrange("u f e -> f u e").bitcast(I32),
             )
 
+        neg_s = sb.tile([P, N], F32, align_bytes=64)
         for h in range(PAGES):
             nc.vector.scalar_tensor_tensor(
-                s[:, h * PAGE : (h + 1) * PAGE], cap[h][:], MASKED, raw[h][:], ALU.add, ALU.min
+                neg_s[:, h * PAGE : (h + 1) * PAGE],
+                hid[:, h * PAGE : (h + 1) * PAGE],
+                HIDDEN,
+                raw[h][:],
+                ALU.min,
+                ALU.subtract,
             )
         neg_m = sb.tile([P, 1], F32)
-        nc.vector.tensor_reduce(neg_m[:], s[:], mybir.AxisListType.X, ALU.max, negate=True)
+        nc.vector.tensor_reduce(neg_m[:], neg_s[:], mybir.AxisListType.X, ALU.min)
 
-        gate_t = sb.tile([P, DV], F32)
-        gate = sb.tile([P, DV], F32)
-        nc.scalar.activation(gate_t[:], og_t[:], ACT.Tanh, scale=0.5)
-        nc.scalar.activation(gate[:], gate_t[:], ACT.Copy, scale=0.5, bias=0.5)
-
-        p = [sb.tile([P, n], F32, name=f"p{c}", tag=f"p{c}", align_bytes=64) for c, (first, n) in enumerate(CHUNKS)]
-        w32 = [sb.tile([P, n], F32, name=f"w32_{c}", align_bytes=64) for c, (first, n) in enumerate(CHUNKS)]
-        w = [sb.tile([P, PAGE], BF16, name=f"w{h}", align_bytes=64) for h in range(PAGES)]
-        sums = sb.tile([P, len(CHUNKS)], F32)
-        for c, (first, n) in enumerate(CHUNKS):
+        p = [sb.tile([P, PACK, P], F32, name=f"p{h}", align_bytes=64) for h in range(PAGES)]
+        sums = sb.tile([P, PAGES], F32)
+        for h in range(PAGES):
             nc.scalar.activation(
-                p[c][:], s[:, first : first + n], ACT.Exp, bias=neg_m[:, 0:1], accum_out=sums[:, c : c + 1]
+                p[h][:].rearrange("q t m -> q m t"),
+                neg_s[:, h * PAGE : (h + 1) * PAGE].rearrange("q (m t) -> q m t", t=PACK),
+                ACT.Exp,
+                scale=-1.0,
+                bias=neg_m[:, 0:1],
+                accum_out=sums[:, h : h + 1],
             )
-        for c, (first, n) in enumerate(CHUNKS):
-            nc.vector.tensor_tensor(w32[c][:], vs_pool[:].indirect(listed(first, n)), p[c][:], ALU.mult)
-        for c, (first, n) in enumerate(CHUNKS):
-            h, within = divmod(first, PAGE)
-            nc.scalar.activation(w[h][:, within : within + n], w32[c][:], ACT.Copy)
 
-        vw = sb.tile([P, PAGES * DV], U32, tag="p3", align_bytes=64)
-        vsc = sb.tile([P, PAGES * DV], U8, tag="p2", align_bytes=64)
-        total = sb.tile([P, 1], F32, tag="p1", align_bytes=64)
-        inv = sb.tile([P, 1], F32)
-        nc.vector.tensor_reduce(total[:], sums[:], mybir.AxisListType.X, ALU.add)
-        nc.vector.tensor_copy(vsc[:], vsc_pool[:].indirect(voffs_t[:]))
-        nc.vector.reciprocal(inv[:], total[:])
+        sizes.append(late.tile([P, PAGE], F32, name="sizes1", align_bytes=64, offset=0))
+        vw = late.tile([P, PAGES * DV], U32, align_bytes=64, offset=4 * PAGE)
+        vsc = late.tile([P, PAGES * DV], U8, align_bytes=64, offset=4 * PAGE + 4 * PAGES * DV)
+        nc.vector.tensor_copy(sizes[1][:], vs_pool[:].indirect(listed(PAGE, PAGE)))
         nc.vector.tensor_copy(vw[:], vw_pool[:].bitcast(U32).indirect(voffs_t[:]))
+        nc.vector.tensor_copy(vsc[:], vsc_pool[:].indirect(voffs_t[:]))
 
         acc = ps.tile([P, DV], F32, tag="acc")
         wt = [sb.tile([P, NQ, PACK], BF16, name=f"wt{h}", align_bytes=64) for h in range(PAGES)]
         codes = [sb.tile([P, NQ], U32, name=f"codes{h}", align_bytes=64) for h in range(PAGES)]
         scales = [sb.tile([P, NQ], U8, name=f"scales{h}", align_bytes=64) for h in range(PAGES)]
         for h in range(PAGES):
-            pairs = w[h][:].bitcast(F32)
-            turned = ps.tile([P, 2, NQ], F32, name=f"w_turned{h}", tag=f"wide{h}")
-            for u in range(2):
-                nc.tensor.transpose(turned[:, u, :], pairs[:, u : PAGE // 2 : 2], ident[:])
-            nc.scalar.copy(wt[h][:].bitcast(F32), turned[:].rearrange("p u q -> p q u"))
+            turned = ps.tile([P, PACK, NQ], F32, name=f"p_turned{h}", tag=f"turn{h}")
+            for t in range(PACK):
+                nc.tensor.transpose(turned[:, t, :], p[h][:, t, :], ident[:])
+            nc.vector.tensor_tensor(
+                wt[h][:],
+                turned[:].rearrange("m t q -> m q t"),
+                sizes[h][:].rearrange("m (q t) -> m q t", t=PACK),
+                ALU.mult,
+            )
+        for h in range(PAGES):
             nc.vector.quantize_mx(
                 out=codes[h][:].bitcast(FP8X4), scales=scales[h][:], in_=wt[h][:].rearrange("p q t -> p (q t)")
             )
+        total = sb.tile([P, 1], F32)
+        inv = sb.tile([P, 1], F32)
+        nc.vector.tensor_reduce(total[:], sums[:], mybir.AxisListType.X, ALU.add)
+        nc.vector.reciprocal(inv[:], total[:])
         for h in range(PAGES):
             nc.tensor.matmul_mx(
                 out=acc[:],

@@ -40,7 +40,7 @@ def tile_attend_pkv8q_soft_draft_gate_kernel(
         offs_t = sb.tile([P, N // LIST], U16)
         voffs_t = sb.tile([P, PAGES * DV // LIST], U16)
         kw_pool = sb.tile([P, T], I32, align_bytes=64, tag="keys_then_value_scales")
-        ks_pool = sb.tile([P, T], U8, align_bytes=64)
+        ks_pool = sb.tile([P, T], U8, align_bytes=64, tag="key_scales_then_sizes")
         vw_pool = sb.tile([P, POOL_PAGES * DV], I32, align_bytes=64)
         pos_pool = sb.tile([P, T], F32, align_bytes=64)
         vs_pool = sb.tile([P, T], F32, align_bytes=64)
@@ -58,13 +58,13 @@ def tile_attend_pkv8q_soft_draft_gate_kernel(
 
         nc.sync.dma_start(offs_t[:], offs)
         nc.sync.dma_start(pos_pool[ROW:P, :], pos[0:1, :])
-        nc.sync.dma_start(kw_pool[:], k_words[0].rearrange("p n t -> p (n t)").bitcast(I32))
         nc.scalar.dma_start(vs_src[:], vs[0:1, :].rearrange("o (u m t) -> (o m) u t", u=POOL_PAGES, t=PACK))
         for quad in range(4):
-            nc.scalar.dma_start(
+            nc.sync.dma_start(
                 ks_pool[32 * quad : 32 * quad + 4, :].bitcast(I32),
                 k_scales[0, 4 * quad : 4 * quad + 4, :].bitcast(I32),
             )
+        nc.sync.dma_start(kw_pool[:], k_words[0].rearrange("p n t -> p (n t)").bitcast(I32))
         nc.sync.dma_start(qpos_t[:], qpos[0])
         nc.sync.dma_start(qw[:], q_words[0, 0].rearrange("p n t -> p (n t)").bitcast(I32))
         for quad in range(4):
@@ -96,7 +96,7 @@ def tile_attend_pkv8q_soft_draft_gate_kernel(
         for h in range(PAGES):
             nc.vector.tensor_copy(pos_row[h][:], pos_pool[:].indirect(listed(h * PAGE, PAGE)))
         nc.vector.tensor_copy(ks[:], ks_pool[:].indirect(offs_t[:]))
-        sizes = [sb.tile([P, PAGE], F32, name="sizes0", align_bytes=64)]
+        sizes = [sb.tile([P, PAGE], F32, name="sizes0", align_bytes=64, tag="key_scales_then_sizes")]
         nc.vector.tensor_copy(sizes[0][:], vs_pool[:].indirect(listed(0, PAGE)))
 
         spread = []

@@ -39,7 +39,8 @@ def tile_attend_pkv8q_soft_draft_gate_kernel(
 
         offs_t = sb.tile([P, N // LIST], U16)
         voffs_t = sb.tile([P, PAGES * DV // LIST], U16)
-        kw_pool = sb.tile([P, T], I32, align_bytes=64, tag="keys_then_value_scales")
+        kw_pool = sb.tile([P, T], I32, align_bytes=64)
+        vsc_pool = sb.tile([P, POOL_PAGES * DV], U8, align_bytes=64)
         ks_pool = sb.tile([P, T], U8, align_bytes=64, tag="key_scales_then_sizes")
         vw_pool = sb.tile([P, POOL_PAGES * DV], I32, align_bytes=64)
         pos_pool = sb.tile([P, T], F32, align_bytes=64)
@@ -53,17 +54,15 @@ def tile_attend_pkv8q_soft_draft_gate_kernel(
 
         make_identity(nc, ident[:])
         nc.gpsimd.memset(qs[:].bitcast(I32), 0)
+        nc.gpsimd.memset(vsc_pool[:].bitcast(I32), 0)
         nc.vector.memset(ks_pool[:].bitcast(I32), 0)
         nc.vector.memset(pos_pool[0:ROW, :], 0.0)
 
         nc.sync.dma_start(offs_t[:], offs)
         nc.sync.dma_start(pos_pool[ROW:P, :], pos[0:1, :])
         nc.scalar.dma_start(vs_src[:], vs[0:1, :].rearrange("o (u m t) -> (o m) u t", u=POOL_PAGES, t=PACK))
-        for quad in range(4):
-            nc.sync.dma_start(
-                ks_pool[32 * quad : 32 * quad + 4, :].bitcast(I32),
-                k_scales[0, 4 * quad : 4 * quad + 4, :].bitcast(I32),
-            )
+        for r in range(4):
+            nc.sync.dma_start(ks_pool[r:P:32, :].bitcast(I32), k_scales[0, r:16:4, :].bitcast(I32))
         nc.sync.dma_start(kw_pool[:], k_words[0].rearrange("p n t -> p (n t)").bitcast(I32))
         nc.sync.dma_start(qpos_t[:], qpos[0])
         nc.sync.dma_start(qw[:], q_words[0, 0].rearrange("p n t -> p (n t)").bitcast(I32))
@@ -72,12 +71,17 @@ def tile_attend_pkv8q_soft_draft_gate_kernel(
                 qs[32 * quad : 32 * quad + 4, :].bitcast(I32),
                 q_scales[0, 0, 4 * quad : 4 * quad + 4, :].bitcast(I32),
             )
-        nc.sync.dma_start(og_t[:], og[0])
-        nc.sync.dma_start(voffs_t[:], voffs)
         nc.sync.dma_start(
             vw_pool[:].rearrange("p (u e) -> p u e", u=POOL_PAGES),
             v_words.rearrange("u p e t -> p u (e t)").bitcast(I32),
         )
+        nc.sync.dma_start(voffs_t[:], voffs)
+        nc.sync.dma_start(og_t[:], og[0])
+        for r in range(4):
+            nc.sync.dma_start(
+                vsc_pool[r:P:32, :].bitcast(I32).rearrange("p (u e) -> p u e", u=POOL_PAGES),
+                v_scales[:, r:16:4, :].rearrange("u f e -> f u e").bitcast(I32),
+            )
 
         def listed(first, count):
             return offs_t[:, first // LIST : (first + count) // LIST]
@@ -137,14 +141,6 @@ def tile_attend_pkv8q_soft_draft_gate_kernel(
                 stop=True,
             )
             raw.append(bank)
-
-        vsc_pool = sb.tile([P, POOL_PAGES * DV], U8, align_bytes=64, tag="keys_then_value_scales")
-        nc.gpsimd.memset(vsc_pool[:].bitcast(I32), 0)
-        for quad in range(4):
-            nc.sync.dma_start(
-                vsc_pool[32 * quad : 32 * quad + 4, :].bitcast(I32).rearrange("p (u e) -> p u e", u=POOL_PAGES),
-                v_scales[:, 4 * quad : 4 * quad + 4, :].rearrange("u f e -> f u e").bitcast(I32),
-            )
 
         neg_s = sb.tile([P, N], F32, align_bytes=64)
         for h in range(PAGES):

@@ -21,6 +21,7 @@ POOL_PAGES = T // PAGE
 PACK = 4
 LIST = 16
 ROW = P - 1
+HEAD = 1536
 STEEP = 2.0**96
 HIDDEN = 2.0**72
 
@@ -40,8 +41,8 @@ def tile_attend_pkv8q_soft_draft_gate_kernel(
         offs_t = sb.tile([P, N // LIST], U16)
         voffs_t = sb.tile([P, PAGES * DV // LIST], U16)
         kw_pool = sb.tile([P, T], I32, align_bytes=64)
-        vsc_pool = sb.tile([P, POOL_PAGES * DV], U8, align_bytes=64)
-        ks_pool = sb.tile([P, T], U8, align_bytes=64, tag="key_scales_then_sizes")
+        vsc_pool = sb.tile([P, POOL_PAGES * DV], U8, align_bytes=64, tag="wt1")
+        ks_pool = sb.tile([P, T], U8, align_bytes=64)
         vw_pool = sb.tile([P, POOL_PAGES * DV], I32, align_bytes=64)
         pos_pool = sb.tile([P, T], F32, align_bytes=64)
         vs_pool = sb.tile([P, T], F32, align_bytes=64)
@@ -60,10 +61,13 @@ def tile_attend_pkv8q_soft_draft_gate_kernel(
 
         nc.sync.dma_start(offs_t[:], offs)
         nc.sync.dma_start(pos_pool[ROW:P, :], pos[0:1, :])
+        nc.scalar.dma_start(og_t[:], og[0])
         nc.scalar.dma_start(vs_src[:], vs[0:1, :].rearrange("o (u m t) -> (o m) u t", u=POOL_PAGES, t=PACK))
+        k_all = k_words[0].rearrange("p n t -> p (n t)").bitcast(I32)
+        nc.sync.dma_start(kw_pool[:, 0:HEAD], k_all[:, 0:HEAD])
         for r in range(4):
             nc.sync.dma_start(ks_pool[r:P:32, :].bitcast(I32), k_scales[0, r:16:4, :].bitcast(I32))
-        nc.sync.dma_start(kw_pool[:], k_words[0].rearrange("p n t -> p (n t)").bitcast(I32))
+        nc.sync.dma_start(kw_pool[:, HEAD:T], k_all[:, HEAD:T])
         nc.sync.dma_start(qpos_t[:], qpos[0])
         nc.sync.dma_start(qw[:], q_words[0, 0].rearrange("p n t -> p (n t)").bitcast(I32))
         for quad in range(4):
@@ -76,7 +80,6 @@ def tile_attend_pkv8q_soft_draft_gate_kernel(
             v_words.rearrange("u p e t -> p u (e t)").bitcast(I32),
         )
         nc.sync.dma_start(voffs_t[:], voffs)
-        nc.sync.dma_start(og_t[:], og[0])
         for r in range(4):
             nc.sync.dma_start(
                 vsc_pool[r:P:32, :].bitcast(I32).rearrange("p (u e) -> p u e", u=POOL_PAGES),
@@ -100,8 +103,6 @@ def tile_attend_pkv8q_soft_draft_gate_kernel(
         for h in range(PAGES):
             nc.vector.tensor_copy(pos_row[h][:], pos_pool[:].indirect(listed(h * PAGE, PAGE)))
         nc.vector.tensor_copy(ks[:], ks_pool[:].indirect(offs_t[:]))
-        sizes = [sb.tile([P, PAGE], F32, name="sizes0", align_bytes=64, tag="key_scales_then_sizes")]
-        nc.vector.tensor_copy(sizes[0][:], vs_pool[:].indirect(listed(0, PAGE)))
 
         spread = []
         for h in range(PAGES):
@@ -124,24 +125,24 @@ def tile_attend_pkv8q_soft_draft_gate_kernel(
         nc.scalar.activation(gate_t[:], og_t[:], ACT.Tanh, scale=0.5)
         nc.scalar.activation(gate[:], gate_t[:], ACT.Copy, scale=0.5, bias=0.5)
 
-        kw = sb.tile([P, N], U32, align_bytes=64)
         raw = []
         for h in range(PAGES):
-            nc.vector.tensor_copy(
-                kw[:, h * PAGE : (h + 1) * PAGE], kw_pool[:].bitcast(U32).indirect(listed(h * PAGE, PAGE))
-            )
+            kw = sb.tile([P, PAGE], U32, name=f"kw{h}", align_bytes=64, tag=f"keys{h}")
+            nc.vector.tensor_copy(kw[:], kw_pool[:].bitcast(U32).indirect(listed(h * PAGE, PAGE)))
             bank = ps.tile([P, PAGE], F32, name=f"raw{h}", tag=f"raw{h}")
             nc.tensor.matmul_mx(
                 out=bank[:],
                 lhsT=qw[:].bitcast(FP8X4),
                 lhsT_scale=qs[:],
-                rhs=kw[:, h * PAGE : (h + 1) * PAGE].bitcast(FP8X4),
+                rhs=kw[:].bitcast(FP8X4),
                 rhs_scale=ks[:, h * PAGE : (h + 1) * PAGE],
                 start=True,
                 stop=True,
             )
             raw.append(bank)
 
+        sizes = [sb.tile([P, PAGE], F32, name="sizes0", align_bytes=64, tag="keys0")]
+        nc.vector.tensor_copy(sizes[0][:], vs_pool[:].indirect(listed(0, PAGE)))
         neg_s = sb.tile([P, N], F32, align_bytes=64)
         for h in range(PAGES):
             nc.vector.scalar_tensor_tensor(
@@ -175,7 +176,7 @@ def tile_attend_pkv8q_soft_draft_gate_kernel(
         nc.vector.tensor_copy(vsc[:], vsc_pool[:].indirect(voffs_t[:]))
 
         acc = ps.tile([P, DV], F32, tag="acc")
-        wt = [sb.tile([P, NQ, PACK], BF16, name=f"wt{h}", align_bytes=64) for h in range(PAGES)]
+        wt = [sb.tile([P, NQ, PACK], BF16, name=f"wt{h}", align_bytes=64, tag=f"wt{h}") for h in range(PAGES)]
         codes = [sb.tile([P, NQ], U32, name=f"codes{h}", align_bytes=64) for h in range(PAGES)]
         scales = [sb.tile([P, NQ], U8, name=f"scales{h}", align_bytes=64) for h in range(PAGES)]
         for h in range(PAGES):

@@ -21,7 +21,6 @@ POOL_PAGES = T // PAGE
 PACK = 4
 LIST = 16
 ROW = P - 1
-HEAD = 1536
 STEEP = 2.0**96
 HIDDEN = 2.0**72
 
@@ -49,7 +48,7 @@ def tile_attend_pkv8q_soft_draft_gate_kernel(
         vs_src = sb.tile([P, POOL_PAGES, PACK], F32, align_bytes=64)
         qw = sb.tile([P, NQ], I32, align_bytes=64)
         qs = sb.tile([P, NQ], U8, align_bytes=64)
-        qpos_t = sb.tile([P, 1], F32)
+        qpos_t = sb.tile([P, 1], F32, align_bytes=64, tag="qpos_then_sizes")
         og_t = sb.tile([P, DV], F32)
         ident = sb.tile([P, P], F32, align_bytes=64)
 
@@ -61,13 +60,10 @@ def tile_attend_pkv8q_soft_draft_gate_kernel(
 
         nc.sync.dma_start(offs_t[:], offs)
         nc.sync.dma_start(pos_pool[ROW:P, :], pos[0:1, :])
-        nc.scalar.dma_start(og_t[:], og[0])
         nc.scalar.dma_start(vs_src[:], vs[0:1, :].rearrange("o (u m t) -> (o m) u t", u=POOL_PAGES, t=PACK))
-        k_all = k_words[0].rearrange("p n t -> p (n t)").bitcast(I32)
-        nc.sync.dma_start(kw_pool[:, 0:HEAD], k_all[:, 0:HEAD])
         for r in range(4):
             nc.sync.dma_start(ks_pool[r:P:32, :].bitcast(I32), k_scales[0, r:16:4, :].bitcast(I32))
-        nc.sync.dma_start(kw_pool[:, HEAD:T], k_all[:, HEAD:T])
+        nc.sync.dma_start(kw_pool[:], k_words[0].rearrange("p n t -> p (n t)").bitcast(I32))
         nc.sync.dma_start(qpos_t[:], qpos[0])
         nc.sync.dma_start(qw[:], q_words[0, 0].rearrange("p n t -> p (n t)").bitcast(I32))
         for quad in range(4):
@@ -85,6 +81,8 @@ def tile_attend_pkv8q_soft_draft_gate_kernel(
                 vsc_pool[r:P:32, :].bitcast(I32).rearrange("p (u e) -> p u e", u=POOL_PAGES),
                 v_scales[:, r:16:4, :].rearrange("u f e -> f u e").bitcast(I32),
             )
+
+        nc.sync.dma_start(og_t[:], og[0])
 
         def listed(first, count):
             return offs_t[:, first // LIST : (first + count) // LIST]
@@ -127,7 +125,7 @@ def tile_attend_pkv8q_soft_draft_gate_kernel(
 
         raw = []
         for h in range(PAGES):
-            kw = sb.tile([P, PAGE], U32, name=f"kw{h}", align_bytes=64, tag=f"keys{h}")
+            kw = sb.tile([P, PAGE], U32, name=f"kw{h}", align_bytes=64)
             nc.vector.tensor_copy(kw[:], kw_pool[:].bitcast(U32).indirect(listed(h * PAGE, PAGE)))
             bank = ps.tile([P, PAGE], F32, name=f"raw{h}", tag=f"raw{h}")
             nc.tensor.matmul_mx(
@@ -141,7 +139,7 @@ def tile_attend_pkv8q_soft_draft_gate_kernel(
             )
             raw.append(bank)
 
-        sizes = [sb.tile([P, PAGE], F32, name="sizes0", align_bytes=64, tag="keys0")]
+        sizes = [sb.tile([P, PAGE], F32, name="sizes0", align_bytes=64, tag="qpos_then_sizes")]
         nc.vector.tensor_copy(sizes[0][:], vs_pool[:].indirect(listed(0, PAGE)))
         neg_s = sb.tile([P, N], F32, align_bytes=64)
         for h in range(PAGES):

@@ -23,6 +23,7 @@ LIST = 16
 ROW = P - 1
 STEEP = 2.0**96
 HIDDEN = 2.0**72
+SCALAR_PAGES = 2
 
 FLOPS = 2 * NQ * N * D + 2 * NQ * N * DV
 BYTES = T * D + 16 * T + T * DV + 16 * 8 * DV + D * NQ + 16 * NQ + 2 * 4 * T + 4 * NQ + 2 * 4 * NQ * DV + 2 * P * (N + 256) // 16
@@ -48,7 +49,7 @@ def tile_attend_pkv8q_soft_draft_gate_kernel(
         vs_src = sb.tile([P, POOL_PAGES, PACK], F32, align_bytes=64)
         qw = sb.tile([P, NQ], I32, align_bytes=64)
         qs = sb.tile([P, NQ], U8, align_bytes=64)
-        qpos_t = sb.tile([P, 1], F32, align_bytes=64, tag="qpos_then_sizes")
+        qpos_t = sb.tile([P, 1], F32, align_bytes=64)
         og_t = sb.tile([P, DV], F32)
         ident = sb.tile([P, P], F32, align_bytes=64)
 
@@ -87,19 +88,18 @@ def tile_attend_pkv8q_soft_draft_gate_kernel(
         def listed(first, count):
             return offs_t[:, first // LIST : (first + count) // LIST]
 
-        nc.scalar.activation(
-            vs_pool[:].rearrange("m (u q t) -> m u q t", u=POOL_PAGES, t=PACK),
-            vs_src[:].rearrange("m u (o t) -> m u o t", o=1).to_broadcast([P, POOL_PAGES, NQ, PACK]),
-            ACT.Copy,
-        )
+        dealt = vs_pool[:].rearrange("m (u q t) -> m u q t", u=POOL_PAGES, t=PACK)
+        spread_src = vs_src[:].rearrange("m u (o t) -> m u o t", o=1).to_broadcast([P, POOL_PAGES, NQ, PACK])
+        nc.scalar.activation(dealt[:, :SCALAR_PAGES], spread_src[:, :SCALAR_PAGES], ACT.Copy)
+        nc.vector.tensor_copy(dealt[:, SCALAR_PAGES:], spread_src[:, SCALAR_PAGES:])
 
         pos_row = [sb.tile([P, PAGE], F32, name=f"pos_row{h}", align_bytes=64) for h in range(PAGES)]
         pos_col = [sb.tile([P, PACK], F32, name=f"pos_col{h}", align_bytes=64) for h in range(PAGES)]
         hid = late.tile([P, N], F32, align_bytes=64, offset=0)
-        edge = sb.tile([P, 1], F32)
+        edge = sb.tile([P, 1], F32, align_bytes=64, tag="edge_then_sizes")
         ks = sb.tile([P, N], U8, align_bytes=64)
         for h in range(PAGES):
-            nc.vector.tensor_copy(pos_row[h][:], pos_pool[:].indirect(listed(h * PAGE, PAGE)))
+            nc.scalar.activation(pos_row[h][:], pos_pool[:].indirect(listed(h * PAGE, PAGE)), ACT.Copy)
         nc.vector.tensor_copy(ks[:], ks_pool[:].indirect(offs_t[:]))
 
         spread = []
@@ -117,6 +117,11 @@ def tile_attend_pkv8q_soft_draft_gate_kernel(
         for h in range(PAGES):
             nc.scalar.activation(
                 hid[:, h * PAGE : (h + 1) * PAGE], spread[h][:], ACT.Relu, scale=STEEP, bias=edge[:, 0:1]
+            )
+        sizes = sb.tile([P, N], F32, align_bytes=64, tag="edge_then_sizes")
+        for h in range(PAGES):
+            nc.scalar.activation(
+                sizes[:, h * PAGE : (h + 1) * PAGE], vs_pool[:].indirect(listed(h * PAGE, PAGE)), ACT.Copy
             )
         gate_t = sb.tile([P, DV], F32)
         gate = sb.tile([P, DV], F32)
@@ -139,8 +144,6 @@ def tile_attend_pkv8q_soft_draft_gate_kernel(
             )
             raw.append(bank)
 
-        sizes = [sb.tile([P, PAGE], F32, name="sizes0", align_bytes=64, tag="qpos_then_sizes")]
-        nc.vector.tensor_copy(sizes[0][:], vs_pool[:].indirect(listed(0, PAGE)))
         neg_s = sb.tile([P, N], F32, align_bytes=64)
         for h in range(PAGES):
             nc.vector.scalar_tensor_tensor(
@@ -154,22 +157,23 @@ def tile_attend_pkv8q_soft_draft_gate_kernel(
         neg_m = sb.tile([P, 1], F32)
         nc.vector.tensor_reduce(neg_m[:], neg_s[:], mybir.AxisListType.X, ALU.min)
 
-        p = [sb.tile([P, PACK, P], F32, name=f"p{h}", align_bytes=64) for h in range(PAGES)]
-        sums = sb.tile([P, PAGES], F32)
-        for h in range(PAGES):
+        p = [sb.tile([P, 2, P], F32, name=f"p{j}", align_bytes=64) for j in range(2 * PAGES)]
+        sums = sb.tile([P, 2 * PAGES], F32)
+        for j in range(2 * PAGES):
+            h, half = divmod(j, 2)
             nc.scalar.activation(
-                p[h][:].rearrange("q t m -> q m t"),
-                neg_s[:, h * PAGE : (h + 1) * PAGE].rearrange("q (m t) -> q m t", t=PACK),
+                p[j][:].rearrange("q t m -> q m t"),
+                neg_s[:, h * PAGE : (h + 1) * PAGE].rearrange("q (m t) -> q m t", t=PACK)[
+                    :, :, 2 * half : 2 * half + 2
+                ],
                 ACT.Exp,
                 scale=-1.0,
                 bias=neg_m[:, 0:1],
-                accum_out=sums[:, h : h + 1],
+                accum_out=sums[:, j : j + 1],
             )
 
-        sizes.append(late.tile([P, PAGE], F32, name="sizes1", align_bytes=64, offset=0))
         vw = late.tile([P, PAGES * DV], U32, align_bytes=64, offset=4 * PAGE)
         vsc = late.tile([P, PAGES * DV], U8, align_bytes=64, offset=4 * PAGE + 4 * PAGES * DV)
-        nc.vector.tensor_copy(sizes[1][:], vs_pool[:].indirect(listed(PAGE, PAGE)))
         nc.vector.tensor_copy(vw[:], vw_pool[:].bitcast(U32).indirect(voffs_t[:]))
         nc.vector.tensor_copy(vsc[:], vsc_pool[:].indirect(voffs_t[:]))
 
@@ -180,11 +184,11 @@ def tile_attend_pkv8q_soft_draft_gate_kernel(
         for h in range(PAGES):
             turned = ps.tile([P, PACK, NQ], F32, name=f"p_turned{h}", tag=f"turn{h}")
             for t in range(PACK):
-                nc.tensor.transpose(turned[:, t, :], p[h][:, t, :], ident[:])
+                nc.tensor.transpose(turned[:, t, :], p[2 * h + t // 2][:, t % 2, :], ident[:])
             nc.vector.tensor_tensor(
                 wt[h][:],
                 turned[:].rearrange("m t q -> m q t"),
-                sizes[h][:].rearrange("m (q t) -> m q t", t=PACK),
+                sizes[:, h * PAGE : (h + 1) * PAGE].rearrange("m (q t) -> m q t", t=PACK),
                 ALU.mult,
             )
         for h in range(PAGES):

@@ -1,7 +1,6 @@
 from contextlib import ExitStack
 
 import concourse.mybir as mybir
-from concourse.masks import make_identity
 
 F32 = mybir.dt.float32
 BF16 = mybir.dt.bfloat16
@@ -23,7 +22,6 @@ LIST = 16
 ROW = P - 1
 STEEP = 2.0**96
 HIDDEN = 2.0**72
-SCALAR_PAGES = 2
 
 FLOPS = 2 * NQ * N * D + 2 * NQ * N * DV
 BYTES = T * D + 16 * T + T * DV + 16 * 8 * DV + D * NQ + 16 * NQ + 2 * 4 * T + 4 * NQ + 2 * 4 * NQ * DV + 2 * P * (N + 256) // 16
@@ -53,11 +51,15 @@ def tile_attend_pkv8q_soft_draft_gate_kernel(
         og_t = sb.tile([P, DV], F32)
         ident = sb.tile([P, P], F32, align_bytes=64)
 
-        make_identity(nc, ident[:])
+        ramp = sb.tile([P, P], F32, align_bytes=64)
+        dist = sb.tile([P, P], F32, align_bytes=64, tag="pos_rows")
+        nc.gpsimd.iota(ramp[:], [[1, P]], base=0, channel_multiplier=-1, allow_small_or_imprecise_dtypes=True)
+        nc.scalar.activation(dist[:], ramp[:], ACT.Abs)
+        nc.scalar.activation(ident[:], dist[:], ACT.Relu, scale=-1.0, bias=1.0)
         nc.gpsimd.memset(qs[:].bitcast(I32), 0)
-        nc.gpsimd.memset(vsc_pool[:].bitcast(I32), 0)
         nc.vector.memset(ks_pool[:].bitcast(I32), 0)
         nc.vector.memset(pos_pool[0:ROW, :], 0.0)
+        nc.vector.memset(vsc_pool[:].bitcast(I32), 0)
 
         nc.sync.dma_start(offs_t[:], offs)
         nc.sync.dma_start(pos_pool[ROW:P, :], pos[0:1, :])
@@ -88,19 +90,19 @@ def tile_attend_pkv8q_soft_draft_gate_kernel(
         def listed(first, count):
             return offs_t[:, first // LIST : (first + count) // LIST]
 
-        dealt = vs_pool[:].rearrange("m (u q t) -> m u q t", u=POOL_PAGES, t=PACK)
-        spread_src = vs_src[:].rearrange("m u (o t) -> m u o t", o=1).to_broadcast([P, POOL_PAGES, NQ, PACK])
-        nc.scalar.activation(dealt[:, :SCALAR_PAGES], spread_src[:, :SCALAR_PAGES], ACT.Copy)
-        nc.vector.tensor_copy(dealt[:, SCALAR_PAGES:], spread_src[:, SCALAR_PAGES:])
-
-        pos_row = [sb.tile([P, PAGE], F32, name=f"pos_row{h}", align_bytes=64) for h in range(PAGES)]
+        pos_rows = sb.tile([P, N], F32, align_bytes=64, tag="pos_rows")
+        pos_row = [pos_rows[:, h * PAGE : (h + 1) * PAGE] for h in range(PAGES)]
         pos_col = [sb.tile([P, PACK], F32, name=f"pos_col{h}", align_bytes=64) for h in range(PAGES)]
         hid = late.tile([P, N], F32, align_bytes=64, offset=0)
         edge = sb.tile([P, 1], F32, align_bytes=64, tag="edge_then_sizes")
         ks = sb.tile([P, N], U8, align_bytes=64)
         for h in range(PAGES):
-            nc.scalar.activation(pos_row[h][:], pos_pool[:].indirect(listed(h * PAGE, PAGE)), ACT.Copy)
+            nc.scalar.activation(pos_row[h], pos_pool[:].indirect(listed(h * PAGE, PAGE)), ACT.Copy)
         nc.vector.tensor_copy(ks[:], ks_pool[:].indirect(offs_t[:]))
+        nc.vector.tensor_copy(
+            vs_pool[:].rearrange("m (u q t) -> m u q t", u=POOL_PAGES, t=PACK),
+            vs_src[:].rearrange("m u (o t) -> m u o t", o=1).to_broadcast([P, POOL_PAGES, NQ, PACK]),
+        )
 
         spread = []
         for h in range(PAGES):
@@ -123,10 +125,6 @@ def tile_attend_pkv8q_soft_draft_gate_kernel(
             nc.scalar.activation(
                 sizes[:, h * PAGE : (h + 1) * PAGE], vs_pool[:].indirect(listed(h * PAGE, PAGE)), ACT.Copy
             )
-        gate_t = sb.tile([P, DV], F32)
-        gate = sb.tile([P, DV], F32)
-        nc.scalar.activation(gate_t[:], og_t[:], ACT.Tanh, scale=0.5)
-        nc.scalar.activation(gate[:], gate_t[:], ACT.Copy, scale=0.5, bias=0.5)
 
         raw = []
         for h in range(PAGES):
@@ -154,7 +152,7 @@ def tile_attend_pkv8q_soft_draft_gate_kernel(
                 ALU.min,
                 ALU.subtract,
             )
-        neg_m = sb.tile([P, 1], F32)
+        neg_m = sb.tile([P, 1], F32, tag="neg_m_then_gate")
         nc.vector.tensor_reduce(neg_m[:], neg_s[:], mybir.AxisListType.X, ALU.min)
 
         p = [sb.tile([P, 2, P], F32, name=f"p{j}", align_bytes=64) for j in range(2 * PAGES)]
@@ -171,6 +169,11 @@ def tile_attend_pkv8q_soft_draft_gate_kernel(
                 bias=neg_m[:, 0:1],
                 accum_out=sums[:, j : j + 1],
             )
+
+        gate_t = sb.tile([P, DV], F32, tag="neg_m_then_gate")
+        gate = sb.tile([P, DV], F32)
+        nc.scalar.activation(gate_t[:], og_t[:], ACT.Tanh, scale=0.5)
+        nc.scalar.activation(gate[:], gate_t[:], ACT.Copy, scale=0.5, bias=0.5)
 
         vw = late.tile([P, PAGES * DV], U32, align_bytes=64, offset=4 * PAGE)
         vsc = late.tile([P, PAGES * DV], U8, align_bytes=64, offset=4 * PAGE + 4 * PAGES * DV)

@@ -41,10 +41,9 @@ def tile_attend_pkv8q_soft_draft_gate_kernel(
         kw_pool = sb.tile([P, T], I32, align_bytes=64)
         vsc_pool = sb.tile([P, POOL_PAGES * DV], U8, align_bytes=64, tag="wt1")
         ks_pool = sb.tile([P, T], U8, align_bytes=64)
-        vw_pool = sb.tile([P, POOL_PAGES * DV], I32, align_bytes=64)
+        vw_pool = sb.tile([P, POOL_PAGES * DV], I32, align_bytes=64, tag="vs_col")
         pos_pool = sb.tile([P, T], F32, align_bytes=64)
         vs_pool = sb.tile([P, T], F32, align_bytes=64)
-        vs_src = sb.tile([P, POOL_PAGES, PACK], F32, align_bytes=64)
         qw = sb.tile([P, NQ], I32, align_bytes=64)
         qs = sb.tile([P, NQ], U8, align_bytes=64)
         qpos_t = sb.tile([P, 1], F32, align_bytes=64)
@@ -59,11 +58,12 @@ def tile_attend_pkv8q_soft_draft_gate_kernel(
         nc.gpsimd.memset(qs[:].bitcast(I32), 0)
         nc.vector.memset(ks_pool[:].bitcast(I32), 0)
         nc.vector.memset(pos_pool[0:ROW, :], 0.0)
+        nc.vector.memset(vs_pool[0:ROW, :], 0.0)
         nc.vector.memset(vsc_pool[:].bitcast(I32), 0)
 
         nc.sync.dma_start(offs_t[:], offs)
         nc.sync.dma_start(pos_pool[ROW:P, :], pos[0:1, :])
-        nc.scalar.dma_start(vs_src[:], vs[0:1, :].rearrange("o (u m t) -> (o m) u t", u=POOL_PAGES, t=PACK))
+        nc.scalar.dma_start(vs_pool[ROW:P, :], vs[0:1, :])
         for r in range(4):
             nc.sync.dma_start(ks_pool[r:P:32, :].bitcast(I32), k_scales[0, r:16:4, :].bitcast(I32))
         nc.sync.dma_start(kw_pool[:], k_words[0].rearrange("p n t -> p (n t)").bitcast(I32))
@@ -92,17 +92,12 @@ def tile_attend_pkv8q_soft_draft_gate_kernel(
 
         pos_rows = sb.tile([P, N], F32, align_bytes=64, tag="pos_rows")
         pos_row = [pos_rows[:, h * PAGE : (h + 1) * PAGE] for h in range(PAGES)]
-        pos_col = [sb.tile([P, PACK], F32, name=f"pos_col{h}", align_bytes=64) for h in range(PAGES)]
+        pos_col = [sb.tile([P, PACK], F32, name=f"pos_col{h}", align_bytes=64, tag=f"pos_col{h}") for h in range(PAGES)]
         hid = late.tile([P, N], F32, align_bytes=64, offset=0)
-        edge = sb.tile([P, 1], F32, align_bytes=64, tag="edge_then_sizes")
         ks = sb.tile([P, N], U8, align_bytes=64)
         for h in range(PAGES):
             nc.scalar.activation(pos_row[h], pos_pool[:].indirect(listed(h * PAGE, PAGE)), ACT.Copy)
         nc.vector.tensor_copy(ks[:], ks_pool[:].indirect(offs_t[:]))
-        nc.vector.tensor_copy(
-            vs_pool[:].rearrange("m (u q t) -> m u q t", u=POOL_PAGES, t=PACK),
-            vs_src[:].rearrange("m u (o t) -> m u o t", o=1).to_broadcast([P, POOL_PAGES, NQ, PACK]),
-        )
 
         spread = []
         for h in range(PAGES):
@@ -115,22 +110,22 @@ def tile_attend_pkv8q_soft_draft_gate_kernel(
                 nc.tensor.transpose(
                     spread[h][:, c * P : (c + 1) * P], pos_col[h][:, c : c + 1].to_broadcast([P, P]), ident[:]
                 )
+        vs_row = [sb.tile([P, PAGE], F32, name="vs_row0", align_bytes=64, tag="pos_rows")]
+        nc.scalar.activation(vs_row[0][:], vs_pool[:].indirect(listed(0, PAGE)), ACT.Copy)
+        edge = sb.tile([P, 1], F32, align_bytes=64, tag="pos_col1")
         nc.scalar.activation(edge[:], qpos_t[:], ACT.Copy, scale=-STEEP)
         for h in range(PAGES):
             nc.scalar.activation(
                 hid[:, h * PAGE : (h + 1) * PAGE], spread[h][:], ACT.Relu, scale=STEEP, bias=edge[:, 0:1]
             )
-        sizes = sb.tile([P, N], F32, align_bytes=64, tag="edge_then_sizes")
-        for h in range(PAGES):
-            nc.scalar.activation(
-                sizes[:, h * PAGE : (h + 1) * PAGE], vs_pool[:].indirect(listed(h * PAGE, PAGE)), ACT.Copy
-            )
+        vs_row.append(sb.tile([P, PAGE], F32, name="vs_row1", align_bytes=64, tag="pos_col1"))
+        nc.scalar.activation(vs_row[1][:], vs_pool[:].indirect(listed(PAGE, PAGE)), ACT.Copy)
 
         raw = []
         for h in range(PAGES):
             kw = sb.tile([P, PAGE], U32, name=f"kw{h}", align_bytes=64)
             nc.vector.tensor_copy(kw[:], kw_pool[:].bitcast(U32).indirect(listed(h * PAGE, PAGE)))
-            bank = ps.tile([P, PAGE], F32, name=f"raw{h}", tag=f"raw{h}")
+            bank = ps.tile([P, PAGE], F32, name=f"raw{h}", tag=f"turn{PAGES - 1 - h}")
             nc.tensor.matmul_mx(
                 out=bank[:],
                 lhsT=qw[:].bitcast(FP8X4),
@@ -180,18 +175,25 @@ def tile_attend_pkv8q_soft_draft_gate_kernel(
         nc.vector.tensor_copy(vw[:], vw_pool[:].bitcast(U32).indirect(voffs_t[:]))
         nc.vector.tensor_copy(vsc[:], vsc_pool[:].indirect(voffs_t[:]))
 
+        vs_col = sb.tile([P, PAGES, PACK], F32, align_bytes=64, tag="vs_col")
+        for h in range(PAGES):
+            turned = ps.tile([P, PACK, P], F32, name=f"vs_turned{h}", tag=f"turn{PAGES - 1 - h}")
+            for t in range(PACK):
+                nc.tensor.transpose(turned[:, t, :], vs_row[h][:, t:PAGE:PACK], ident[:])
+            nc.vector.tensor_copy(vs_col[:, h, :], turned[:, :, ROW])
+
         acc = ps.tile([P, DV], F32, tag="acc")
         wt = [sb.tile([P, NQ, PACK], BF16, name=f"wt{h}", align_bytes=64, tag=f"wt{h}") for h in range(PAGES)]
         codes = [sb.tile([P, NQ], U32, name=f"codes{h}", align_bytes=64) for h in range(PAGES)]
         scales = [sb.tile([P, NQ], U8, name=f"scales{h}", align_bytes=64) for h in range(PAGES)]
         for h in range(PAGES):
-            turned = ps.tile([P, PACK, NQ], F32, name=f"p_turned{h}", tag=f"turn{h}")
+            turned = ps.tile([P, PACK, NQ], F32, name=f"p_turned{h}", tag=f"weights{h}")
             for t in range(PACK):
                 nc.tensor.transpose(turned[:, t, :], p[2 * h + t // 2][:, t % 2, :], ident[:])
             nc.vector.tensor_tensor(
                 wt[h][:],
                 turned[:].rearrange("m t q -> m q t"),
-                sizes[:, h * PAGE : (h + 1) * PAGE].rearrange("m (q t) -> m q t", t=PACK),
+                vs_col[:, h : h + 1, :].to_broadcast([P, NQ, PACK]),
                 ALU.mult,
             )
         for h in range(PAGES):

@@ -20,6 +20,7 @@ POOL_PAGES = T // PAGE
 PACK = 4
 LIST = 16
 ROW = P - 1
+ODD = POOL_PAGES * DV // PACK - 1
 STEEP = 2.0**96
 HIDDEN = 2.0**72
 
@@ -34,6 +35,7 @@ def tile_attend_pkv8q_soft_draft_gate_kernel(
     with ExitStack() as ctx:
         sb = ctx.enter_context(tc.tile_pool(name="sb", bufs=1))
         late = ctx.enter_context(tc.tile_pool(name="late", bufs=1))
+        early = ctx.enter_context(tc.tile_pool(name="early", bufs=1))
         ps = ctx.enter_context(tc.psum_pool(name="ps", bufs=1))
 
         offs_t = sb.tile([P, N // LIST], U16)
@@ -43,7 +45,6 @@ def tile_attend_pkv8q_soft_draft_gate_kernel(
         ks_pool = sb.tile([P, T], U8, align_bytes=64)
         vw_pool = sb.tile([P, POOL_PAGES * DV], I32, align_bytes=64, tag="vs_col")
         pos_pool = sb.tile([P, T], F32, align_bytes=64)
-        vs_pool = sb.tile([P, T], F32, align_bytes=64)
         qw = sb.tile([P, NQ], I32, align_bytes=64)
         qs = sb.tile([P, NQ], U8, align_bytes=64)
         qpos_t = sb.tile([P, 1], F32, align_bytes=64)
@@ -51,23 +52,26 @@ def tile_attend_pkv8q_soft_draft_gate_kernel(
         ident = sb.tile([P, P], F32, align_bytes=64)
 
         ramp = sb.tile([P, P], F32, align_bytes=64)
-        dist = sb.tile([P, P], F32, align_bytes=64, tag="pos_rows")
+        dist = early.tile([P, P], F32, align_bytes=64, offset=4 * (T - P // 2))
         nc.gpsimd.iota(ramp[:], [[1, P]], base=0, channel_multiplier=-1, allow_small_or_imprecise_dtypes=True)
         nc.scalar.activation(dist[:], ramp[:], ACT.Abs)
         nc.scalar.activation(ident[:], dist[:], ACT.Relu, scale=-1.0, bias=1.0)
-        nc.gpsimd.memset(qs[:].bitcast(I32), 0)
+        vs_pool = early.tile([P, T], F32, align_bytes=64, offset=0)
+        vsc_words = vsc_pool[:].bitcast(I32)
         nc.vector.memset(ks_pool[:].bitcast(I32), 0)
+        nc.vector.memset(qs[:].bitcast(I32), 0)
+        nc.vector.memset(vsc_words[:, :ODD], 0)
+        nc.vector.memset(vsc_words[:, ODD:], 0)
         nc.vector.memset(pos_pool[0:ROW, :], 0.0)
-        nc.vector.memset(vs_pool[0:ROW, :], 0.0)
-        nc.vector.memset(vsc_pool[:].bitcast(I32), 0)
+        nc.gpsimd.memset(vs_pool[0:ROW, :], 0.0)
 
         nc.sync.dma_start(offs_t[:], offs)
         nc.sync.dma_start(pos_pool[ROW:P, :], pos[0:1, :])
-        nc.scalar.dma_start(vs_pool[ROW:P, :], vs[0:1, :])
+        nc.sync.dma_start(qpos_t[:], qpos[0])
         for r in range(4):
             nc.sync.dma_start(ks_pool[r:P:32, :].bitcast(I32), k_scales[0, r:16:4, :].bitcast(I32))
         nc.sync.dma_start(kw_pool[:], k_words[0].rearrange("p n t -> p (n t)").bitcast(I32))
-        nc.sync.dma_start(qpos_t[:], qpos[0])
+        nc.sync.dma_start(vs_pool[ROW:P, :], vs[0:1, :])
         nc.sync.dma_start(qw[:], q_words[0, 0].rearrange("p n t -> p (n t)").bitcast(I32))
         for quad in range(4):
             nc.sync.dma_start(
@@ -90,13 +94,15 @@ def tile_attend_pkv8q_soft_draft_gate_kernel(
         def listed(first, count):
             return offs_t[:, first // LIST : (first + count) // LIST]
 
-        pos_rows = sb.tile([P, N], F32, align_bytes=64, tag="pos_rows")
-        pos_row = [pos_rows[:, h * PAGE : (h + 1) * PAGE] for h in range(PAGES)]
+        pos_row = [
+            early.tile([P, PAGE], F32, name=f"pos_row{h}", align_bytes=64, offset=4 * (T + h * PAGE))
+            for h in range(PAGES)
+        ]
         pos_col = [sb.tile([P, PACK], F32, name=f"pos_col{h}", align_bytes=64, tag=f"pos_col{h}") for h in range(PAGES)]
         hid = late.tile([P, N], F32, align_bytes=64, offset=0)
         ks = sb.tile([P, N], U8, align_bytes=64)
-        for h in range(PAGES):
-            nc.scalar.activation(pos_row[h], pos_pool[:].indirect(listed(h * PAGE, PAGE)), ACT.Copy)
+        nc.scalar.activation(pos_row[0][:], pos_pool[:].indirect(listed(0, PAGE)), ACT.Copy)
+        nc.vector.tensor_copy(pos_row[1][:], pos_pool[:].indirect(listed(PAGE, PAGE)))
         nc.vector.tensor_copy(ks[:], ks_pool[:].indirect(offs_t[:]))
 
         spread = []
@@ -110,16 +116,16 @@ def tile_attend_pkv8q_soft_draft_gate_kernel(
                 nc.tensor.transpose(
                     spread[h][:, c * P : (c + 1) * P], pos_col[h][:, c : c + 1].to_broadcast([P, P]), ident[:]
                 )
-        vs_row = [sb.tile([P, PAGE], F32, name="vs_row0", align_bytes=64, tag="pos_rows")]
-        nc.scalar.activation(vs_row[0][:], vs_pool[:].indirect(listed(0, PAGE)), ACT.Copy)
-        edge = sb.tile([P, 1], F32, align_bytes=64, tag="pos_col1")
+        edge = sb.tile([P, 1], F32, align_bytes=64, tag="vs_rows")
         nc.scalar.activation(edge[:], qpos_t[:], ACT.Copy, scale=-STEEP)
         for h in range(PAGES):
             nc.scalar.activation(
                 hid[:, h * PAGE : (h + 1) * PAGE], spread[h][:], ACT.Relu, scale=STEEP, bias=edge[:, 0:1]
             )
-        vs_row.append(sb.tile([P, PAGE], F32, name="vs_row1", align_bytes=64, tag="pos_col1"))
-        nc.scalar.activation(vs_row[1][:], vs_pool[:].indirect(listed(PAGE, PAGE)), ACT.Copy)
+        vs_rows = sb.tile([P, N], F32, align_bytes=64, tag="vs_rows")
+        vs_row = [vs_rows[:, h * PAGE : (h + 1) * PAGE] for h in range(PAGES)]
+        for h in range(PAGES):
+            nc.scalar.activation(vs_row[h], vs_pool[:].indirect(listed(h * PAGE, PAGE)), ACT.Copy)
 
         raw = []
         for h in range(PAGES):

@@ -20,7 +20,7 @@ POOL_PAGES = T // PAGE
 PACK = 4
 LIST = 16
 ROW = P - 1
-ODD = POOL_PAGES * DV // PACK - 1
+ODD = 193
 STEEP = 2.0**96
 HIDDEN = 2.0**72
 
@@ -34,7 +34,6 @@ def tile_attend_pkv8q_soft_draft_gate_kernel(
     nc = tc.nc
     with ExitStack() as ctx:
         sb = ctx.enter_context(tc.tile_pool(name="sb", bufs=1))
-        late = ctx.enter_context(tc.tile_pool(name="late", bufs=1))
         early = ctx.enter_context(tc.tile_pool(name="early", bufs=1))
         ps = ctx.enter_context(tc.psum_pool(name="ps", bufs=1))
 
@@ -52,7 +51,7 @@ def tile_attend_pkv8q_soft_draft_gate_kernel(
         ident = sb.tile([P, P], F32, align_bytes=64)
 
         ramp = sb.tile([P, P], F32, align_bytes=64)
-        dist = early.tile([P, P], F32, align_bytes=64, offset=4 * (T - P // 2))
+        dist = early.tile([P, P], F32, align_bytes=64, offset=4 * (T + PAGE - P // 2))
         nc.gpsimd.iota(ramp[:], [[1, P]], base=0, channel_multiplier=-1, allow_small_or_imprecise_dtypes=True)
         nc.scalar.activation(dist[:], ramp[:], ACT.Abs)
         nc.scalar.activation(ident[:], dist[:], ACT.Relu, scale=-1.0, bias=1.0)
@@ -61,17 +60,17 @@ def tile_attend_pkv8q_soft_draft_gate_kernel(
         nc.vector.memset(ks_pool[:].bitcast(I32), 0)
         nc.vector.memset(qs[:].bitcast(I32), 0)
         nc.vector.memset(vsc_words[:, :ODD], 0)
-        nc.vector.memset(vsc_words[:, ODD:], 0)
         nc.vector.memset(pos_pool[0:ROW, :], 0.0)
-        nc.gpsimd.memset(vs_pool[0:ROW, :], 0.0)
+        nc.vector.memset(vsc_words[:, ODD:], 0)
+        nc.vector.memset(vs_pool[0:ROW, :], 0.0)
 
         nc.sync.dma_start(offs_t[:], offs)
         nc.sync.dma_start(pos_pool[ROW:P, :], pos[0:1, :])
+        nc.sync.dma_start(vs_pool[ROW:P, :], vs[0:1, :])
         nc.sync.dma_start(qpos_t[:], qpos[0])
         for r in range(4):
             nc.sync.dma_start(ks_pool[r:P:32, :].bitcast(I32), k_scales[0, r:16:4, :].bitcast(I32))
         nc.sync.dma_start(kw_pool[:], k_words[0].rearrange("p n t -> p (n t)").bitcast(I32))
-        nc.sync.dma_start(vs_pool[ROW:P, :], vs[0:1, :])
         nc.sync.dma_start(qw[:], q_words[0, 0].rearrange("p n t -> p (n t)").bitcast(I32))
         for quad in range(4):
             nc.sync.dma_start(
@@ -99,10 +98,9 @@ def tile_attend_pkv8q_soft_draft_gate_kernel(
             for h in range(PAGES)
         ]
         pos_col = [sb.tile([P, PACK], F32, name=f"pos_col{h}", align_bytes=64, tag=f"pos_col{h}") for h in range(PAGES)]
-        hid = late.tile([P, N], F32, align_bytes=64, offset=0)
         ks = sb.tile([P, N], U8, align_bytes=64)
-        nc.scalar.activation(pos_row[0][:], pos_pool[:].indirect(listed(0, PAGE)), ACT.Copy)
-        nc.vector.tensor_copy(pos_row[1][:], pos_pool[:].indirect(listed(PAGE, PAGE)))
+        for h in range(PAGES):
+            nc.scalar.activation(pos_row[h][:], pos_pool[:].indirect(listed(h * PAGE, PAGE)), ACT.Copy)
         nc.vector.tensor_copy(ks[:], ks_pool[:].indirect(offs_t[:]))
 
         spread = []
@@ -116,22 +114,30 @@ def tile_attend_pkv8q_soft_draft_gate_kernel(
                 nc.tensor.transpose(
                     spread[h][:, c * P : (c + 1) * P], pos_col[h][:, c : c + 1].to_broadcast([P, P]), ident[:]
                 )
-        edge = sb.tile([P, 1], F32, align_bytes=64, tag="vs_rows")
+        vs_row = [sb.tile([P, PAGE], F32, name=f"vs_row{h}", align_bytes=64) for h in range(PAGES)]
+        for h in range(PAGES):
+            nc.scalar.activation(vs_row[h][:], vs_pool[:].indirect(listed(h * PAGE, PAGE)), ACT.Copy)
+        vs_turned = []
+
+        def turn_vs(h, bank):
+            vs_turned.append(ps.tile([P, PACK, P], F32, name=f"vs_turned{h}", tag=bank))
+            for t in range(PACK):
+                nc.tensor.transpose(vs_turned[h][:, t, :], vs_row[h][:, t:PAGE:PACK], ident[:])
+
+        turn_vs(0, "turn0")
+        hid = early.tile([P, N], F32, align_bytes=64, offset=0)
+        edge = early.tile([P, 1], F32, align_bytes=64, offset=4 * N)
         nc.scalar.activation(edge[:], qpos_t[:], ACT.Copy, scale=-STEEP)
         for h in range(PAGES):
             nc.scalar.activation(
                 hid[:, h * PAGE : (h + 1) * PAGE], spread[h][:], ACT.Relu, scale=STEEP, bias=edge[:, 0:1]
             )
-        vs_rows = sb.tile([P, N], F32, align_bytes=64, tag="vs_rows")
-        vs_row = [vs_rows[:, h * PAGE : (h + 1) * PAGE] for h in range(PAGES)]
-        for h in range(PAGES):
-            nc.scalar.activation(vs_row[h], vs_pool[:].indirect(listed(h * PAGE, PAGE)), ACT.Copy)
 
         raw = []
         for h in range(PAGES):
             kw = sb.tile([P, PAGE], U32, name=f"kw{h}", align_bytes=64)
             nc.vector.tensor_copy(kw[:], kw_pool[:].bitcast(U32).indirect(listed(h * PAGE, PAGE)))
-            bank = ps.tile([P, PAGE], F32, name=f"raw{h}", tag=f"turn{PAGES - 1 - h}")
+            bank = ps.tile([P, PAGE], F32, name=f"raw{h}", tag=f"raw{h}")
             nc.tensor.matmul_mx(
                 out=bank[:],
                 lhsT=qw[:].bitcast(FP8X4),
@@ -153,6 +159,7 @@ def tile_attend_pkv8q_soft_draft_gate_kernel(
                 ALU.min,
                 ALU.subtract,
             )
+        turn_vs(1, "raw0")
         neg_m = sb.tile([P, 1], F32, tag="neg_m_then_gate")
         nc.vector.tensor_reduce(neg_m[:], neg_s[:], mybir.AxisListType.X, ALU.min)
 
@@ -176,24 +183,21 @@ def tile_attend_pkv8q_soft_draft_gate_kernel(
         nc.scalar.activation(gate_t[:], og_t[:], ACT.Tanh, scale=0.5)
         nc.scalar.activation(gate[:], gate_t[:], ACT.Copy, scale=0.5, bias=0.5)
 
-        vw = late.tile([P, PAGES * DV], U32, align_bytes=64, offset=4 * PAGE)
-        vsc = late.tile([P, PAGES * DV], U8, align_bytes=64, offset=4 * PAGE + 4 * PAGES * DV)
+        vw = early.tile([P, PAGES * DV], U32, align_bytes=64, offset=4 * PAGE)
+        vsc = early.tile([P, PAGES * DV], U8, align_bytes=64, offset=4 * PAGE + 4 * PAGES * DV)
         nc.vector.tensor_copy(vw[:], vw_pool[:].bitcast(U32).indirect(voffs_t[:]))
         nc.vector.tensor_copy(vsc[:], vsc_pool[:].indirect(voffs_t[:]))
 
         vs_col = sb.tile([P, PAGES, PACK], F32, align_bytes=64, tag="vs_col")
         for h in range(PAGES):
-            turned = ps.tile([P, PACK, P], F32, name=f"vs_turned{h}", tag=f"turn{PAGES - 1 - h}")
-            for t in range(PACK):
-                nc.tensor.transpose(turned[:, t, :], vs_row[h][:, t:PAGE:PACK], ident[:])
-            nc.vector.tensor_copy(vs_col[:, h, :], turned[:, :, ROW])
+            nc.vector.tensor_copy(vs_col[:, h, :], vs_turned[h][:, :, ROW])
 
         acc = ps.tile([P, DV], F32, tag="acc")
         wt = [sb.tile([P, NQ, PACK], BF16, name=f"wt{h}", align_bytes=64, tag=f"wt{h}") for h in range(PAGES)]
         codes = [sb.tile([P, NQ], U32, name=f"codes{h}", align_bytes=64) for h in range(PAGES)]
         scales = [sb.tile([P, NQ], U8, name=f"scales{h}", align_bytes=64) for h in range(PAGES)]
         for h in range(PAGES):
-            turned = ps.tile([P, PACK, NQ], F32, name=f"p_turned{h}", tag=f"weights{h}")
+            turned = ps.tile([P, PACK, NQ], F32, name=f"p_turned{h}", tag=f"wide{h}")
             for t in range(PACK):
                 nc.tensor.transpose(turned[:, t, :], p[2 * h + t // 2][:, t % 2, :], ident[:])
             nc.vector.tensor_tensor(

@@ -34,6 +34,7 @@ def tile_attend_pkv8q_soft_draft_gate_kernel(
     nc = tc.nc
     with ExitStack() as ctx:
         sb = ctx.enter_context(tc.tile_pool(name="sb", bufs=1))
+        late = ctx.enter_context(tc.tile_pool(name="late", bufs=1))
         early = ctx.enter_context(tc.tile_pool(name="early", bufs=1))
         ps = ctx.enter_context(tc.psum_pool(name="ps", bufs=1))
 
@@ -66,17 +67,21 @@ def tile_attend_pkv8q_soft_draft_gate_kernel(
 
         nc.sync.dma_start(offs_t[:], offs)
         nc.sync.dma_start(pos_pool[ROW:P, :], pos[0:1, :])
-        nc.sync.dma_start(vs_pool[ROW:P, :], vs[0:1, :])
         nc.sync.dma_start(qpos_t[:], qpos[0])
-        for r in range(4):
-            nc.sync.dma_start(ks_pool[r:P:32, :].bitcast(I32), k_scales[0, r:16:4, :].bitcast(I32))
         nc.sync.dma_start(kw_pool[:], k_words[0].rearrange("p n t -> p (n t)").bitcast(I32))
+        nc.sync.dma_start(vs_pool[ROW:P, :], vs[0:1, :])
         nc.sync.dma_start(qw[:], q_words[0, 0].rearrange("p n t -> p (n t)").bitcast(I32))
-        for quad in range(4):
+
+        def load_query_scales(quad):
             nc.sync.dma_start(
                 qs[32 * quad : 32 * quad + 4, :].bitcast(I32),
                 q_scales[0, 0, 4 * quad : 4 * quad + 4, :].bitcast(I32),
             )
+
+        for quad in range(4):
+            load_query_scales(quad)
+        for r in range(4):
+            nc.scalar.dma_start(ks_pool[r:P:32, :].bitcast(I32), k_scales[0, r:16:4, :].bitcast(I32))
         nc.sync.dma_start(
             vw_pool[:].rearrange("p (u e) -> p u e", u=POOL_PAGES),
             v_words.rearrange("u p e t -> p u (e t)").bitcast(I32),
@@ -114,9 +119,6 @@ def tile_attend_pkv8q_soft_draft_gate_kernel(
                 nc.tensor.transpose(
                     spread[h][:, c * P : (c + 1) * P], pos_col[h][:, c : c + 1].to_broadcast([P, P]), ident[:]
                 )
-        vs_row = [sb.tile([P, PAGE], F32, name=f"vs_row{h}", align_bytes=64) for h in range(PAGES)]
-        for h in range(PAGES):
-            nc.scalar.activation(vs_row[h][:], vs_pool[:].indirect(listed(h * PAGE, PAGE)), ACT.Copy)
         vs_turned = []
 
         def turn_vs(h, bank):
@@ -124,14 +126,17 @@ def tile_attend_pkv8q_soft_draft_gate_kernel(
             for t in range(PACK):
                 nc.tensor.transpose(vs_turned[h][:, t, :], vs_row[h][:, t:PAGE:PACK], ident[:])
 
-        turn_vs(0, "turn0")
-        hid = early.tile([P, N], F32, align_bytes=64, offset=0)
-        edge = early.tile([P, 1], F32, align_bytes=64, offset=4 * N)
+        hid = late.tile([P, N], F32, align_bytes=64, offset=0)
+        edge = sb.tile([P, 1], F32, align_bytes=64, tag="edge_then_vs0")
         nc.scalar.activation(edge[:], qpos_t[:], ACT.Copy, scale=-STEEP)
         for h in range(PAGES):
             nc.scalar.activation(
                 hid[:, h * PAGE : (h + 1) * PAGE], spread[h][:], ACT.Relu, scale=STEEP, bias=edge[:, 0:1]
             )
+        vs_rows = sb.tile([P, N], F32, align_bytes=64, tag="edge_then_vs0")
+        vs_row = [vs_rows[:, h * PAGE : (h + 1) * PAGE] for h in range(PAGES)]
+        for h in range(PAGES):
+            nc.scalar.activation(vs_row[h], vs_pool[:].indirect(listed(h * PAGE, PAGE)), ACT.Copy)
 
         raw = []
         for h in range(PAGES):
@@ -159,7 +164,8 @@ def tile_attend_pkv8q_soft_draft_gate_kernel(
                 ALU.min,
                 ALU.subtract,
             )
-        turn_vs(1, "raw0")
+        for h in range(PAGES):
+            turn_vs(h, f"raw{h}")
         neg_m = sb.tile([P, 1], F32, tag="neg_m_then_gate")
         nc.vector.tensor_reduce(neg_m[:], neg_s[:], mybir.AxisListType.X, ALU.min)
 
@@ -183,8 +189,8 @@ def tile_attend_pkv8q_soft_draft_gate_kernel(
         nc.scalar.activation(gate_t[:], og_t[:], ACT.Tanh, scale=0.5)
         nc.scalar.activation(gate[:], gate_t[:], ACT.Copy, scale=0.5, bias=0.5)
 
-        vw = early.tile([P, PAGES * DV], U32, align_bytes=64, offset=4 * PAGE)
-        vsc = early.tile([P, PAGES * DV], U8, align_bytes=64, offset=4 * PAGE + 4 * PAGES * DV)
+        vw = late.tile([P, PAGES * DV], U32, align_bytes=64, offset=4 * PAGE)
+        vsc = late.tile([P, PAGES * DV], U8, align_bytes=64, offset=4 * PAGE + 4 * PAGES * DV)
         nc.vector.tensor_copy(vw[:], vw_pool[:].bitcast(U32).indirect(voffs_t[:]))
         nc.vector.tensor_copy(vsc[:], vsc_pool[:].indirect(voffs_t[:]))
 

@@ -20,6 +20,7 @@ POOL_PAGES = T // PAGE
 PACK = 4
 LIST = 16
 ROW = P - 1
+SCALES_AT = P - 16
 ODD = 193
 STEEP = 2.0**96
 HIDDEN = 2.0**72
@@ -42,8 +43,8 @@ def tile_attend_pkv8q_soft_draft_gate_kernel(
         voffs_t = sb.tile([P, PAGES * DV // LIST], U16)
         kw_pool = sb.tile([P, T], I32, align_bytes=64)
         vsc_pool = sb.tile([P, POOL_PAGES * DV], U8, align_bytes=64, tag="wt1")
-        ks_pool = sb.tile([P, T], U8, align_bytes=64)
-        vw_pool = sb.tile([P, POOL_PAGES * DV], I32, align_bytes=64, tag="vs_col")
+        ks_pool = sb.tile([P, T], U8, align_bytes=64, tag="ks_then_vw")
+        ks = sb.tile([P, N], U8, align_bytes=64)
         pos_pool = sb.tile([P, T], F32, align_bytes=64)
         qw = sb.tile([P, NQ], I32, align_bytes=64)
         qs = sb.tile([P, NQ], U8, align_bytes=64)
@@ -58,19 +59,12 @@ def tile_attend_pkv8q_soft_draft_gate_kernel(
         nc.scalar.activation(ident[:], dist[:], ACT.Relu, scale=-1.0, bias=1.0)
         vs_pool = early.tile([P, T], F32, align_bytes=64, offset=0)
         vsc_words = vsc_pool[:].bitcast(I32)
-        nc.vector.memset(ks_pool[:].bitcast(I32), 0)
         nc.vector.memset(qs[:].bitcast(I32), 0)
+        nc.vector.memset(ks_pool[0:SCALES_AT, :].bitcast(I32), 0)
         nc.vector.memset(vsc_words[:, :ODD], 0)
+        nc.vector.memset(ks[:].bitcast(I32), 0)
         nc.vector.memset(pos_pool[0:ROW, :], 0.0)
         nc.vector.memset(vsc_words[:, ODD:], 0)
-        nc.vector.memset(vs_pool[0:ROW, :], 0.0)
-
-        nc.sync.dma_start(offs_t[:], offs)
-        nc.sync.dma_start(pos_pool[ROW:P, :], pos[0:1, :])
-        nc.sync.dma_start(qpos_t[:], qpos[0])
-        nc.sync.dma_start(kw_pool[:], k_words[0].rearrange("p n t -> p (n t)").bitcast(I32))
-        nc.sync.dma_start(vs_pool[ROW:P, :], vs[0:1, :])
-        nc.sync.dma_start(qw[:], q_words[0, 0].rearrange("p n t -> p (n t)").bitcast(I32))
 
         def load_query_scales(quad):
             nc.sync.dma_start(
@@ -78,10 +72,23 @@ def tile_attend_pkv8q_soft_draft_gate_kernel(
                 q_scales[0, 0, 4 * quad : 4 * quad + 4, :].bitcast(I32),
             )
 
-        for quad in range(4):
+        nc.sync.dma_start(offs_t[:], offs)
+        nc.sync.dma_start(ks_pool[SCALES_AT:P, :].bitcast(I32), k_scales[0].bitcast(I32))
+        nc.sync.dma_start(pos_pool[ROW:P, :], pos[0:1, :])
+        nc.sync.dma_start(qpos_t[:], qpos[0])
+        for quad in range(3):
             load_query_scales(quad)
+        nc.sync.dma_start(kw_pool[:], k_words[0].rearrange("p n t -> p (n t)").bitcast(I32))
+        load_query_scales(3)
+        nc.sync.dma_start(qw[:], q_words[0, 0].rearrange("p n t -> p (n t)").bitcast(I32))
+        nc.sync.dma_start(vs_pool[ROW:P, :], vs[0:1, :])
+
+        ks_rows = sb.tile([P, N], U8, align_bytes=64)
+        nc.vector.tensor_copy(ks_rows[:], ks_pool[:].indirect(offs_t[:]))
+        nc.vector.memset(vs_pool[0:ROW, :], 0.0)
         for r in range(4):
-            nc.scalar.dma_start(ks_pool[r:P:32, :].bitcast(I32), k_scales[0, r:16:4, :].bitcast(I32))
+            nc.sync.dma_start(ks[r:P:32, :].bitcast(I32), ks_rows[SCALES_AT + r : P : 4, :].bitcast(I32))
+        vw_pool = sb.tile([P, POOL_PAGES * DV], I32, align_bytes=64, tag="ks_then_vw")
         nc.sync.dma_start(
             vw_pool[:].rearrange("p (u e) -> p u e", u=POOL_PAGES),
             v_words.rearrange("u p e t -> p u (e t)").bitcast(I32),
@@ -92,7 +99,6 @@ def tile_attend_pkv8q_soft_draft_gate_kernel(
                 vsc_pool[r:P:32, :].bitcast(I32).rearrange("p (u e) -> p u e", u=POOL_PAGES),
                 v_scales[:, r:16:4, :].rearrange("u f e -> f u e").bitcast(I32),
             )
-
         nc.sync.dma_start(og_t[:], og[0])
 
         def listed(first, count):
@@ -103,10 +109,8 @@ def tile_attend_pkv8q_soft_draft_gate_kernel(
             for h in range(PAGES)
         ]
         pos_col = [sb.tile([P, PACK], F32, name=f"pos_col{h}", align_bytes=64, tag=f"pos_col{h}") for h in range(PAGES)]
-        ks = sb.tile([P, N], U8, align_bytes=64)
         for h in range(PAGES):
             nc.scalar.activation(pos_row[h][:], pos_pool[:].indirect(listed(h * PAGE, PAGE)), ACT.Copy)
-        nc.vector.tensor_copy(ks[:], ks_pool[:].indirect(offs_t[:]))
 
         spread = []
         for h in range(PAGES):
@@ -194,7 +198,7 @@ def tile_attend_pkv8q_soft_draft_gate_kernel(
         nc.vector.tensor_copy(vw[:], vw_pool[:].bitcast(U32).indirect(voffs_t[:]))
         nc.vector.tensor_copy(vsc[:], vsc_pool[:].indirect(voffs_t[:]))
 
-        vs_col = sb.tile([P, PAGES, PACK], F32, align_bytes=64, tag="vs_col")
+        vs_col = sb.tile([P, PAGES, PACK], F32, align_bytes=64, tag="ks_then_vw")
         for h in range(PAGES):
             nc.vector.tensor_copy(vs_col[:, h, :], vs_turned[h][:, :, ROW])
 

@@ -53,7 +53,7 @@ def tile_attend_pkv8q_soft_draft_gate_kernel(
         ident = sb.tile([P, P], F32, align_bytes=64)
 
         ramp = sb.tile([P, P], F32, align_bytes=64)
-        dist = early.tile([P, P], F32, align_bytes=64, offset=4 * (T + PAGE - P // 2))
+        dist = early.tile([P, P], F32, align_bytes=64, offset=4 * (T - P // 2))
         nc.gpsimd.iota(ramp[:], [[1, P]], base=0, channel_multiplier=-1, allow_small_or_imprecise_dtypes=True)
         nc.scalar.activation(dist[:], ramp[:], ACT.Abs)
         nc.scalar.activation(ident[:], dist[:], ACT.Relu, scale=-1.0, bias=1.0)
@@ -65,6 +65,7 @@ def tile_attend_pkv8q_soft_draft_gate_kernel(
         nc.vector.memset(ks[:].bitcast(I32), 0)
         nc.vector.memset(pos_pool[0:ROW, :], 0.0)
         nc.vector.memset(vsc_words[:, ODD:], 0)
+        nc.gpsimd.memset(vs_pool[0:ROW, :], 0.0)
 
         def load_query_scales(quad):
             nc.sync.dma_start(
@@ -85,7 +86,6 @@ def tile_attend_pkv8q_soft_draft_gate_kernel(
 
         ks_rows = sb.tile([P, N], U8, align_bytes=64)
         nc.vector.tensor_copy(ks_rows[:], ks_pool[:].indirect(offs_t[:]))
-        nc.vector.memset(vs_pool[0:ROW, :], 0.0)
         for r in range(4):
             nc.sync.dma_start(ks[r:P:32, :].bitcast(I32), ks_rows[SCALES_AT + r : P : 4, :].bitcast(I32))
         vw_pool = sb.tile([P, POOL_PAGES * DV], I32, align_bytes=64, tag="ks_then_vw")
@@ -104,13 +104,11 @@ def tile_attend_pkv8q_soft_draft_gate_kernel(
         def listed(first, count):
             return offs_t[:, first // LIST : (first + count) // LIST]
 
-        pos_row = [
-            early.tile([P, PAGE], F32, name=f"pos_row{h}", align_bytes=64, offset=4 * (T + h * PAGE))
-            for h in range(PAGES)
-        ]
+        pos_rows = early.tile([P, N], F32, align_bytes=64, offset=4 * T)
+        pos_row = [pos_rows[:, h * PAGE : (h + 1) * PAGE] for h in range(PAGES)]
         pos_col = [sb.tile([P, PACK], F32, name=f"pos_col{h}", align_bytes=64, tag=f"pos_col{h}") for h in range(PAGES)]
         for h in range(PAGES):
-            nc.scalar.activation(pos_row[h][:], pos_pool[:].indirect(listed(h * PAGE, PAGE)), ACT.Copy)
+            nc.scalar.activation(pos_row[h], pos_pool[:].indirect(listed(h * PAGE, PAGE)), ACT.Copy)
 
         spread = []
         for h in range(PAGES):

@@ -21,7 +21,7 @@ PACK = 4
 LIST = 16
 ROW = P - 1
 SCALES_AT = P - 16
-ODD = 193
+Q_PLANE = 4
 STEEP = 2.0**96
 HIDDEN = 2.0**72
 
@@ -44,38 +44,34 @@ def tile_attend_pkv8q_soft_draft_gate_kernel(
         kw_pool = sb.tile([P, T], I32, align_bytes=64)
         vsc_pool = sb.tile([P, POOL_PAGES * DV], U8, align_bytes=64, tag="wt1")
         ks_pool = sb.tile([P, T], U8, align_bytes=64, tag="ks_then_vw")
-        ks = sb.tile([P, N], U8, align_bytes=64)
+        planes = sb.tile([P, N], U8, align_bytes=64)
         pos_pool = sb.tile([P, T], F32, align_bytes=64)
         qw = sb.tile([P, NQ], I32, align_bytes=64)
-        qs = sb.tile([P, NQ], U8, align_bytes=64)
         qpos_t = sb.tile([P, 1], F32, align_bytes=64)
         og_t = sb.tile([P, DV], F32)
         ident = sb.tile([P, P], F32, align_bytes=64)
 
-        ramp = sb.tile([P, P], F32, align_bytes=64)
-        dist = early.tile([P, P], F32, align_bytes=64, offset=4 * (T - P // 2))
+        ramp = early.tile([P, P], F32, align_bytes=64, offset=0)
+        dist = sb.tile([P, P], F32, align_bytes=64, tag="dist_then_pos")
         nc.gpsimd.iota(ramp[:], [[1, P]], base=0, channel_multiplier=-1, allow_small_or_imprecise_dtypes=True)
         nc.scalar.activation(dist[:], ramp[:], ACT.Abs)
         nc.scalar.activation(ident[:], dist[:], ACT.Relu, scale=-1.0, bias=1.0)
         vs_pool = early.tile([P, T], F32, align_bytes=64, offset=0)
-        vsc_words = vsc_pool[:].bitcast(I32)
-        nc.vector.memset(qs[:].bitcast(I32), 0)
+        nc.vector.memset(planes[:].bitcast(I32), 0)
         nc.vector.memset(ks_pool[0:SCALES_AT, :].bitcast(I32), 0)
-        nc.vector.memset(vsc_words[:, :ODD], 0)
-        nc.vector.memset(ks[:].bitcast(I32), 0)
+        nc.vector.memset(vsc_pool[:].bitcast(I32), 0)
         nc.vector.memset(pos_pool[0:ROW, :], 0.0)
-        nc.vector.memset(vsc_words[:, ODD:], 0)
         nc.gpsimd.memset(vs_pool[0:ROW, :], 0.0)
 
         def load_query_scales(quad):
             nc.sync.dma_start(
-                qs[32 * quad : 32 * quad + 4, :].bitcast(I32),
+                planes[32 * quad + Q_PLANE : 32 * quad + Q_PLANE + 4, :NQ].bitcast(I32),
                 q_scales[0, 0, 4 * quad : 4 * quad + 4, :].bitcast(I32),
             )
 
         nc.sync.dma_start(offs_t[:], offs)
-        nc.sync.dma_start(ks_pool[SCALES_AT:P, :].bitcast(I32), k_scales[0].bitcast(I32))
         nc.sync.dma_start(pos_pool[ROW:P, :], pos[0:1, :])
+        nc.sync.dma_start(ks_pool[SCALES_AT:P, :].bitcast(I32), k_scales[0].bitcast(I32))
         nc.sync.dma_start(qpos_t[:], qpos[0])
         for quad in range(3):
             load_query_scales(quad)
@@ -84,10 +80,19 @@ def tile_attend_pkv8q_soft_draft_gate_kernel(
         nc.sync.dma_start(qw[:], q_words[0, 0].rearrange("p n t -> p (n t)").bitcast(I32))
         nc.sync.dma_start(vs_pool[ROW:P, :], vs[0:1, :])
 
+        def listed(first, count):
+            return offs_t[:, first // LIST : (first + count) // LIST]
+
+        pos_row = [
+            sb.tile([P, PAGE], F32, name="pos_row0", align_bytes=64),
+            sb.tile([P, PAGE], F32, name="pos_row1", align_bytes=64, tag="dist_then_pos"),
+        ]
+        nc.vector.tensor_copy(pos_row[0][:], pos_pool[:].indirect(listed(0, PAGE)))
+        nc.scalar.activation(pos_row[1][:], pos_pool[:].indirect(listed(PAGE, PAGE)), ACT.Copy)
         ks_rows = sb.tile([P, N], U8, align_bytes=64)
         nc.vector.tensor_copy(ks_rows[:], ks_pool[:].indirect(offs_t[:]))
         for r in range(4):
-            nc.sync.dma_start(ks[r:P:32, :].bitcast(I32), ks_rows[SCALES_AT + r : P : 4, :].bitcast(I32))
+            nc.sync.dma_start(planes[r:P:32, :].bitcast(I32), ks_rows[SCALES_AT + r : P : 4, :].bitcast(I32))
         vw_pool = sb.tile([P, POOL_PAGES * DV], I32, align_bytes=64, tag="ks_then_vw")
         nc.sync.dma_start(
             vw_pool[:].rearrange("p (u e) -> p u e", u=POOL_PAGES),
@@ -101,14 +106,7 @@ def tile_attend_pkv8q_soft_draft_gate_kernel(
             )
         nc.sync.dma_start(og_t[:], og[0])
 
-        def listed(first, count):
-            return offs_t[:, first // LIST : (first + count) // LIST]
-
-        pos_rows = early.tile([P, N], F32, align_bytes=64, offset=4 * T)
-        pos_row = [pos_rows[:, h * PAGE : (h + 1) * PAGE] for h in range(PAGES)]
         pos_col = [sb.tile([P, PACK], F32, name=f"pos_col{h}", align_bytes=64, tag=f"pos_col{h}") for h in range(PAGES)]
-        for h in range(PAGES):
-            nc.scalar.activation(pos_row[h], pos_pool[:].indirect(listed(h * PAGE, PAGE)), ACT.Copy)
 
         spread = []
         for h in range(PAGES):
@@ -148,9 +146,9 @@ def tile_attend_pkv8q_soft_draft_gate_kernel(
             nc.tensor.matmul_mx(
                 out=bank[:],
                 lhsT=qw[:].bitcast(FP8X4),
-                lhsT_scale=qs[:],
+                lhsT_scale=planes[Q_PLANE:P, :NQ],
                 rhs=kw[:].bitcast(FP8X4),
-                rhs_scale=ks[:, h * PAGE : (h + 1) * PAGE],
+                rhs_scale=planes[:, h * PAGE : (h + 1) * PAGE],
                 start=True,
                 stop=True,
             )

@@ -91,8 +91,11 @@ def tile_attend_pkv8q_soft_draft_gate_kernel(
         nc.scalar.activation(pos_row[1][:], pos_pool[:].indirect(listed(PAGE, PAGE)), ACT.Copy)
         ks_rows = sb.tile([P, N], U8, align_bytes=64)
         nc.vector.tensor_copy(ks_rows[:], ks_pool[:].indirect(offs_t[:]))
-        for r in range(4):
-            nc.sync.dma_start(planes[r:P:32, :].bitcast(I32), ks_rows[SCALES_AT + r : P : 4, :].bitcast(I32))
+        for quad in range(4):
+            nc.sync.dma_start(
+                planes[32 * quad : 32 * quad + 4, :].bitcast(I32),
+                ks_rows[SCALES_AT + 4 * quad : SCALES_AT + 4 * quad + 4, :].bitcast(I32),
+            )
         vw_pool = sb.tile([P, POOL_PAGES * DV], I32, align_bytes=64, tag="ks_then_vw")
         nc.sync.dma_start(
             vw_pool[:].rearrange("p (u e) -> p u e", u=POOL_PAGES),

@@ -22,6 +22,7 @@ LIST = 16
 ROW = P - 1
 SCALES_AT = P - 16
 Q_PLANE = 4
+KEY_PIECES = ((0, PAGE), (PAGE, PAGE // 2), (PAGE + PAGE // 2, PAGE // 2))
 STEEP = 2.0**96
 HIDDEN = 2.0**72
 
@@ -142,28 +143,27 @@ def tile_attend_pkv8q_soft_draft_gate_kernel(
             nc.scalar.activation(vs_row[h], vs_pool[:].indirect(listed(h * PAGE, PAGE)), ACT.Copy)
 
         raw = []
-        for h in range(PAGES):
-            kw = sb.tile([P, PAGE], U32, name=f"kw{h}", align_bytes=64)
-            nc.vector.tensor_copy(kw[:], kw_pool[:].bitcast(U32).indirect(listed(h * PAGE, PAGE)))
-            bank = ps.tile([P, PAGE], F32, name=f"raw{h}", tag=f"raw{h}")
+        for j, (first, count) in enumerate(KEY_PIECES):
+            kw = sb.tile([P, count], U32, name=f"kw{j}", align_bytes=64)
+            nc.vector.tensor_copy(kw[:], kw_pool[:].bitcast(U32).indirect(listed(first, count)))
+            raw.append(ps.tile([P, count], F32, name=f"raw{j}", tag=f"raw{j}"))
             nc.tensor.matmul_mx(
-                out=bank[:],
+                out=raw[j][:],
                 lhsT=qw[:].bitcast(FP8X4),
                 lhsT_scale=planes[Q_PLANE:P, :NQ],
                 rhs=kw[:].bitcast(FP8X4),
-                rhs_scale=planes[:, h * PAGE : (h + 1) * PAGE],
+                rhs_scale=planes[:, first : first + count],
                 start=True,
                 stop=True,
             )
-            raw.append(bank)
 
         neg_s = sb.tile([P, N], F32, align_bytes=64)
-        for h in range(PAGES):
+        for j, (first, count) in enumerate(KEY_PIECES):
             nc.vector.scalar_tensor_tensor(
-                neg_s[:, h * PAGE : (h + 1) * PAGE],
-                hid[:, h * PAGE : (h + 1) * PAGE],
+                neg_s[:, first : first + count],
+                hid[:, first : first + count],
                 HIDDEN,
-                raw[h][:],
+                raw[j][:],
                 ALU.min,
                 ALU.subtract,
             )

@@ -22,6 +22,7 @@ LIST = 16
 ROW = P - 1
 SCALES_AT = P - 16
 Q_PLANE = 4
+VECTOR_SHARE = N // 4
 KEY_PIECES = ((0, PAGE), (PAGE, PAGE // 2), (PAGE + PAGE // 2, PAGE // 2))
 STEEP = 2.0**96
 HIDDEN = 2.0**72
@@ -60,7 +61,9 @@ def tile_attend_pkv8q_soft_draft_gate_kernel(
         vs_pool = early.tile([P, T], F32, align_bytes=64, offset=0)
         nc.vector.memset(planes[:].bitcast(I32), 0)
         nc.vector.memset(ks_pool[0:SCALES_AT, :].bitcast(I32), 0)
-        nc.vector.memset(vsc_pool[:].bitcast(I32), 0)
+        vsc_words = vsc_pool[:].bitcast(I32)
+        nc.vector.memset(vsc_words[:, 1:], 0)
+        nc.vector.memset(vsc_words[:, :1], 0)
         nc.vector.memset(pos_pool[0:ROW, :], 0.0)
         nc.gpsimd.memset(vs_pool[0:ROW, :], 0.0)
 
@@ -84,12 +87,21 @@ def tile_attend_pkv8q_soft_draft_gate_kernel(
         def listed(first, count):
             return offs_t[:, first // LIST : (first + count) // LIST]
 
-        pos_row = [
-            sb.tile([P, PAGE], F32, name="pos_row0", align_bytes=64),
-            sb.tile([P, PAGE], F32, name="pos_row1", align_bytes=64, tag="dist_then_pos"),
-        ]
-        nc.vector.tensor_copy(pos_row[0][:], pos_pool[:].indirect(listed(0, PAGE)))
-        nc.scalar.activation(pos_row[1][:], pos_pool[:].indirect(listed(PAGE, PAGE)), ACT.Copy)
+        pos_first = sb.tile([P, VECTOR_SHARE], F32, align_bytes=64)
+        pos_rest = sb.tile([P, N - VECTOR_SHARE], F32, align_bytes=64, tag="dist_then_pos")
+        nc.vector.tensor_copy(pos_first[:], pos_pool[:].indirect(listed(0, VECTOR_SHARE)))
+        for first, end in ((VECTOR_SHARE, PAGE), (PAGE, N)):
+            nc.scalar.activation(
+                pos_rest[:, first - VECTOR_SHARE : end - VECTOR_SHARE],
+                pos_pool[:].indirect(listed(first, end - first)),
+                ACT.Copy,
+            )
+
+        def pos_block(first):
+            if first < VECTOR_SHARE:
+                return pos_first[:, first : first + P]
+            return pos_rest[:, first - VECTOR_SHARE : first - VECTOR_SHARE + P]
+
         ks_rows = sb.tile([P, N], U8, align_bytes=64)
         nc.vector.tensor_copy(ks_rows[:], ks_pool[:].indirect(offs_t[:]))
         for quad in range(4):
@@ -116,7 +128,7 @@ def tile_attend_pkv8q_soft_draft_gate_kernel(
         for h in range(PAGES):
             turned = ps.tile([P, PACK, P], F32, name=f"pos_turned{h}", tag=f"turn{h}")
             for c in range(PACK):
-                nc.tensor.transpose(turned[:, c, :], pos_row[h][:, c * P : (c + 1) * P], ident[:])
+                nc.tensor.transpose(turned[:, c, :], pos_block(h * PAGE + c * P), ident[:])
             nc.scalar.copy(pos_col[h][:], turned[:, :, ROW])
             spread.append(ps.tile([P, PAGE], F32, name=f"pos_all{h}", tag=f"wide{h}"))
             for c in range(PACK):

@@ -20,9 +20,8 @@ POOL_PAGES = T // PAGE
 PACK = 4
 LIST = 16
 ROW = P - 1
-SCALES_AT = P - 16
-Q_PLANE = 4
-VECTOR_SHARE = N // 4
+SPREAD_FROM, SPREAD_TO = 32, 96
+VECTOR_PAGES = 5
 KEY_PIECES = ((0, PAGE), (PAGE, PAGE // 2), (PAGE + PAGE // 2, PAGE // 2))
 STEEP = 2.0**96
 HIDDEN = 2.0**72
@@ -44,10 +43,12 @@ def tile_attend_pkv8q_soft_draft_gate_kernel(
         offs_t = sb.tile([P, N // LIST], U16)
         voffs_t = sb.tile([P, PAGES * DV // LIST], U16)
         kw_pool = sb.tile([P, T], I32, align_bytes=64)
-        vsc_pool = sb.tile([P, POOL_PAGES * DV], U8, align_bytes=64, tag="wt1")
-        ks_pool = sb.tile([P, T], U8, align_bytes=64, tag="ks_then_vw")
-        planes = sb.tile([P, N], U8, align_bytes=64)
+        ks_pool = sb.tile([P, T], U8, align_bytes=64, tag="ks_vw_wt0")
+        q_plane = sb.tile([P, NQ], U8, align_bytes=64)
+        k_plane = sb.tile([P, N], U8, align_bytes=64)
         pos_pool = sb.tile([P, T], F32, align_bytes=64)
+        vs_pool = sb.tile([P, T], F32, align_bytes=64)
+        vs_pages = sb.tile([P, PAGE], F32, align_bytes=64)
         qw = sb.tile([P, NQ], I32, align_bytes=64)
         qpos_t = sb.tile([P, 1], F32, align_bytes=64)
         og_t = sb.tile([P, DV], F32)
@@ -58,58 +59,58 @@ def tile_attend_pkv8q_soft_draft_gate_kernel(
         nc.gpsimd.iota(ramp[:], [[1, P]], base=0, channel_multiplier=-1, allow_small_or_imprecise_dtypes=True)
         nc.scalar.activation(dist[:], ramp[:], ACT.Abs)
         nc.scalar.activation(ident[:], dist[:], ACT.Relu, scale=-1.0, bias=1.0)
-        vs_pool = early.tile([P, T], F32, align_bytes=64, offset=0)
-        nc.vector.memset(planes[:].bitcast(I32), 0)
-        nc.vector.memset(ks_pool[0:SCALES_AT, :].bitcast(I32), 0)
-        vsc_words = vsc_pool[:].bitcast(I32)
-        nc.vector.memset(vsc_words[:, 1:], 0)
-        nc.vector.memset(vsc_words[:, :1], 0)
+        vsc_pool = early.tile([P, POOL_PAGES * DV], U8, align_bytes=64, offset=0)
+        nc.vector.memset(q_plane[:].bitcast(I32), 0)
+        nc.vector.memset(ks_pool[:].bitcast(I32), 0)
+        nc.vector.memset(vs_pages[:], 0.0)
+        k_plane_words = k_plane[:].bitcast(I32)
+        nc.vector.memset(k_plane_words[:, 1:], 0)
+        nc.vector.memset(k_plane_words[:, :1], 0)
         nc.vector.memset(pos_pool[0:ROW, :], 0.0)
-        nc.gpsimd.memset(vs_pool[0:ROW, :], 0.0)
+        nc.gpsimd.memset(vsc_pool[:].bitcast(I32), 0)
 
         def load_query_scales(quad):
             nc.sync.dma_start(
-                planes[32 * quad + Q_PLANE : 32 * quad + Q_PLANE + 4, :NQ].bitcast(I32),
+                q_plane[32 * quad : 32 * quad + 4, :].bitcast(I32),
                 q_scales[0, 0, 4 * quad : 4 * quad + 4, :].bitcast(I32),
             )
 
         nc.sync.dma_start(offs_t[:], offs)
         nc.sync.dma_start(pos_pool[ROW:P, :], pos[0:1, :])
-        nc.sync.dma_start(ks_pool[SCALES_AT:P, :].bitcast(I32), k_scales[0].bitcast(I32))
         nc.sync.dma_start(qpos_t[:], qpos[0])
-        for quad in range(3):
+        for quad in range(2):
             load_query_scales(quad)
+        nc.sync.dma_start(ks_pool[SPREAD_FROM:SPREAD_TO:4, :].bitcast(I32), k_scales[0].bitcast(I32))
+        nc.sync.dma_start(vs_pages[SPREAD_FROM:SPREAD_TO:8, :], vs[0].rearrange("(u j) -> u j", j=PAGE))
         nc.sync.dma_start(kw_pool[:], k_words[0].rearrange("p n t -> p (n t)").bitcast(I32))
-        load_query_scales(3)
+        for quad in range(2, 4):
+            load_query_scales(quad)
         nc.sync.dma_start(qw[:], q_words[0, 0].rearrange("p n t -> p (n t)").bitcast(I32))
-        nc.sync.dma_start(vs_pool[ROW:P, :], vs[0:1, :])
 
         def listed(first, count):
             return offs_t[:, first // LIST : (first + count) // LIST]
 
-        pos_first = sb.tile([P, VECTOR_SHARE], F32, align_bytes=64)
-        pos_rest = sb.tile([P, N - VECTOR_SHARE], F32, align_bytes=64, tag="dist_then_pos")
-        nc.vector.tensor_copy(pos_first[:], pos_pool[:].indirect(listed(0, VECTOR_SHARE)))
-        for first, end in ((VECTOR_SHARE, PAGE), (PAGE, N)):
-            nc.scalar.activation(
-                pos_rest[:, first - VECTOR_SHARE : end - VECTOR_SHARE],
-                pos_pool[:].indirect(listed(first, end - first)),
-                ACT.Copy,
-            )
+        vs_turned = ps.tile([P, PACK, P], F32, tag="acc")
+        for t in range(PACK):
+            nc.tensor.transpose(vs_turned[:, t, :], vs_pages[:, t:PAGE:PACK], ident[:])
 
-        def pos_block(first):
-            if first < VECTOR_SHARE:
-                return pos_first[:, first : first + P]
-            return pos_rest[:, first - VECTOR_SHARE : first - VECTOR_SHARE + P]
+        pos_rows = sb.tile([P, N], F32, align_bytes=64, tag="dist_then_pos")
+        for h in range(PAGES):
+            nc.scalar.activation(
+                pos_rows[:, h * PAGE : (h + 1) * PAGE], pos_pool[:].indirect(listed(h * PAGE, PAGE)), ACT.Copy
+            )
 
         ks_rows = sb.tile([P, N], U8, align_bytes=64)
-        nc.vector.tensor_copy(ks_rows[:], ks_pool[:].indirect(offs_t[:]))
-        for quad in range(4):
+        vs_col = sb.tile([P, POOL_PAGES, PACK], F32, align_bytes=64)
+        nc.vector.tensor_copy(ks_rows[:, :PAGE], ks_pool[:].indirect(listed(0, PAGE)))
+        nc.vector.tensor_copy(vs_col[:], vs_turned[:, :, SPREAD_FROM:SPREAD_TO:8].rearrange("p t u -> p u t"))
+        nc.vector.tensor_copy(ks_rows[:, PAGE:], ks_pool[:].indirect(listed(PAGE, PAGE)))
+        for r in range(4):
             nc.sync.dma_start(
-                planes[32 * quad : 32 * quad + 4, :].bitcast(I32),
-                ks_rows[SCALES_AT + 4 * quad : SCALES_AT + 4 * quad + 4, :].bitcast(I32),
+                k_plane[r:P:32, :].bitcast(I32),
+                ks_rows[SPREAD_FROM + 4 * r : SPREAD_TO : 16, :].bitcast(I32),
             )
-        vw_pool = sb.tile([P, POOL_PAGES * DV], I32, align_bytes=64, tag="ks_then_vw")
+        vw_pool = sb.tile([P, POOL_PAGES * DV], I32, align_bytes=64, tag="ks_vw_wt0")
         nc.sync.dma_start(
             vw_pool[:].rearrange("p (u e) -> p u e", u=POOL_PAGES),
             v_words.rearrange("u p e t -> p u (e t)").bitcast(I32),
@@ -122,37 +123,42 @@ def tile_attend_pkv8q_soft_draft_gate_kernel(
             )
         nc.sync.dma_start(og_t[:], og[0])
 
-        pos_col = [sb.tile([P, PACK], F32, name=f"pos_col{h}", align_bytes=64, tag=f"pos_col{h}") for h in range(PAGES)]
+        def fill_views(u):
+            page = vs_pool[:, u * PAGE : (u + 1) * PAGE].rearrange("p (q t) -> p q t", t=PACK)
+            return page, vs_col[:, u : u + 1, :].to_broadcast([P, NQ, PACK])
 
+        for u in range(VECTOR_PAGES):
+            nc.vector.tensor_copy(*fill_views(u))
+
+        pos_col = [sb.tile([P, PACK], F32, name=f"pos_col{h}", align_bytes=64, tag=f"pos_col{h}") for h in range(PAGES)]
         spread = []
         for h in range(PAGES):
             turned = ps.tile([P, PACK, P], F32, name=f"pos_turned{h}", tag=f"turn{h}")
             for c in range(PACK):
-                nc.tensor.transpose(turned[:, c, :], pos_block(h * PAGE + c * P), ident[:])
+                first = h * PAGE + c * P
+                nc.tensor.transpose(turned[:, c, :], pos_rows[:, first : first + P], ident[:])
             nc.scalar.copy(pos_col[h][:], turned[:, :, ROW])
             spread.append(ps.tile([P, PAGE], F32, name=f"pos_all{h}", tag=f"wide{h}"))
             for c in range(PACK):
                 nc.tensor.transpose(
                     spread[h][:, c * P : (c + 1) * P], pos_col[h][:, c : c + 1].to_broadcast([P, P]), ident[:]
                 )
-        vs_turned = []
-
-        def turn_vs(h, bank):
-            vs_turned.append(ps.tile([P, PACK, P], F32, name=f"vs_turned{h}", tag=bank))
-            for t in range(PACK):
-                nc.tensor.transpose(vs_turned[h][:, t, :], vs_row[h][:, t:PAGE:PACK], ident[:])
 
         hid = late.tile([P, N], F32, align_bytes=64, offset=0)
-        edge = sb.tile([P, 1], F32, align_bytes=64, tag="edge_then_vs0")
+        edge = sb.tile([P, 1], F32, align_bytes=64, tag="edge_then_vs")
         nc.scalar.activation(edge[:], qpos_t[:], ACT.Copy, scale=-STEEP)
         for h in range(PAGES):
             nc.scalar.activation(
                 hid[:, h * PAGE : (h + 1) * PAGE], spread[h][:], ACT.Relu, scale=STEEP, bias=edge[:, 0:1]
             )
-        vs_rows = sb.tile([P, N], F32, align_bytes=64, tag="edge_then_vs0")
-        vs_row = [vs_rows[:, h * PAGE : (h + 1) * PAGE] for h in range(PAGES)]
+        for u in range(VECTOR_PAGES, POOL_PAGES):
+            page, source = fill_views(u)
+            nc.scalar.activation(page, source, ACT.Copy)
+        vs_dealt = sb.tile([P, N], F32, align_bytes=64, tag="edge_then_vs")
         for h in range(PAGES):
-            nc.scalar.activation(vs_row[h], vs_pool[:].indirect(listed(h * PAGE, PAGE)), ACT.Copy)
+            nc.scalar.activation(
+                vs_dealt[:, h * PAGE : (h + 1) * PAGE], vs_pool[:].indirect(listed(h * PAGE, PAGE)), ACT.Copy
+            )
 
         raw = []
         for j, (first, count) in enumerate(KEY_PIECES):
@@ -162,9 +168,9 @@ def tile_attend_pkv8q_soft_draft_gate_kernel(
             nc.tensor.matmul_mx(
                 out=raw[j][:],
                 lhsT=qw[:].bitcast(FP8X4),
-                lhsT_scale=planes[Q_PLANE:P, :NQ],
+                lhsT_scale=q_plane[:],
                 rhs=kw[:].bitcast(FP8X4),
-                rhs_scale=planes[:, first : first + count],
+                rhs_scale=k_plane[:, first : first + count],
                 start=True,
                 stop=True,
             )
@@ -179,8 +185,6 @@ def tile_attend_pkv8q_soft_draft_gate_kernel(
                 ALU.min,
                 ALU.subtract,
             )
-        for h in range(PAGES):
-            turn_vs(h, f"raw{h}")
         neg_m = sb.tile([P, 1], F32, tag="neg_m_then_gate")
         nc.vector.tensor_reduce(neg_m[:], neg_s[:], mybir.AxisListType.X, ALU.min)
 
@@ -209,12 +213,11 @@ def tile_attend_pkv8q_soft_draft_gate_kernel(
         nc.vector.tensor_copy(vw[:], vw_pool[:].bitcast(U32).indirect(voffs_t[:]))
         nc.vector.tensor_copy(vsc[:], vsc_pool[:].indirect(voffs_t[:]))
 
-        vs_col = sb.tile([P, PAGES, PACK], F32, align_bytes=64, tag="ks_then_vw")
-        for h in range(PAGES):
-            nc.vector.tensor_copy(vs_col[:, h, :], vs_turned[h][:, :, ROW])
-
         acc = ps.tile([P, DV], F32, tag="acc")
-        wt = [sb.tile([P, NQ, PACK], BF16, name=f"wt{h}", align_bytes=64, tag=f"wt{h}") for h in range(PAGES)]
+        wt = [
+            sb.tile([P, NQ, PACK], BF16, name="wt0", align_bytes=64, tag="ks_vw_wt0"),
+            early.tile([P, NQ, PACK], BF16, name="wt1", align_bytes=64, offset=0),
+        ]
         codes = [sb.tile([P, NQ], U32, name=f"codes{h}", align_bytes=64) for h in range(PAGES)]
         scales = [sb.tile([P, NQ], U8, name=f"scales{h}", align_bytes=64) for h in range(PAGES)]
         for h in range(PAGES):
@@ -224,7 +227,7 @@ def tile_attend_pkv8q_soft_draft_gate_kernel(
             nc.vector.tensor_tensor(
                 wt[h][:],
                 turned[:].rearrange("m t q -> m q t"),
-                vs_col[:, h : h + 1, :].to_broadcast([P, NQ, PACK]),
+                vs_dealt[:, h * PAGE : (h + 1) * PAGE].rearrange("m (q t) -> m q t", t=PACK),
                 ALU.mult,
             )
         for h in range(PAGES):

@@ -21,7 +21,8 @@ PACK = 4
 LIST = 16
 ROW = P - 1
 SPREAD_FROM, SPREAD_TO = 32, 96
-VECTOR_PAGES = 5
+PAGES_AT = P - POOL_PAGES
+VECTOR_PAGES = 4
 KEY_PIECES = ((0, PAGE), (PAGE, PAGE // 2), (PAGE + PAGE // 2, PAGE // 2))
 STEEP = 2.0**96
 HIDDEN = 2.0**72
@@ -62,10 +63,10 @@ def tile_attend_pkv8q_soft_draft_gate_kernel(
         vsc_pool = early.tile([P, POOL_PAGES * DV], U8, align_bytes=64, offset=0)
         nc.vector.memset(q_plane[:].bitcast(I32), 0)
         nc.vector.memset(ks_pool[:].bitcast(I32), 0)
-        nc.vector.memset(vs_pages[:], 0.0)
         k_plane_words = k_plane[:].bitcast(I32)
         nc.vector.memset(k_plane_words[:, 1:], 0)
         nc.vector.memset(k_plane_words[:, :1], 0)
+        nc.vector.memset(vs_pages[0:PAGES_AT, :], 0.0)
         nc.vector.memset(pos_pool[0:ROW, :], 0.0)
         nc.gpsimd.memset(vsc_pool[:].bitcast(I32), 0)
 
@@ -77,11 +78,11 @@ def tile_attend_pkv8q_soft_draft_gate_kernel(
 
         nc.sync.dma_start(offs_t[:], offs)
         nc.sync.dma_start(pos_pool[ROW:P, :], pos[0:1, :])
+        nc.sync.dma_start(vs_pages[PAGES_AT:P, :], vs[0].rearrange("(u j) -> u j", j=PAGE))
         nc.sync.dma_start(qpos_t[:], qpos[0])
         for quad in range(2):
             load_query_scales(quad)
         nc.sync.dma_start(ks_pool[SPREAD_FROM:SPREAD_TO:4, :].bitcast(I32), k_scales[0].bitcast(I32))
-        nc.sync.dma_start(vs_pages[SPREAD_FROM:SPREAD_TO:8, :], vs[0].rearrange("(u j) -> u j", j=PAGE))
         nc.sync.dma_start(kw_pool[:], k_words[0].rearrange("p n t -> p (n t)").bitcast(I32))
         for quad in range(2, 4):
             load_query_scales(quad)
@@ -103,7 +104,7 @@ def tile_attend_pkv8q_soft_draft_gate_kernel(
         ks_rows = sb.tile([P, N], U8, align_bytes=64)
         vs_col = sb.tile([P, POOL_PAGES, PACK], F32, align_bytes=64)
         nc.vector.tensor_copy(ks_rows[:, :PAGE], ks_pool[:].indirect(listed(0, PAGE)))
-        nc.vector.tensor_copy(vs_col[:], vs_turned[:, :, SPREAD_FROM:SPREAD_TO:8].rearrange("p t u -> p u t"))
+        nc.vector.tensor_copy(vs_col[:], vs_turned[:, :, PAGES_AT:P].rearrange("p t u -> p u t"))
         nc.vector.tensor_copy(ks_rows[:, PAGE:], ks_pool[:].indirect(listed(PAGE, PAGE)))
         for r in range(4):
             nc.sync.dma_start(

@@ -22,7 +22,8 @@ LIST = 16
 ROW = P - 1
 SPREAD_FROM, SPREAD_TO = 32, 96
 PAGES_AT = P - POOL_PAGES
-VECTOR_PAGES = 4
+VECTOR_PAGES = 3
+POS_FIRST = N // 4
 KEY_PIECES = ((0, PAGE), (PAGE, PAGE // 2), (PAGE + PAGE // 2, PAGE // 2))
 STEEP = 2.0**96
 HIDDEN = 2.0**72
@@ -49,7 +50,7 @@ def tile_attend_pkv8q_soft_draft_gate_kernel(
         k_plane = sb.tile([P, N], U8, align_bytes=64)
         pos_pool = sb.tile([P, T], F32, align_bytes=64)
         vs_pool = sb.tile([P, T], F32, align_bytes=64)
-        vs_pages = sb.tile([P, PAGE], F32, align_bytes=64)
+        vs_pages = sb.tile([P, PAGE], F32, align_bytes=64, tag="vs_pages_then_pos")
         qw = sb.tile([P, NQ], I32, align_bytes=64)
         qpos_t = sb.tile([P, 1], F32, align_bytes=64)
         og_t = sb.tile([P, DV], F32)
@@ -95,17 +96,26 @@ def tile_attend_pkv8q_soft_draft_gate_kernel(
         for t in range(PACK):
             nc.tensor.transpose(vs_turned[:, t, :], vs_pages[:, t:PAGE:PACK], ident[:])
 
-        pos_rows = sb.tile([P, N], F32, align_bytes=64, tag="dist_then_pos")
-        for h in range(PAGES):
+        vs_col = sb.tile([P, POOL_PAGES, PACK], F32, align_bytes=64)
+        nc.scalar.copy(vs_col[:], vs_turned[:, :, PAGES_AT:P].rearrange("p t u -> p u t"))
+
+        pos_first = sb.tile([P, POS_FIRST], F32, align_bytes=64, tag="dist_then_pos")
+        pos_rest = sb.tile([P, N - POS_FIRST], F32, align_bytes=64, tag="vs_pages_then_pos")
+        nc.scalar.activation(pos_first[:], pos_pool[:].indirect(listed(0, POS_FIRST)), ACT.Copy)
+        for first, end in ((POS_FIRST, PAGE), (PAGE, N)):
             nc.scalar.activation(
-                pos_rows[:, h * PAGE : (h + 1) * PAGE], pos_pool[:].indirect(listed(h * PAGE, PAGE)), ACT.Copy
+                pos_rest[:, first - POS_FIRST : end - POS_FIRST],
+                pos_pool[:].indirect(listed(first, end - first)),
+                ACT.Copy,
             )
 
+        def pos_block(first):
+            if first < POS_FIRST:
+                return pos_first[:, first : first + P]
+            return pos_rest[:, first - POS_FIRST : first - POS_FIRST + P]
+
         ks_rows = sb.tile([P, N], U8, align_bytes=64)
-        vs_col = sb.tile([P, POOL_PAGES, PACK], F32, align_bytes=64)
-        nc.vector.tensor_copy(ks_rows[:, :PAGE], ks_pool[:].indirect(listed(0, PAGE)))
-        nc.vector.tensor_copy(vs_col[:], vs_turned[:, :, PAGES_AT:P].rearrange("p t u -> p u t"))
-        nc.vector.tensor_copy(ks_rows[:, PAGE:], ks_pool[:].indirect(listed(PAGE, PAGE)))
+        nc.vector.tensor_copy(ks_rows[:], ks_pool[:].indirect(offs_t[:]))
         for r in range(4):
             nc.sync.dma_start(
                 k_plane[r:P:32, :].bitcast(I32),
@@ -128,16 +138,16 @@ def tile_attend_pkv8q_soft_draft_gate_kernel(
             page = vs_pool[:, u * PAGE : (u + 1) * PAGE].rearrange("p (q t) -> p q t", t=PACK)
             return page, vs_col[:, u : u + 1, :].to_broadcast([P, NQ, PACK])
 
-        for u in range(VECTOR_PAGES):
-            nc.vector.tensor_copy(*fill_views(u))
+        for u in range(POOL_PAGES):
+            engine = nc.vector if u < VECTOR_PAGES else nc.gpsimd
+            engine.tensor_copy(*fill_views(u))
 
         pos_col = [sb.tile([P, PACK], F32, name=f"pos_col{h}", align_bytes=64, tag=f"pos_col{h}") for h in range(PAGES)]
         spread = []
         for h in range(PAGES):
             turned = ps.tile([P, PACK, P], F32, name=f"pos_turned{h}", tag=f"turn{h}")
             for c in range(PACK):
-                first = h * PAGE + c * P
-                nc.tensor.transpose(turned[:, c, :], pos_rows[:, first : first + P], ident[:])
+                nc.tensor.transpose(turned[:, c, :], pos_block(h * PAGE + c * P), ident[:])
             nc.scalar.copy(pos_col[h][:], turned[:, :, ROW])
             spread.append(ps.tile([P, PAGE], F32, name=f"pos_all{h}", tag=f"wide{h}"))
             for c in range(PACK):
@@ -152,9 +162,6 @@ def tile_attend_pkv8q_soft_draft_gate_kernel(
             nc.scalar.activation(
                 hid[:, h * PAGE : (h + 1) * PAGE], spread[h][:], ACT.Relu, scale=STEEP, bias=edge[:, 0:1]
             )
-        for u in range(VECTOR_PAGES, POOL_PAGES):
-            page, source = fill_views(u)
-            nc.scalar.activation(page, source, ACT.Copy)
         vs_dealt = sb.tile([P, N], F32, align_bytes=64, tag="edge_then_vs")
         for h in range(PAGES):
             nc.scalar.activation(

@@ -20,10 +20,9 @@ POOL_PAGES = T // PAGE
 PACK = 4
 LIST = 16
 ROW = P - 1
+SCALES_AT = P - 16
 SPREAD_FROM, SPREAD_TO = 32, 96
-PAGES_AT = P - POOL_PAGES
-VECTOR_PAGES = 3
-POS_FIRST = N // 4
+VECTOR_SHARE = N // 4
 KEY_PIECES = ((0, PAGE), (PAGE, PAGE // 2), (PAGE + PAGE // 2, PAGE // 2))
 STEEP = 2.0**96
 HIDDEN = 2.0**72
@@ -62,13 +61,13 @@ def tile_attend_pkv8q_soft_draft_gate_kernel(
         nc.scalar.activation(dist[:], ramp[:], ACT.Abs)
         nc.scalar.activation(ident[:], dist[:], ACT.Relu, scale=-1.0, bias=1.0)
         vsc_pool = early.tile([P, POOL_PAGES * DV], U8, align_bytes=64, offset=0)
+        nc.vector.memset(vs_pages[:], 0.0)
         nc.vector.memset(q_plane[:].bitcast(I32), 0)
-        nc.vector.memset(ks_pool[:].bitcast(I32), 0)
         k_plane_words = k_plane[:].bitcast(I32)
         nc.vector.memset(k_plane_words[:, 1:], 0)
         nc.vector.memset(k_plane_words[:, :1], 0)
-        nc.vector.memset(vs_pages[0:PAGES_AT, :], 0.0)
         nc.vector.memset(pos_pool[0:ROW, :], 0.0)
+        nc.vector.memset(ks_pool[0:SCALES_AT, :].bitcast(I32), 0)
         nc.gpsimd.memset(vsc_pool[:].bitcast(I32), 0)
 
         def load_query_scales(quad):
@@ -79,11 +78,11 @@ def tile_attend_pkv8q_soft_draft_gate_kernel(
 
         nc.sync.dma_start(offs_t[:], offs)
         nc.sync.dma_start(pos_pool[ROW:P, :], pos[0:1, :])
-        nc.sync.dma_start(vs_pages[PAGES_AT:P, :], vs[0].rearrange("(u j) -> u j", j=PAGE))
+        nc.sync.dma_start(ks_pool[SCALES_AT:P, :].bitcast(I32), k_scales[0].bitcast(I32))
         nc.sync.dma_start(qpos_t[:], qpos[0])
+        nc.sync.dma_start(vs_pages[SPREAD_FROM:SPREAD_TO:8, :], vs[0].rearrange("(u j) -> u j", j=PAGE))
         for quad in range(2):
             load_query_scales(quad)
-        nc.sync.dma_start(ks_pool[SPREAD_FROM:SPREAD_TO:4, :].bitcast(I32), k_scales[0].bitcast(I32))
         nc.sync.dma_start(kw_pool[:], k_words[0].rearrange("p n t -> p (n t)").bitcast(I32))
         for quad in range(2, 4):
             load_query_scales(quad)
@@ -97,29 +96,29 @@ def tile_attend_pkv8q_soft_draft_gate_kernel(
             nc.tensor.transpose(vs_turned[:, t, :], vs_pages[:, t:PAGE:PACK], ident[:])
 
         vs_col = sb.tile([P, POOL_PAGES, PACK], F32, align_bytes=64)
-        nc.scalar.copy(vs_col[:], vs_turned[:, :, PAGES_AT:P].rearrange("p t u -> p u t"))
+        nc.scalar.copy(vs_col[:], vs_turned[:, :, SPREAD_FROM:SPREAD_TO:8].rearrange("p t u -> p u t"))
 
-        pos_first = sb.tile([P, POS_FIRST], F32, align_bytes=64, tag="dist_then_pos")
-        pos_rest = sb.tile([P, N - POS_FIRST], F32, align_bytes=64, tag="vs_pages_then_pos")
-        nc.scalar.activation(pos_first[:], pos_pool[:].indirect(listed(0, POS_FIRST)), ACT.Copy)
-        for first, end in ((POS_FIRST, PAGE), (PAGE, N)):
-            nc.scalar.activation(
-                pos_rest[:, first - POS_FIRST : end - POS_FIRST],
-                pos_pool[:].indirect(listed(first, end - first)),
-                ACT.Copy,
-            )
-
-        def pos_block(first):
-            if first < POS_FIRST:
-                return pos_first[:, first : first + P]
-            return pos_rest[:, first - POS_FIRST : first - POS_FIRST + P]
+        pos_pieces = (
+            (nc.scalar, 0, PAGE, "dist_then_pos"),
+            (nc.scalar, PAGE, PAGE - VECTOR_SHARE, "vs_pages_then_pos"),
+            (nc.vector, N - VECTOR_SHARE, VECTOR_SHARE, "pos_last"),
+        )
+        pos_blocks = []
+        for j, (engine, first, count, tag) in enumerate(pos_pieces):
+            rows = sb.tile([P, count], F32, name=f"pos_rows{j}", align_bytes=64, tag=tag)
+            window = pos_pool[:].indirect(listed(first, count))
+            if tag != "pos_last":
+                nc.scalar.activation(rows[:], window, ACT.Copy)
+            else:
+                nc.vector.tensor_copy(rows[:], window)
+            pos_blocks.extend(rows[:, c : c + P] for c in range(0, count, P))
 
         ks_rows = sb.tile([P, N], U8, align_bytes=64)
         nc.vector.tensor_copy(ks_rows[:], ks_pool[:].indirect(offs_t[:]))
-        for r in range(4):
+        for quad in range(4):
             nc.sync.dma_start(
-                k_plane[r:P:32, :].bitcast(I32),
-                ks_rows[SPREAD_FROM + 4 * r : SPREAD_TO : 16, :].bitcast(I32),
+                k_plane[32 * quad : 32 * quad + 4, :].bitcast(I32),
+                ks_rows[SCALES_AT + 4 * quad : SCALES_AT + 4 * quad + 4, :].bitcast(I32),
             )
         vw_pool = sb.tile([P, POOL_PAGES * DV], I32, align_bytes=64, tag="ks_vw_wt0")
         nc.sync.dma_start(
@@ -138,16 +137,16 @@ def tile_attend_pkv8q_soft_draft_gate_kernel(
             page = vs_pool[:, u * PAGE : (u + 1) * PAGE].rearrange("p (q t) -> p q t", t=PACK)
             return page, vs_col[:, u : u + 1, :].to_broadcast([P, NQ, PACK])
 
-        for u in range(POOL_PAGES):
-            engine = nc.vector if u < VECTOR_PAGES else nc.gpsimd
-            engine.tensor_copy(*fill_views(u))
+        nc.vector.tensor_copy(*fill_views(0))
+        for u in range(2, POOL_PAGES):
+            nc.gpsimd.tensor_copy(*fill_views(u))
 
         pos_col = [sb.tile([P, PACK], F32, name=f"pos_col{h}", align_bytes=64, tag=f"pos_col{h}") for h in range(PAGES)]
         spread = []
         for h in range(PAGES):
             turned = ps.tile([P, PACK, P], F32, name=f"pos_turned{h}", tag=f"turn{h}")
             for c in range(PACK):
-                nc.tensor.transpose(turned[:, c, :], pos_block(h * PAGE + c * P), ident[:])
+                nc.tensor.transpose(turned[:, c, :], pos_blocks[h * PACK + c], ident[:])
             nc.scalar.copy(pos_col[h][:], turned[:, :, ROW])
             spread.append(ps.tile([P, PAGE], F32, name=f"pos_all{h}", tag=f"wide{h}"))
             for c in range(PACK):
@@ -162,6 +161,7 @@ def tile_attend_pkv8q_soft_draft_gate_kernel(
             nc.scalar.activation(
                 hid[:, h * PAGE : (h + 1) * PAGE], spread[h][:], ACT.Relu, scale=STEEP, bias=edge[:, 0:1]
             )
+        nc.scalar.activation(*fill_views(1), ACT.Copy)
         vs_dealt = sb.tile([P, N], F32, align_bytes=64, tag="edge_then_vs")
         for h in range(PAGES):
             nc.scalar.activation(

@@ -23,7 +23,8 @@ ROW = P - 1
 SCALES_AT = P - 16
 SPREAD_FROM, SPREAD_TO = 32, 96
 VECTOR_SHARE = N // 4
-KEY_PIECES = ((0, PAGE), (PAGE, PAGE // 2), (PAGE + PAGE // 2, PAGE // 2))
+KEY_PIECE = PAGE // 2
+EXP_PIECES = ((0, 2), (2, 1), (3, 1))
 STEEP = 2.0**96
 HIDDEN = 2.0**72
 
@@ -44,7 +45,7 @@ def tile_attend_pkv8q_soft_draft_gate_kernel(
         offs_t = sb.tile([P, N // LIST], U16)
         voffs_t = sb.tile([P, PAGES * DV // LIST], U16)
         kw_pool = sb.tile([P, T], I32, align_bytes=64)
-        ks_pool = sb.tile([P, T], U8, align_bytes=64, tag="ks_vw_wt0")
+        ks_pool = early.tile([P, T], U8, align_bytes=64, offset=POOL_PAGES * DV)
         q_plane = sb.tile([P, NQ], U8, align_bytes=64)
         k_plane = sb.tile([P, N], U8, align_bytes=64)
         pos_pool = sb.tile([P, T], F32, align_bytes=64)
@@ -120,7 +121,7 @@ def tile_attend_pkv8q_soft_draft_gate_kernel(
                 k_plane[32 * quad : 32 * quad + 4, :].bitcast(I32),
                 ks_rows[SCALES_AT + 4 * quad : SCALES_AT + 4 * quad + 4, :].bitcast(I32),
             )
-        vw_pool = sb.tile([P, POOL_PAGES * DV], I32, align_bytes=64, tag="ks_vw_wt0")
+        vw_pool = early.tile([P, POOL_PAGES * DV], I32, align_bytes=64, offset=POOL_PAGES * DV)
         nc.sync.dma_start(
             vw_pool[:].rearrange("p (u e) -> p u e", u=POOL_PAGES),
             v_words.rearrange("u p e t -> p u (e t)").bitcast(I32),
@@ -154,12 +155,15 @@ def tile_attend_pkv8q_soft_draft_gate_kernel(
                     spread[h][:, c * P : (c + 1) * P], pos_col[h][:, c : c + 1].to_broadcast([P, P]), ident[:]
                 )
 
+        def strips(tile, h):
+            return tile[:, h * PAGE : (h + 1) * PAGE].rearrange("q (t m) -> q t m", t=PACK)
+
         hid = late.tile([P, N], F32, align_bytes=64, offset=0)
         edge = sb.tile([P, 1], F32, align_bytes=64, tag="edge_then_vs")
         nc.scalar.activation(edge[:], qpos_t[:], ACT.Copy, scale=-STEEP)
         for h in range(PAGES):
             nc.scalar.activation(
-                hid[:, h * PAGE : (h + 1) * PAGE], spread[h][:], ACT.Relu, scale=STEEP, bias=edge[:, 0:1]
+                strips(hid, h), spread[h][:].rearrange("q (m t) -> q t m", t=PACK), ACT.Relu, scale=STEEP, bias=edge[:, 0:1]
             )
         nc.scalar.activation(*fill_views(1), ACT.Copy)
         vs_dealt = sb.tile([P, N], F32, align_bytes=64, tag="edge_then_vs")
@@ -169,47 +173,51 @@ def tile_attend_pkv8q_soft_draft_gate_kernel(
             )
 
         raw = []
-        for j, (first, count) in enumerate(KEY_PIECES):
-            kw = sb.tile([P, count], U32, name=f"kw{j}", align_bytes=64)
-            nc.vector.tensor_copy(kw[:], kw_pool[:].bitcast(U32).indirect(listed(first, count)))
-            raw.append(ps.tile([P, count], F32, name=f"raw{j}", tag=f"raw{j}"))
+        for j, bank in enumerate(("raw0", "raw1", "raw2", "turn0")):
+            first = j * KEY_PIECE
+            kw = sb.tile([P, KEY_PIECE], U32, name=f"kw{j}", align_bytes=64)
+            nc.vector.tensor_copy(kw[:], kw_pool[:].bitcast(U32).indirect(listed(first, KEY_PIECE)))
+            raw.append(ps.tile([P, KEY_PIECE], F32, name=f"raw{j}", tag=bank))
             nc.tensor.matmul_mx(
                 out=raw[j][:],
                 lhsT=qw[:].bitcast(FP8X4),
                 lhsT_scale=q_plane[:],
                 rhs=kw[:].bitcast(FP8X4),
-                rhs_scale=k_plane[:, first : first + count],
+                rhs_scale=k_plane[:, first : first + KEY_PIECE],
                 start=True,
                 stop=True,
             )
 
         neg_s = sb.tile([P, N], F32, align_bytes=64)
-        for j, (first, count) in enumerate(KEY_PIECES):
+        for j in range(N // KEY_PIECE):
+            h, half = divmod(j, 2)
+            words = slice(half * KEY_PIECE // PACK, (half + 1) * KEY_PIECE // PACK)
             nc.vector.scalar_tensor_tensor(
-                neg_s[:, first : first + count],
-                hid[:, first : first + count],
+                strips(neg_s, h)[:, :, words],
+                strips(hid, h)[:, :, words],
                 HIDDEN,
-                raw[j][:],
+                raw[j][:].rearrange("q (m t) -> q t m", t=PACK),
                 ALU.min,
                 ALU.subtract,
             )
         neg_m = sb.tile([P, 1], F32, tag="neg_m_then_gate")
         nc.vector.tensor_reduce(neg_m[:], neg_s[:], mybir.AxisListType.X, ALU.min)
 
-        p = [sb.tile([P, 2, P], F32, name=f"p{j}", align_bytes=64) for j in range(2 * PAGES)]
-        sums = sb.tile([P, 2 * PAGES], F32)
-        for j in range(2 * PAGES):
-            h, half = divmod(j, 2)
-            nc.scalar.activation(
-                p[j][:].rearrange("q t m -> q m t"),
-                neg_s[:, h * PAGE : (h + 1) * PAGE].rearrange("q (m t) -> q m t", t=PACK)[
-                    :, :, 2 * half : 2 * half + 2
-                ],
-                ACT.Exp,
-                scale=-1.0,
-                bias=neg_m[:, 0:1],
-                accum_out=sums[:, j : j + 1],
-            )
+        p_strips = []
+        sums = sb.tile([P, PAGES * len(EXP_PIECES)], F32)
+        for h in range(PAGES):
+            for j, (first, count) in enumerate(EXP_PIECES):
+                p = sb.tile([P, count, P], F32, name=f"p{h}_{j}", align_bytes=64)
+                column = h * len(EXP_PIECES) + j
+                nc.scalar.activation(
+                    p[:],
+                    strips(neg_s, h)[:, first : first + count, :],
+                    ACT.Exp,
+                    scale=-1.0,
+                    bias=neg_m[:, 0:1],
+                    accum_out=sums[:, column : column + 1],
+                )
+                p_strips.extend(p[:, t, :] for t in range(count))
 
         gate_t = sb.tile([P, DV], F32, tag="neg_m_then_gate")
         gate = sb.tile([P, DV], F32)
@@ -223,15 +231,15 @@ def tile_attend_pkv8q_soft_draft_gate_kernel(
 
         acc = ps.tile([P, DV], F32, tag="acc")
         wt = [
-            sb.tile([P, NQ, PACK], BF16, name="wt0", align_bytes=64, tag="ks_vw_wt0"),
-            early.tile([P, NQ, PACK], BF16, name="wt1", align_bytes=64, offset=0),
+            early.tile([P, NQ, PACK], BF16, name="wt0", align_bytes=64, offset=POOL_PAGES * DV // 2),
+            sb.tile([P, NQ, PACK], BF16, name="wt1", align_bytes=64),
         ]
         codes = [sb.tile([P, NQ], U32, name=f"codes{h}", align_bytes=64) for h in range(PAGES)]
         scales = [sb.tile([P, NQ], U8, name=f"scales{h}", align_bytes=64) for h in range(PAGES)]
         for h in range(PAGES):
             turned = ps.tile([P, PACK, NQ], F32, name=f"p_turned{h}", tag=f"wide{h}")
             for t in range(PACK):
-                nc.tensor.transpose(turned[:, t, :], p[2 * h + t // 2][:, t % 2, :], ident[:])
+                nc.tensor.transpose(turned[:, t, :], p_strips[h * PACK + t], ident[:])
             nc.vector.tensor_tensor(
                 wt[h][:],
                 turned[:].rearrange("m t q -> m q t"),

@@ -22,7 +22,7 @@ LIST = 16
 ROW = P - 1
 SCALES_AT = P - 16
 SPREAD_FROM, SPREAD_TO = 32, 96
-VECTOR_SHARE = N // 4
+VECTOR_PAGES = 2
 KEY_PIECE = PAGE // 2
 EXP_PIECES = ((0, 2), (2, 1), (3, 1))
 STEEP = 2.0**96
@@ -45,23 +45,23 @@ def tile_attend_pkv8q_soft_draft_gate_kernel(
         offs_t = sb.tile([P, N // LIST], U16)
         voffs_t = sb.tile([P, PAGES * DV // LIST], U16)
         kw_pool = sb.tile([P, T], I32, align_bytes=64)
-        ks_pool = early.tile([P, T], U8, align_bytes=64, offset=POOL_PAGES * DV)
+        ks_pool = early.tile([P, T], U8, align_bytes=64, offset=4096)
         q_plane = sb.tile([P, NQ], U8, align_bytes=64)
         k_plane = sb.tile([P, N], U8, align_bytes=64)
         pos_pool = sb.tile([P, T], F32, align_bytes=64)
         vs_pool = sb.tile([P, T], F32, align_bytes=64)
-        vs_pages = sb.tile([P, PAGE], F32, align_bytes=64, tag="vs_pages_then_pos")
+        vs_pages = early.tile([P, PAGE], F32, align_bytes=64, offset=1536)
         qw = sb.tile([P, NQ], I32, align_bytes=64)
         qpos_t = sb.tile([P, 1], F32, align_bytes=64)
         og_t = sb.tile([P, DV], F32)
         ident = sb.tile([P, P], F32, align_bytes=64)
 
-        ramp = early.tile([P, P], F32, align_bytes=64, offset=0)
+        ramp = sb.tile([P, P], F32, align_bytes=64)
         dist = sb.tile([P, P], F32, align_bytes=64, tag="dist_then_pos")
         nc.gpsimd.iota(ramp[:], [[1, P]], base=0, channel_multiplier=-1, allow_small_or_imprecise_dtypes=True)
         nc.scalar.activation(dist[:], ramp[:], ACT.Abs)
         nc.scalar.activation(ident[:], dist[:], ACT.Relu, scale=-1.0, bias=1.0)
-        vsc_pool = early.tile([P, POOL_PAGES * DV], U8, align_bytes=64, offset=0)
+        vsc_pool = early.tile([P, POOL_PAGES * DV], U8, align_bytes=64, offset=3072)
         nc.vector.memset(vs_pages[:], 0.0)
         nc.vector.memset(q_plane[:].bitcast(I32), 0)
         k_plane_words = k_plane[:].bitcast(I32)
@@ -69,7 +69,6 @@ def tile_attend_pkv8q_soft_draft_gate_kernel(
         nc.vector.memset(k_plane_words[:, :1], 0)
         nc.vector.memset(pos_pool[0:ROW, :], 0.0)
         nc.vector.memset(ks_pool[0:SCALES_AT, :].bitcast(I32), 0)
-        nc.gpsimd.memset(vsc_pool[:].bitcast(I32), 0)
 
         def load_query_scales(quad):
             nc.sync.dma_start(
@@ -77,9 +76,9 @@ def tile_attend_pkv8q_soft_draft_gate_kernel(
                 q_scales[0, 0, 4 * quad : 4 * quad + 4, :].bitcast(I32),
             )
 
-        nc.sync.dma_start(offs_t[:], offs)
         nc.sync.dma_start(pos_pool[ROW:P, :], pos[0:1, :])
         nc.sync.dma_start(ks_pool[SCALES_AT:P, :].bitcast(I32), k_scales[0].bitcast(I32))
+        nc.sync.dma_start(offs_t[:], offs)
         nc.sync.dma_start(qpos_t[:], qpos[0])
         nc.sync.dma_start(vs_pages[SPREAD_FROM:SPREAD_TO:8, :], vs[0].rearrange("(u j) -> u j", j=PAGE))
         for quad in range(2):
@@ -99,20 +98,19 @@ def tile_attend_pkv8q_soft_draft_gate_kernel(
         vs_col = sb.tile([P, POOL_PAGES, PACK], F32, align_bytes=64)
         nc.scalar.copy(vs_col[:], vs_turned[:, :, SPREAD_FROM:SPREAD_TO:8].rearrange("p t u -> p u t"))
 
-        pos_pieces = (
-            (nc.scalar, 0, PAGE, "dist_then_pos"),
-            (nc.scalar, PAGE, PAGE - VECTOR_SHARE, "vs_pages_then_pos"),
-            (nc.vector, N - VECTOR_SHARE, VECTOR_SHARE, "pos_last"),
-        )
-        pos_blocks = []
-        for j, (engine, first, count, tag) in enumerate(pos_pieces):
-            rows = sb.tile([P, count], F32, name=f"pos_rows{j}", align_bytes=64, tag=tag)
-            window = pos_pool[:].indirect(listed(first, count))
-            if tag != "pos_last":
-                nc.scalar.activation(rows[:], window, ACT.Copy)
-            else:
-                nc.vector.tensor_copy(rows[:], window)
-            pos_blocks.extend(rows[:, c : c + P] for c in range(0, count, P))
+        nc.gpsimd.memset(vsc_pool[:].bitcast(I32), 0)
+
+        pos_rows = [
+            sb.tile([P, PAGE], F32, name="pos_rows0", align_bytes=64, tag="dist_then_pos"),
+            early.tile([P, PAGE], F32, name="pos_rows1", align_bytes=64, offset=1024),
+        ]
+        for h, first, count in ((0, 0, PAGE), (1, 0, PAGE // 2), (1, PAGE // 2, PAGE // 2)):
+            nc.scalar.activation(
+                pos_rows[h][:, first : first + count],
+                pos_pool[:].indirect(listed(h * PAGE + first, count)),
+                ACT.Copy,
+            )
+        pos_blocks = [pos_rows[h][:, c : c + P] for h in range(PAGES) for c in range(0, PAGE, P)]
 
         ks_rows = sb.tile([P, N], U8, align_bytes=64)
         nc.vector.tensor_copy(ks_rows[:], ks_pool[:].indirect(offs_t[:]))
@@ -121,7 +119,7 @@ def tile_attend_pkv8q_soft_draft_gate_kernel(
                 k_plane[32 * quad : 32 * quad + 4, :].bitcast(I32),
                 ks_rows[SCALES_AT + 4 * quad : SCALES_AT + 4 * quad + 4, :].bitcast(I32),
             )
-        vw_pool = early.tile([P, POOL_PAGES * DV], I32, align_bytes=64, offset=POOL_PAGES * DV)
+        vw_pool = early.tile([P, POOL_PAGES * DV], I32, align_bytes=64, offset=4096)
         nc.sync.dma_start(
             vw_pool[:].rearrange("p (u e) -> p u e", u=POOL_PAGES),
             v_words.rearrange("u p e t -> p u (e t)").bitcast(I32),
@@ -138,8 +136,14 @@ def tile_attend_pkv8q_soft_draft_gate_kernel(
             page = vs_pool[:, u * PAGE : (u + 1) * PAGE].rearrange("p (q t) -> p q t", t=PACK)
             return page, vs_col[:, u : u + 1, :].to_broadcast([P, NQ, PACK])
 
-        nc.vector.tensor_copy(*fill_views(0))
-        for u in range(2, POOL_PAGES):
+        nc.vector.tensor_copy(
+            vs_pool[:, : VECTOR_PAGES * PAGE].rearrange("p (u q t) -> p u q t", u=VECTOR_PAGES, t=PACK),
+            vs_turned[:, :, SPREAD_FROM : SPREAD_FROM + 8 * VECTOR_PAGES : 8]
+            .rearrange("p t u -> p u t")
+            .unsqueeze(2)
+            .to_broadcast([P, VECTOR_PAGES, NQ, PACK]),
+        )
+        for u in range(VECTOR_PAGES + 1, POOL_PAGES):
             nc.gpsimd.tensor_copy(*fill_views(u))
 
         pos_col = [sb.tile([P, PACK], F32, name=f"pos_col{h}", align_bytes=64, tag=f"pos_col{h}") for h in range(PAGES)]
@@ -165,7 +169,7 @@ def tile_attend_pkv8q_soft_draft_gate_kernel(
             nc.scalar.activation(
                 strips(hid, h), spread[h][:].rearrange("q (m t) -> q t m", t=PACK), ACT.Relu, scale=STEEP, bias=edge[:, 0:1]
             )
-        nc.scalar.activation(*fill_views(1), ACT.Copy)
+        nc.scalar.activation(*fill_views(VECTOR_PAGES), ACT.Copy)
         vs_dealt = sb.tile([P, N], F32, align_bytes=64, tag="edge_then_vs")
         for h in range(PAGES):
             nc.scalar.activation(
@@ -231,7 +235,7 @@ def tile_attend_pkv8q_soft_draft_gate_kernel(
 
         acc = ps.tile([P, DV], F32, tag="acc")
         wt = [
-            early.tile([P, NQ, PACK], BF16, name="wt0", align_bytes=64, offset=POOL_PAGES * DV // 2),
+            early.tile([P, NQ, PACK], BF16, name="wt0", align_bytes=64, offset=3584),
             sb.tile([P, NQ, PACK], BF16, name="wt1", align_bytes=64),
         ]
         codes = [sb.tile([P, NQ], U32, name=f"codes{h}", align_bytes=64) for h in range(PAGES)]

from contextlib import ExitStack

import concourse.mybir as mybir

F32 = mybir.dt.float32
BF16 = mybir.dt.bfloat16
I32 = mybir.dt.int32
U32 = mybir.dt.uint32
U16 = mybir.dt.uint16
U8 = mybir.dt.uint8
FP8X4 = mybir.dt.float8_e4m3fn_x4
ALU = mybir.AluOpType
ACT = mybir.ActivationFunctionType

P = 128
N, T, D, DV, NQ = 1024, 4096, 512, 128, 128
PAGE = 512
PAGES = N // PAGE
POOL_PAGES = T // PAGE
PACK = 4
LIST = 16
ROW = P - 1
SCALES_AT = P - 16
SPREAD_FROM, SPREAD_TO = 32, 96
VECTOR_PAGES = 2
KEY_PIECE = PAGE // 2
EXP_PIECES = ((0, 2), (2, 1), (3, 1))
STEEP = 2.0**96
HIDDEN = 2.0**72

FLOPS = 2 * NQ * N * D + 2 * NQ * N * DV
BYTES = T * D + 16 * T + T * DV + 16 * 8 * DV + D * NQ + 16 * NQ + 2 * 4 * T + 4 * NQ + 2 * 4 * NQ * DV + 2 * P * (N + 256) // 16


def tile_attend_pkv8q_soft_draft_gate_kernel(
    tc, q_words, q_scales, k_words, k_scales, v_words, v_scales, vs, pos, qpos, og, offs, voffs, out
):
    nc = tc.nc
    with ExitStack() as ctx:
        sb = ctx.enter_context(tc.tile_pool(name="sb", bufs=1))
        late = ctx.enter_context(tc.tile_pool(name="late", bufs=1))
        early = ctx.enter_context(tc.tile_pool(name="early", bufs=1))
        ps = ctx.enter_context(tc.psum_pool(name="ps", bufs=1))

        offs_t = sb.tile([P, N // LIST], U16)
        voffs_t = sb.tile([P, PAGES * DV // LIST], U16)
        kw_pool = sb.tile([P, T], I32, align_bytes=64)
        ks_pool = early.tile([P, T], U8, align_bytes=64, offset=4096)
        q_plane = sb.tile([P, NQ], U8, align_bytes=64)
        k_plane = sb.tile([P, N], U8, align_bytes=64)
        pos_pool = sb.tile([P, T], F32, align_bytes=64)
        vs_pool = sb.tile([P, T], F32, align_bytes=64)
        vs_pages = early.tile([P, PAGE], F32, align_bytes=64, offset=1536)
        qw = sb.tile([P, NQ], I32, align_bytes=64)
        qpos_t = sb.tile([P, 1], F32, align_bytes=64)
        og_t = sb.tile([P, DV], F32)
        ident = sb.tile([P, P], F32, align_bytes=64)

        ramp = sb.tile([P, P], F32, align_bytes=64)
        dist = sb.tile([P, P], F32, align_bytes=64, tag="dist_then_pos")
        nc.gpsimd.iota(ramp[:], [[1, P]], base=0, channel_multiplier=-1, allow_small_or_imprecise_dtypes=True)
        nc.scalar.activation(dist[:], ramp[:], ACT.Abs)
        nc.scalar.activation(ident[:], dist[:], ACT.Relu, scale=-1.0, bias=1.0)
        vsc_pool = early.tile([P, POOL_PAGES * DV], U8, align_bytes=64, offset=3072)
        nc.vector.memset(vs_pages[:], 0.0)
        nc.vector.memset(q_plane[:].bitcast(I32), 0)
        k_plane_words = k_plane[:].bitcast(I32)
        nc.vector.memset(k_plane_words[:, 1:], 0)
        nc.vector.memset(k_plane_words[:, :1], 0)
        nc.vector.memset(pos_pool[0:ROW, :], 0.0)
        nc.vector.memset(ks_pool[0:SCALES_AT, :].bitcast(I32), 0)

        def load_query_scales(quad):
            nc.sync.dma_start(
                q_plane[32 * quad : 32 * quad + 4, :].bitcast(I32),
                q_scales[0, 0, 4 * quad : 4 * quad + 4, :].bitcast(I32),
            )

        nc.sync.dma_start(pos_pool[ROW:P, :], pos[0:1, :])
        nc.sync.dma_start(ks_pool[SCALES_AT:P, :].bitcast(I32), k_scales[0].bitcast(I32))
        nc.sync.dma_start(offs_t[:], offs)
        nc.sync.dma_start(qpos_t[:], qpos[0])
        nc.sync.dma_start(vs_pages[SPREAD_FROM:SPREAD_TO:8, :], vs[0].rearrange("(u j) -> u j", j=PAGE))
        for quad in range(2):
            load_query_scales(quad)
        nc.sync.dma_start(kw_pool[:], k_words[0].rearrange("p n t -> p (n t)").bitcast(I32))
        for quad in range(2, 4):
            load_query_scales(quad)
        nc.sync.dma_start(qw[:], q_words[0, 0].rearrange("p n t -> p (n t)").bitcast(I32))

        def listed(first, count):
            return offs_t[:, first // LIST : (first + count) // LIST]

        vs_turned = ps.tile([P, PACK, P], F32, tag="acc")
        for t in range(PACK):
            nc.tensor.transpose(vs_turned[:, t, :], vs_pages[:, t:PAGE:PACK], ident[:])

        vs_col = sb.tile([P, POOL_PAGES, PACK], F32, align_bytes=64)
        nc.scalar.copy(vs_col[:], vs_turned[:, :, SPREAD_FROM:SPREAD_TO:8].rearrange("p t u -> p u t"))

        nc.gpsimd.memset(vsc_pool[:].bitcast(I32), 0)

        pos_rows = [
            sb.tile([P, PAGE], F32, name="pos_rows0", align_bytes=64, tag="dist_then_pos"),
            early.tile([P, PAGE], F32, name="pos_rows1", align_bytes=64, offset=1024),
        ]
        for h, first, count in ((0, 0, PAGE), (1, 0, PAGE // 2), (1, PAGE // 2, PAGE // 2)):
            nc.scalar.activation(
                pos_rows[h][:, first : first + count],
                pos_pool[:].indirect(listed(h * PAGE + first, count)),
                ACT.Copy,
            )
        pos_blocks = [pos_rows[h][:, c : c + P] for h in range(PAGES) for c in range(0, PAGE, P)]

        ks_rows = sb.tile([P, N], U8, align_bytes=64)
        nc.vector.tensor_copy(ks_rows[:], ks_pool[:].indirect(offs_t[:]))
        for quad in range(4):
            nc.sync.dma_start(
                k_plane[32 * quad : 32 * quad + 4, :].bitcast(I32),
                ks_rows[SCALES_AT + 4 * quad : SCALES_AT + 4 * quad + 4, :].bitcast(I32),
            )
        vw_pool = early.tile([P, POOL_PAGES * DV], I32, align_bytes=64, offset=4096)
        nc.sync.dma_start(
            vw_pool[:].rearrange("p (u e) -> p u e", u=POOL_PAGES),
            v_words.rearrange("u p e t -> p u (e t)").bitcast(I32),
        )
        nc.sync.dma_start(voffs_t[:], voffs)
        for r in range(4):
            nc.sync.dma_start(
                vsc_pool[r:P:32, :].bitcast(I32).rearrange("p (u e) -> p u e", u=POOL_PAGES),
                v_scales[:, r:16:4, :].rearrange("u f e -> f u e").bitcast(I32),
            )
        nc.sync.dma_start(og_t[:], og[0])

        def fill_views(u):
            page = vs_pool[:, u * PAGE : (u + 1) * PAGE].rearrange("p (q t) -> p q t", t=PACK)
            return page, vs_col[:, u : u + 1, :].to_broadcast([P, NQ, PACK])

        nc.vector.tensor_copy(
            vs_pool[:, : VECTOR_PAGES * PAGE].rearrange("p (u q t) -> p u q t", u=VECTOR_PAGES, t=PACK),
            vs_turned[:, :, SPREAD_FROM : SPREAD_FROM + 8 * VECTOR_PAGES : 8]
            .rearrange("p t u -> p u t")
            .unsqueeze(2)
            .to_broadcast([P, VECTOR_PAGES, NQ, PACK]),
        )
        for u in range(VECTOR_PAGES + 1, POOL_PAGES):
            nc.gpsimd.tensor_copy(*fill_views(u))

        pos_col = [sb.tile([P, PACK], F32, name=f"pos_col{h}", align_bytes=64, tag=f"pos_col{h}") for h in range(PAGES)]
        spread = []
        for h in range(PAGES):
            turned = ps.tile([P, PACK, P], F32, name=f"pos_turned{h}", tag=f"turn{h}")
            for c in range(PACK):
                nc.tensor.transpose(turned[:, c, :], pos_blocks[h * PACK + c], ident[:])
            nc.scalar.copy(pos_col[h][:], turned[:, :, ROW])
            spread.append(ps.tile([P, PAGE], F32, name=f"pos_all{h}", tag=f"wide{h}"))
            for c in range(PACK):
                nc.tensor.transpose(
                    spread[h][:, c * P : (c + 1) * P], pos_col[h][:, c : c + 1].to_broadcast([P, P]), ident[:]
                )

        def strips(tile, h):
            return tile[:, h * PAGE : (h + 1) * PAGE].rearrange("q (t m) -> q t m", t=PACK)

        hid = late.tile([P, N], F32, align_bytes=64, offset=0)
        edge = sb.tile([P, 1], F32, align_bytes=64, tag="edge_then_vs")
        nc.scalar.activation(edge[:], qpos_t[:], ACT.Copy, scale=-STEEP)
        for h in range(PAGES):
            nc.scalar.activation(
                strips(hid, h), spread[h][:].rearrange("q (m t) -> q t m", t=PACK), ACT.Relu, scale=STEEP, bias=edge[:, 0:1]
            )
        nc.scalar.activation(*fill_views(VECTOR_PAGES), ACT.Copy)
        vs_dealt = sb.tile([P, N], F32, align_bytes=64, tag="edge_then_vs")
        for h in range(PAGES):
            nc.scalar.activation(
                vs_dealt[:, h * PAGE : (h + 1) * PAGE], vs_pool[:].indirect(listed(h * PAGE, PAGE)), ACT.Copy
            )

        raw = []
        for j, bank in enumerate(("raw0", "raw1", "raw2", "turn0")):
            first = j * KEY_PIECE
            kw = sb.tile([P, KEY_PIECE], U32, name=f"kw{j}", align_bytes=64)
            nc.vector.tensor_copy(kw[:], kw_pool[:].bitcast(U32).indirect(listed(first, KEY_PIECE)))
            raw.append(ps.tile([P, KEY_PIECE], F32, name=f"raw{j}", tag=bank))
            nc.tensor.matmul_mx(
                out=raw[j][:],
                lhsT=qw[:].bitcast(FP8X4),
                lhsT_scale=q_plane[:],
                rhs=kw[:].bitcast(FP8X4),
                rhs_scale=k_plane[:, first : first + KEY_PIECE],
                start=True,
                stop=True,
            )

        neg_s = sb.tile([P, N], F32, align_bytes=64)
        for j in range(N // KEY_PIECE):
            h, half = divmod(j, 2)
            words = slice(half * KEY_PIECE // PACK, (half + 1) * KEY_PIECE // PACK)
            nc.vector.scalar_tensor_tensor(
                strips(neg_s, h)[:, :, words],
                strips(hid, h)[:, :, words],
                HIDDEN,
                raw[j][:].rearrange("q (m t) -> q t m", t=PACK),
                ALU.min,
                ALU.subtract,
            )
        neg_m = sb.tile([P, 1], F32, tag="neg_m_then_gate")
        nc.vector.tensor_reduce(neg_m[:], neg_s[:], mybir.AxisListType.X, ALU.min)

        p_strips = []
        sums = sb.tile([P, PAGES * len(EXP_PIECES)], F32)
        for h in range(PAGES):
            for j, (first, count) in enumerate(EXP_PIECES):
                p = sb.tile([P, count, P], F32, name=f"p{h}_{j}", align_bytes=64)
                column = h * len(EXP_PIECES) + j
                nc.scalar.activation(
                    p[:],
                    strips(neg_s, h)[:, first : first + count, :],
                    ACT.Exp,
                    scale=-1.0,
                    bias=neg_m[:, 0:1],
                    accum_out=sums[:, column : column + 1],
                )
                p_strips.extend(p[:, t, :] for t in range(count))

        gate_t = sb.tile([P, DV], F32, tag="neg_m_then_gate")
        gate = sb.tile([P, DV], F32)
        nc.scalar.activation(gate_t[:], og_t[:], ACT.Tanh, scale=0.5)
        nc.scalar.activation(gate[:], gate_t[:], ACT.Copy, scale=0.5, bias=0.5)

        vw = late.tile([P, PAGES * DV], U32, align_bytes=64, offset=4 * PAGE)
        vsc = late.tile([P, PAGES * DV], U8, align_bytes=64, offset=4 * PAGE + 4 * PAGES * DV)
        nc.vector.tensor_copy(vw[:], vw_pool[:].bitcast(U32).indirect(voffs_t[:]))
        nc.vector.tensor_copy(vsc[:], vsc_pool[:].indirect(voffs_t[:]))

        acc = ps.tile([P, DV], F32, tag="acc")
        wt = [
            early.tile([P, NQ, PACK], BF16, name="wt0", align_bytes=64, offset=3584),
            sb.tile([P, NQ, PACK], BF16, name="wt1", align_bytes=64),
        ]
        codes = [sb.tile([P, NQ], U32, name=f"codes{h}", align_bytes=64) for h in range(PAGES)]
        scales = [sb.tile([P, NQ], U8, name=f"scales{h}", align_bytes=64) for h in range(PAGES)]
        for h in range(PAGES):
            turned = ps.tile([P, PACK, NQ], F32, name=f"p_turned{h}", tag=f"wide{h}")
            for t in range(PACK):
                nc.tensor.transpose(turned[:, t, :], p_strips[h * PACK + t], ident[:])
            nc.vector.tensor_tensor(
                wt[h][:],
                turned[:].rearrange("m t q -> m q t"),
                vs_dealt[:, h * PAGE : (h + 1) * PAGE].rearrange("m (q t) -> m q t", t=PACK),
                ALU.mult,
            )
        for h in range(PAGES):
            nc.vector.quantize_mx(
                out=codes[h][:].bitcast(FP8X4), scales=scales[h][:], in_=wt[h][:].rearrange("p q t -> p (q t)")
            )
        total = sb.tile([P, 1], F32)
        inv = sb.tile([P, 1], F32)
        nc.vector.tensor_reduce(total[:], sums[:], mybir.AxisListType.X, ALU.add)
        nc.vector.reciprocal(inv[:], total[:])
        for h in range(PAGES):
            nc.tensor.matmul_mx(
                out=acc[:],
                lhsT=codes[h][:].bitcast(FP8X4),
                lhsT_scale=scales[h][:],
                rhs=vw[:, h * DV : (h + 1) * DV].bitcast(FP8X4),
                rhs_scale=vsc[:, h * DV : (h + 1) * DV],
                start=(h == 0),
                stop=(h == PAGES - 1),
            )
        result = sb.tile([P, DV], F32)
        nc.vector.scalar_tensor_tensor(result[:], acc[:], inv[:, 0:1], gate[:], ALU.mult, ALU.mult)
        nc.sync.dma_start(out[0], result[:])
